import numpy as np, ml_dtypes
CORES = [6,15,38,47]
N = 4
import mx_ref
BF = ml_dtypes.bfloat16
def gentries(a):
    return np.ascontiguousarray(a.reshape(8, 16, -1).transpose(0, 2, 1)).reshape(8, -1)
def gtable(e):
    e = np.asarray(e); return np.ascontiguousarray(e.reshape(8, -1, 16).transpose(0, 2, 1)).reshape(128, -1).astype(np.int32)
def gcols(t, e):
    v = np.concatenate([t.reshape(8, 16, -1, 4), np.zeros((8, 16, 1, 4), BF)], axis=2)
    return np.ascontiguousarray(np.stack([v[g][:, e[g]] for g in range(8)])).reshape(128, -1)
def tile(rs):
    return np.stack(rs, axis=2).reshape(128, -1).astype(BF)
def pick(q, e):
    c = np.concatenate([q[0].reshape(128, -1, 4), np.zeros((128, 1, 4), np.uint8)], axis=1); s = np.concatenate([q[1], np.ones((16, 1), np.uint8)], axis=1)
    return (np.ascontiguousarray(c[:, e].reshape(128, -1)), np.ascontiguousarray(s[:, e]))
def join(*qs):
    return (np.concatenate([q[0] for q in qs], axis=1), np.concatenate([q[1] for q in qs], axis=1))
def put(q, e, v):
    c, s = q[0].reshape(128, -1, 4).copy(), q[1].copy(); c[:, e] = v[0].reshape(128, -1, 4); s[:, e] = v[1]
    return (c.reshape(128, -1), s)
def pk(c, s):
    return (np.ascontiguousarray(c), mx_ref.live(s))
def emit(q):
    return q[0], q[1]
def packed(v, rng):
    q = [mx_ref.quantize(np.ascontiguousarray(v[r])) for r in range(N)]
    return np.stack([a for a, b in q]), np.stack([mx_ref.plane(b, rng) for a, b in q])
def values_of_codes():
    e, c = np.zeros((128, 128, 4), np.float32), np.zeros((128, 2, 4), np.uint8)
    e[np.arange(128), np.arange(128), 0] = 1
    c[:127, :, 0] = np.arange(256).reshape(2, 128).T[:127]
    return mx_ref.matmul(mx_ref.quantize(e.reshape(128, 512).astype(BF)), (c.reshape(128, 8), np.full((16, 2), 127, np.uint8))).T.reshape(-1).astype(np.float64)
CODE_VALUE, SCALE_VALUE = values_of_codes(), 2.0 ** (np.arange(256) - 127.0)
def decode(q):
    return (CODE_VALUE[q[0]].reshape(16, 8, -1, 4) * SCALE_VALUE[q[1]][:, None, :, None] + 0.0).reshape(128, -1).astype(np.float32)
def f(rng, *shape):
    return mx_ref.flush((rng.standard_normal(shape, dtype=np.float32) * np.exp2(rng.integers(-2, 3, shape[:-1] + (1,)))).astype(BF))
def wide(rng, *shape, cols=0):
    v = rng.standard_normal(shape, dtype=np.float32) * np.exp2(rng.integers(-12, 13, shape)).astype(np.float32)
    if cols: v *= np.repeat(np.exp2(rng.integers(-cols, cols + 1, shape[:-2] + (1, shape[-1] // 4))) * (rng.random(shape[:-2] + (1, shape[-1] // 4)) > 0.0625), 4, axis=-1).astype(np.float32)
    return mx_ref.flush(v.astype(BF))
C, K, M, R = 448, 32, 14, 3
BASE = M * np.concatenate([np.arange(K), np.arange(K)])
def matrices(a):
    return a.reshape(8, 16, K // 16, M, M).transpose(0, 2, 1, 3, 4).reshape(8, K, M, M).astype(np.int64)
def stored(m):
    return np.ascontiguousarray(m.reshape(8, K // 16, 16, M, M).transpose(0, 2, 1, 3, 4)).reshape(128, -1)
def numbers_of(rng):
    return {"x": np.array(f(rng, N, 128, 4 * C)), "u": np.array(f(rng, N, 128, 512)), "v": np.array(f(rng, N, 128, 512))}
def nodes(rng):
    return np.stack([gtable(np.stack([rng.permutation(C) for g in range(8)])) for r in range(N)])
def arrows(a):
    a = np.triu(a, 1)
    a = a - a.swapaxes(-1, -2)
    return np.stack([stored(a[r]) for r in range(N)]).astype(np.int32)
def some_arrows(rng):
    return rng.integers(-3, 4, (N, 8, K, M, M)) * (rng.random((N, 8, K, M, M)) < 0.6)
def laid(w, nd):
    w = w.reshape(N, 8, 16, C, 4)
    t = np.zeros_like(w)
    for r in range(N):
        e = gentries(nd[r])
        for g in range(8): t[r, g][:, e[g]] = w[r, g]
    return t.reshape(N, 128, 4 * C).astype(BF)
def weights(rng, still=[], by=1.0):
    w = np.array(f(rng, N, 128, 2048)).reshape(N, 8, 16, 4, 8, 16, 4)
    for i in still:
        w[:, :, i] = 0
        w[:, :, :, :, :, i] = 0
    w = mx_ref.flush((w.astype(np.float32) * np.float32(by)).astype(BF))
    c, s = packed(np.ascontiguousarray(w).reshape(N, 128, 2048), rng)
    return {"wc": c, "ws": s}
def setup_inputs(rng):
    return {**numbers_of(rng), "nd": nodes(rng), "ar": arrows(some_arrows(rng)), **weights(rng)}
def setup_inputs_ties(rng):
    d = numbers_of(rng)
    nd = nodes(rng)
    w = d["x"].reshape(N, 8, 16, C, 4)
    w[:, :, 0] = 0
    w[:, :, 0, :, 0] = rng.integers(1, 4, (N, 8, C)).astype(np.float32).astype(BF)
    u = d["u"].reshape(N, 128, 128, 4)
    u[:, :, ::16] = 0
    o = rng.permutation(N)
    for r in range(N):
        for h in range(0, 128, 16): u[r, h, h, 0] = 0.0 if r == o[0] else -1.0 if r == o[1] else 1.0
    return {"x": laid(w, nd), "u": u.reshape(N, 128, 512), "v": d["v"], "nd": nd, "ar": arrows(some_arrows(rng)), **weights(rng, [0])}
def setup_inputs_near(rng):
    d = numbers_of(rng)
    nd = nodes(rng)
    w = d["x"].astype(np.float32).reshape(N, 8, 16, K, M, 4)
    w[:, :, 0] = 0
    w[:, :, 8:] = 0
    s = rng.integers(0, 16, (N, 8, K, M))
    w[:, :, 8] = ((s[..., None] >> np.arange(4)) & 1) * np.exp2(np.arange(4) - 23.0)
    u = d["u"].reshape(N, 128, 128, 4)
    u[:, :, ::16] = 0
    o = rng.permutation(N) % 4
    for r in range(N):
        k = 1.0 if o[r] == 0 else 2.0 ** -30
        c = rng.choice([-1.0, 1.0], (8, K, 1))
        if o[r] < 2:
            w[r, :, 0, :, :, 0] = c
            w[r, :, 11, :, :, 0] = 2.0 ** -10
        elif o[r] == 2:
            far = np.argsort(rng.random((8, K, M)), axis=2)
            w[r, :, 0, :, :, 0] = 1.0 * (far == 0) - 1.0 * (far == 1)
            for g in rng.permutation(8)[:4]: w[r, g, 0, rng.integers(K), rng.integers(M), 0] = 2.0 ** 26
        else:
            w[r, :, 8] = 0
            w[r, :, 8, :, :, 0] = c * rng.integers(8, 16, (8, K, M)) * 2.0 ** -27
        for h in range(0, 128, 16):
            if o[r] < 2:
                u[r, h, h, 0] = k
                u[r, h + 11, h, 0] = k
            if o[r] == 2: u[r, h, h, 0] = 16.0
            if o[r] < 3: u[r, h + 8, h] = k
            else: u[r, h + 8, h, 0] = k
    return {"x": laid(w, nd), "u": u.reshape(N, 128, 512), "v": d["v"], "nd": nd, "ar": arrows(some_arrows(rng)), **weights(rng, [0, 8, 9, 10, 11, 12, 13, 14, 15])}
def setup_inputs_huge(rng):
    d = numbers_of(rng)
    o = rng.permutation(N)
    a = some_arrows(rng)
    x = 0.8 + 0.1 * rng.random((N, 128, C, 4))
    u = d["u"].reshape(N, 128, 128, 4)
    for r in range(N):
        c = rng.choice([-1.0, 1.0], (C, 1))
        k = 2.0 ** 30 * (1.0 - 0.1 * rng.random((128, 8, 4)))
        if o[r] < 2: c = -np.ones((C, 1))
        if o[r] == 3:
            c = -np.ones((C, 1))
            c[rng.permutation(C)[:K]] = 1.0
            x[r] = 0.9375
            k[:] = 2.0 ** 30
        if o[r] % 2 == 1: a[r] = 0
        x[r] *= c * (2.0 ** 30 if o[r] % 2 == 1 else 2.0 ** 28 if o[r] == 0 else 2.0 ** 27)
        u[r, :, ::16] = k.astype(np.float32).astype(BF)
    return {"x": x.astype(np.float32).reshape(N, 128, 4 * C).astype(BF), "u": u.reshape(N, 128, 512), "v": d["v"], "nd": nodes(rng), "ar": arrows(a), **weights(rng, [], 2.0 ** -14)}
def setup_inputs_knots(rng):
    d = numbers_of(rng)
    e = rng.permutation(N)
    kind = rng.integers(0, 4, (N, 8, K, 1, 1))
    kind[e[0]] = 0
    kind[e[1]] = 1
    sign = rng.choice([-1, 1], (N, 8, K, M, M))
    half = sign * (rng.random((N, 8, K, M, M)) < 0.5)
    a = np.where(kind == 0, 0, np.where(kind == 1, sign * rng.integers(1, 4, (N, 8, K, M, M)), np.where(kind == 2, half, 3 * half)))
    place = np.arange(8)[:, None, None] * 4 + np.arange(4)
    most = place == rng.integers(0, 32, (N, 16, 1, C, 1))
    x = (129.0 + 2.0 * rng.integers(0, 64, (N, 16, 8, C, 4))) * np.exp2(-7.0 - rng.integers(8, 15, (N, 16, 8, C, 4)))
    x = np.where(most, 1.96875, x) * rng.choice([-1.0, 1.0], (N, 16, 8, C, 4)) * np.exp2(rng.integers(-2, 3, (N, 16, 1, C, 1)))
    return {"x": x.astype(np.float32).reshape(N, 128, 4 * C).astype(BF), "u": d["u"], "v": d["v"], "nd": nodes(rng), "ar": arrows(a), **weights(rng)}
def setup_inputs_spread(rng):
    d = setup_inputs(rng)
    d["x"] = wide(rng, N, 128, 4 * C, cols=6)
    return d
def check_inputs(d):
    b = []
    for k in ("x", "u", "v"):
        a = np.abs(d[k].astype(np.float32))
        if not (np.isfinite(a).all() and ((a == 0) | (a >= 2.0 ** -30) & (a <= 2.0 ** 30)).all()): b.append("a value of " + k)
    none, least, most = [emit(mx_ref.quantize(np.full((128, 16), k, np.float32).astype(BF)))[1][0, 0] for k in (0.0, 2.0 ** -30, 2.0 ** 30)]
    for r in range(N):
        if (np.sort(gentries(d["nd"][r]), axis=1) != np.arange(C)).any(): b.append("nd: a group without every column once")
        a = matrices(d["ar"][r])
        if (np.abs(a) > 3).any(): b.append("an entry of ar")
        if (a != -a.swapaxes(-1, -2)).any(): b.append("ar: B[j, i] isn't -B[i, j]")
        if ((d["wc"][r] & 0x7F) == 0x7F).any(): b.append("wc: a code that is no number")
        s = mx_ref.live(d["ws"][r])
        if ((s != none) & ((s < least) | (s > most))).any(): b.append("ws: a scale out of range")
    return b
def parts(t, n, e):
    return gcols(t, np.where(e < 0, -1, np.take_along_axis(n, BASE + np.maximum(e, 0), axis=1))).astype(np.float32)
def pair(t, n, w):
    e = np.argsort(-w, axis=2, kind="stable")[:, :, :2]
    e = np.where(np.take_along_axis(w, e, axis=2) > 0, e, -1)
    return ((parts(t, n, e[:, :, 0]) + parts(t, n, e[:, :, 1])) * np.float32(0.5)).astype(BF).astype(np.float32)
def reference(x, u, v, nd, ar, wc, ws):
    qu = [mx_ref.quantize(u[r]) for r in range(N)]
    lay = [pk(wc[r], ws[r]) for r in range(N)]
    now = [x[r] for r in range(N)]
    node = [gentries(nd[r]) for r in range(N)]
    arrow = [matrices(ar[r]) for r in range(N)]
    for t in range(R):
        held, made, sent, into = [], [], [], []
        for r in range(N):
            q = mx_ref.quantize(now[r])
            own = decode(q).astype(BF)
            s = mx_ref.matmul(qu[r], q)[::16] + np.float32(0.0)
            s = np.take_along_axis(s, node[r], axis=1).reshape(8, K, M)
            first = np.argmax(s, axis=2)
            row = np.take_along_axis(arrow[r], first[:, :, None, None], axis=2)[:, :, 0]
            free = (row == 0) & (np.arange(M) != first[:, :, None])
            second = np.argmax(np.where(free, s, -np.inf), axis=2)
            k = np.concatenate([first, second], axis=1)
            full = np.concatenate([np.ones((8, K), bool), free.any(axis=2)], axis=1)
            row = np.concatenate([row, np.take_along_axis(arrow[r], second[:, :, None, None], axis=2)[:, :, 0]], axis=1) * full[:, :, None]
            y = (np.maximum(pair(own, node[r], -row), pair(own, node[r], row)) - parts(own, node[r], np.where(full, k, -1))).astype(BF)
            held.append(own)
            made.append(y)
            sent.append(mx_ref.quantize(y))
            e = np.tile(np.arange(C), (8, 1))
            g, i = np.nonzero(full)
            e[g, np.take_along_axis(node[r], BASE + k, axis=1)[g, i]] = C + i
            into.append(e)
            more = (np.abs(row)[:, :, :, None] * row[:, :, None, :] - row[:, :, :, None] * np.abs(row)[:, :, None, :]) // 2
            turn = np.ones((8, 2 * K, M), np.int64)
            np.put_along_axis(turn, k[:, :, None], np.where(full, -1, 1)[:, :, None], axis=2)
            turn = turn[:, :K] * turn[:, K:]
            arrow[r] = np.clip(arrow[r] + more[:, :K] + more[:, K:], -3, 3) * turn[:, :, :, None] * turn[:, :, None, :]
        for r in range(N):
            q = sent[(r - 1) % N]
            new = tile([mx_ref.matmul(pick(lay[r], np.arange(128 * b, 128 * b + 128)), q) * np.float32(0.03125) + made[r][:, b::4].astype(np.float32) for b in range(4)])
            now[r] = gcols(np.concatenate([held[r], new], axis=1), into[r])
    y, oa = np.zeros((N, 128, C), np.float32), np.zeros(ar.shape, np.float32)
    oc, osc = np.zeros((N, 128, 4 * C), np.uint8), np.zeros((N, 16, C), np.uint8)
    for r in range(N):
        q = mx_ref.quantize(now[r])
        y[r] = mx_ref.matmul(mx_ref.quantize(v[r]), q)
        oa[r] = stored(arrow[r])
        oc[r], osc[r] = emit(q)
    return {"y": y, "oa": oa, "oc": oc, "osc": osc}

@@ -1,0 +1,486 @@
+from concourse.mybir import dt, AluOpType, ActivationFunctionType
+
+ROUNDS, C = 3, 448
+CUTS = (0, 160, 320, 448)
+XW = 1936
+UNIT = 65536.0
+MARK = 16384.0
+FLOOR = 65536.0 + 4 * 448
+BIG = 2.0 ** 99
+LOW = -(2.0 ** 98)
+RND16 = 1.5 * 2.0 ** 39
+RND0 = 1.5 * 2.0 ** 23
+
+F32, B16, I32, U16, QC, U8 = "float32", "bfloat16", "int32", "uint16", "float8_e4m3fn_x4", "uint8"
+SCRATCH = {"pp": ("psum", [128, 1024], F32), "pd": ("psum", [128, 2048], F32), "pq": ("psum", [128, 1024], F32)}
+for _d, _list in [
+        (B16, "xin 1792 ft0 1936 ft1 1936 ft2 1936 ut 512 vt 512 eb 516 ones 516 ie 528 mask 448 cap16 448 capf 448 rst14 28 "
+              "sg 1344 cw 528 ds0 1024 ds1 1024 ds2 1024 av 160 eq 56 ph0 28 xg 896 st 1344 so 1344 ltb 56 cnt 56 ge 512 "
+              "rf 1024 ag 512 su2 512 ys 512 yd 512 yt 512 y32 256 vv 256"),
+        (F32, "iw 448 r1 448 r2 448 r3 448 ps 448 smk 448 scn 448 pmf 448 oa1 400 wb 256 yo 448 key 113 ep 112 tmn 112 p2 112 "
+              "capz 112"),
+        (I32, "ndin 28 arin 392")]:
+    _w = _list.split()
+    for _k in range(0, len(_w), 2):
+        SCRATCH[_w[_k]] = ("sbuf", [128, int(_w[_k + 1])], _d)
+for _n, _c in [("qw", 512), ("qu", 128), ("qr", 128), ("qv", 128), ("qe", 512), ("qx0", 448), ("qx1", 448), ("qx2", 448),
+               ("qx3", 448), ("qy0", 128), ("qy1", 128), ("qy2", 128), ("ld", 256)]:
+    SCRATCH[_n] = ("sbuf", [128, _c], QC)
+    SCRATCH["s" + _n] = ("sbuf", [128, _c], U8)
+SMALL = {}
+for _buf, _d, _step, _list in [
+        ("smalli", I32, 8, "lane0 56 lane 56 t28a 28 t28b 28 t28c 28 t8 8 ndw 32 ndh 32 ndl 32 dum 2 dum0 2 kc 28 h14 14 d14 14 "
+                           "h196 14 t14a 14 t14b 14 t14c 14 t14d 14 t14e 14 t14f 14 fj 56 fh 56 fi0 56 fi 56 fl 56 "
+                           "fm 56 fn 56 fo 56 f1 56 f2 56 f3 56 f4 56 f5 56 f6 56 f7 56 f8 56 f9 56 fa 56 fx 8 lfi 64 oe0 25 oi 16 "
+                           "oim 16 ow 4"),
+        ("smallu", U16, 16, "lrep 28 lu 8 ndn 28 nd16 28 li 14 lk 14 lc 14 lf 64 loa 25 off 64 ox 16"),
+        ("smallf", F32, 8, "lanef 1 capb 30 nd4 28 kb 28 oe 25 o1 25 o2 25 o3 25 o4 25 pm1 30 pen 28 s2 30")]:
+    _w, _at = _list.split(), 0
+    for _k in range(0, len(_w), 2):
+        SMALL[_w[_k]] = (_buf, _at, int(_w[_k + 1]))
+        _at += (int(_w[_k + 1]) + _step - 1) // _step * _step
+    SCRATCH[_buf] = ("sbuf", [128, _at], _d)
+
+NDMA = 24
+SEMAPHORES = ["cv", "cs", "ct", "cg", "ready", "loc", "arr0", "arr1", "arr2"] + ["dma%d" % _k for _k in range(NDMA)]
+
+
+def rank_program(g, core, T, topo):
+    rank = T.rank_of(core)
+    if rank is None:
+        return
+    A = AluOpType
+    COPY, SIGN, IDENT = ActivationFunctionType.Copy, ActivationFunctionType.Sign, ActivationFunctionType.Identity
+    n = len(T.cores)
+    nxt, prv = T.cores[(rank + 1) % n], T.cores[(rank - 1) % n]
+
+    queue = {"v": g.vector, "s": g.scalar, "t": g.tensor, "g": g, "y": g.sync}
+    semof = {"v": "cv", "s": "cs", "t": "ct", "g": "cg"}
+    count = {"cv": 0, "cs": 0, "ct": 0, "cg": 0}
+    state, seen, ndma = {}, {}, [0]
+
+    def entry(t):
+        return state.setdefault(t, [[], [], [], True])
+
+    def need(q, sem, val):
+        if seen.get((q, sem), 0) < val:
+            queue[q].wait_ge(T.sem[sem], val)
+            seen[(q, sem)] = val
+
+    def order(q, R, W, dma):
+        want = []
+        for t in R:
+            want += entry(t)[0]
+        for t in W:
+            s = entry(t.lstrip("+"))
+            if t[0] != "+" or s[1] or s[3]:
+                s[2] = s[0] + [e for e in s[1] if dma or e[2] != q]
+                s[0], s[1], s[3] = [], [], t[0] != "+"
+            want += s[2]
+        most = {}
+        for sem, val, w in want:
+            most[sem] = max(most.get(sem, 0), val)
+        for sem in most:
+            need(q, sem, most[sem])
+
+    def note(R, W, e):
+        for t in R:
+            entry(t)[1].append(e)
+        for t in W:
+            entry(t.lstrip("+"))[0].append(e)
+
+    def op(q, R, W, f):
+        R, W = R.split(), W.split()
+        order(q, R, W, False)
+        s = semof[q]
+        count[s] += 1
+        f(queue[q]).then_inc(T.sem[s], 1)
+        note(R, W, (s, count[s], q))
+
+    def dma(q, R, W, out, in_):
+        R, W = R.split(), W.split()
+        order(q, R, W, True)
+        s = "dma%d" % ndma[0]
+        ndma[0] += 1
+        queue[q].dma_start(out, in_).then_inc(T.sem[s], 16)
+        note(R, W, (s, 16, "dma"))
+
+    def b(name, lo=0, hi=None, step=1):
+        buf, at, cols = SMALL[name] if name in SMALL else (name, 0, SCRATCH[name][1][1])
+        hi = cols if hi is None else hi
+        return T[buf][:, at + lo:at + hi:step] if step > 1 else T[buf][:, at + lo:at + hi]
+
+    def ts(R, W, out, in0, s1, op0, s2=None, op1=None):
+        if op1 is None:
+            op("v", R, W, lambda e: e.tensor_scalar(out, in0, s1, None, op0))
+        else:
+            op("v", R, W, lambda e: e.tensor_scalar(out, in0, s1, s2, op0, op1))
+
+    def tt(R, W, out, in0, in1, o):
+        op("v", R, W, lambda e: e.tensor_tensor(out, in0, in1, o))
+
+    def cp(R, W, out, in_):
+        op("v", R, W, lambda e: e.tensor_copy(out, in_))
+
+    def fill(W, out, c):
+        op("v", "", W, lambda e: e.memset(out, c))
+
+    def scan(R, W, out, d0, d1, init, o0, o1):
+        op("v", R, W, lambda e: e.tensor_tensor_scan(out, d0, d1, init, o0, o1))
+
+    def act(R, W, out, in_, scale=1.0, func=COPY):
+        if scale == 1.0:
+            op("s", R, W, lambda e: e.activation(out, in_, func))
+        else:
+            op("s", R, W, lambda e: e.activation(out, in_, func, scale=scale))
+
+    def const(W, out, c, cols):
+        op("s", "ie", W, lambda e: e.activation(out, b("ie", 0, cols), IDENT, bias=c, scale=0.0))
+
+    def quant(R, W, q, s, in_):
+        op("v", R, W, lambda e: e.quantize_mx(q, s, in_))
+
+    def mm(R, W, out, a, sa, m, sm):
+        op("t", R, W, lambda e: e.matmul_mx(out, a, sa, m, sm, True, True))
+
+    def iota(W, out, pattern, base, cm, small=False):
+        if small:
+            op("g", "", W, lambda e: e.iota(out, pattern, base, cm, allow_small_or_imprecise_dtypes=True))
+        else:
+            op("g", "", W, lambda e: e.iota(out, pattern, base, cm))
+
+    dma("y", "", "ndin", b("ndin"), T.nd[:, :])
+    dma("s", "", "xb", b("xin", 896, 1792), T.x[:, 896:1792])
+    dma("y", "", "ut", b("ut"), T.u[:, :])
+    dma("y", "", "xa", b("xin", 0, 896), T.x[:, 0:896])
+    dma("y", "", "arin", b("arin"), T.ar[:, :])
+    dma("y", "", "sw", b("sqw"), T.ws[:, :])
+    dma("y", "", "qw", T.qw[:, :].bitcast(dt.uint8), T.wc[:, :])
+    dma("y", "", "vt", b("vt"), T.v[:, :])
+
+    iota("lane0", b("lane0"), [[0, 56]], 0, 1)
+    iota("fi0", b("fi0"), [[0, 28], [8, 2]], 0, 0)
+    iota("fj", b("fj"), [[0, 2], [1, 14], [0, 2]], 0, 0)
+    iota("t28a", b("t28a"), [[224, 2], [1, 14]], 0, 0)
+    iota("d14", b("d14"), [[0, 2], [1, 7]], 1, 0)
+    iota("fh", b("fh"), [[112, 2], [0, 28]], 0, 0)
+    iota("t8", b("t8"), [[16, 8]], 0, 0)
+    iota("iw", b("iw"), [[1, 448]], 0, 0, True)
+    iota("ie", b("ie"), [[0, 33], [1, 16]], 0, 0, True)
+    iota("h14", b("h14"), [[14, 2], [0, 7]], 0, 0)
+    iota("h196", b("h196"), [[196, 2], [0, 7]], 0, 0)
+    iota("+fx", b("fx", 0, 4), [[32, 2], [8, 2]], 448, 0)
+    iota("+fx", b("fx", 4, 8), [[32, 2], [8, 2]], 464, 0)
+    iota("dum0", b("dum0"), [[16, 2]], 449, 0)
+
+    fill("cap16", b("cap16"), BIG)
+    ts("lane0", "lane", b("lane"), b("lane0"), 15, A.bitwise_and)
+    ts("lane", "fm", b("fm"), b("lane"), 1, A.arith_shift_right)
+    ts("lane", "fn", b("fn"), b("lane"), 1, A.bitwise_and)
+    ts("lane", "t28b", b("t28b"), b("lane", 0, 28), 14, A.mult)
+    tt("fm fn", "fo", b("fo"), b("fm"), b("fn"), A.subtract)
+    ts("lane", "t14e", b("t14e"), b("lane", 0, 14), 14, A.mult)
+    ts("fo", "fl", b("fl"), b("fo"), 1, A.add)
+    cp("lane", "lanef", b("lanef"), b("lane", 0, 1))
+    tt("fl fi0", "fi", b("fi"), b("fl"), b("fi0"), A.add)
+    fill("cap16", b("cap16", 0, 448, 16), -BIG)
+    tt("fi fj", "f1", b("f1"), b("fi"), b("fj"), A.subtract)
+    tt("t28b t28a", "t28c", b("t28c"), b("t28b"), b("t28a"), A.add)
+    ts("f1", "f2", b("f2"), b("f1"), 0, A.is_lt, 14, A.mult)
+    cp("t28c", "lrep", b("lrep"), b("t28c"))
+    tt("f1 f2", "f3", b("f3"), b("f1"), b("f2"), A.add)
+    tt("d14 lane", "t14a", b("t14a"), b("d14"), b("lane", 0, 14), A.add)
+    ts("f3", "f4", b("f4"), b("f3"), 16, A.mult, -16, A.add)
+    ts("f3", "f6", b("f6"), b("f3"), -16, A.mult, 432, A.add)
+    cp("ndin", "ndn", b("ndn"), b("ndin"))
+    act("iw ndn", "r1", b("r1"), T.iw[:, 0:448].indirect(b("ndn")))
+    const("ones", b("ones"), 1.0, 516)
+    op("g", "ones", "eb", lambda e: e.affine_select(b("eb"), b("ones"), [[-1, 516]], A.is_equal, 0.0, 3, 4))
+    iota("kc", b("kc"), [[0, 2], [-2048, 14]], 14 * 2048, 0)
+    iota("ds0", b("ds0"), [[0, 512], [-1, 2]], 0, 0, True)
+    ts("f3", "f8", b("f8"), b("f3"), 7, A.is_le)
+    tt("f4 fj", "f5", b("f5"), b("f4"), b("fj"), A.add)
+    tt("f6 fi", "f7", b("f7"), b("f6"), b("fi"), A.add)
+    ts("t14a", "t14b", b("t14b"), b("t14a"), 14, A.is_ge, -14, A.mult)
+    tt("f5 f7", "f9", b("f9"), b("f5"), b("f7"), A.subtract)
+    ts("f3", "f4", b("f4"), b("f3"), 0, A.is_equal, 512, A.mult)
+    tt("f8 f9", "fa", b("fa"), b("f8"), b("f9"), A.mult)
+    tt("t14a t14b", "t14c", b("t14c"), b("t14a"), b("t14b"), A.add)
+    tt("fa f7", "f1", b("f1"), b("fa"), b("f7"), A.add)
+    ts("fi", "f6", b("f6"), b("fi"), 14, A.is_ge, 513, A.mult)
+    tt("f1 fh", "f2", b("f2"), b("f1"), b("fh"), A.add)
+    cp("t8", "lu", b("lu"), b("t8"))
+    tt("f2 f4", "f5", b("f5"), b("f2"), b("f4"), A.max)
+    ts("ie lanef", "mask0", b("mask"), b("ie", 0, 448), b("lanef"), A.is_equal, BIG, A.mult)
+    tt("f5 f6", "+lfi", b("lfi", 4, 60), b("f5"), b("f6"), A.max)
+    quant("ut", "qu", b("qu"), b("squ"), b("ut"))
+    ts("mask0", "mask", b("mask"), b("mask"), LOW, A.add)
+    op("v", "qu lu", "qr", lambda e: e.tensor_copy(T.qr[:, 0:128].bitcast(dt.uint32), T.qu[:, 0:128].bitcast(dt.uint32).indirect(b("lu"))))
+    act("qu lu", "sr", b("sqr"), T.squ[:, 0:128].indirect(b("lu")))
+    tt("r1 lrep mask", "r2", b("r2"), T.r1[:, 0:448].indirect(b("lrep")), b("mask"), A.min)
+    tt("t14e h196", "t14f", b("t14f"), b("t14e"), b("h196"), A.add)
+    scan("cap16 r2", "r3", b("r3"), b("cap16"), b("r2"), 0.0, A.min, A.max)
+    const("yt", b("yt"), 0.0, 512)
+    const("capf", b("capf"), BIG, 448)
+    const("capz", b("capz"), BIG, 112)
+    const("av0 av1 av2", b("av"), 0.0, 160)
+    for h in range(2):
+        act("ie", "+rst14", b("rst14", 14 * h, 14 * h + 14), b("ie", 0, 14), 1.0, SIGN)
+    for t in range(ROUNDS):
+        const("fz%d" % t, b("ft%d" % t, 1792, XW), 0.0, XW - 1792)
+
+    def bank(k, cols):
+        return (T.pp[:, 0:cols], T.pp[:, 512:512 + cols], T.pq[:, 0:cols])[k]
+
+    def quantise_state(r, src, ta, tb):
+        qx, sx = T["qx%d" % r], T["sqx%d" % r]
+        for k in range(3):
+            lo, hi = CUTS[k], CUTS[k + 1]
+            quant((ta, ta + " " + tb, tb)[k], "q%d%d" % (k, r), qx[:, lo:hi], sx[:, lo:hi], src[:, 4 * lo:4 * hi])
+        return qx, sx
+
+    def begin(r, src, ta, tb):
+        qx, sx = quantise_state(r, src, ta, tb)
+        if r == 0:
+            cp("r3", "nd16", b("nd16"), b("r3", 15, 448, 16))
+            for k in range(4):
+                quant("eb", "+qe", T.qe[:, 128 * k:128 * k + 128], T.sqe[:, 128 * k:128 * k + 128], T.eb[:, 3 - k:515 - k])
+        for k in range(3):
+            lo, hi = CUTS[k], CUTS[k + 1]
+            mm("qr sr q%d%d" % (k, r), ("pp0", "pp1", "pq0")[k], bank(k, hi - lo), b("qr"), b("sqr"), qx[:, lo:hi], sx[:, lo:hi])
+        for k in range(4):
+            mm("qe q0%d q1%d q2%d" % (r, r, r), "pd%d" % k, T.pd[:, 512 * k:512 * k + 448], T.qe[:, 128 * k:128 * k + 128],
+               T.sqe[:, 128 * k:128 * k + 128], qx[:, 0:448], sx[:, 0:448])
+        act("pp0", "ps0", b("ps", 0, 160), bank(0, 160))
+        act("pp1", "ps1", b("ps", 160, 320), bank(1, 160))
+
+    def decode(r):
+        ft = "ft%d" % r
+        for k in range(4):
+            act("pd%d" % k, "+" + ft, b(ft, k, 1792, 4), T.pd[:, 512 * k:512 * k + 448])
+
+    def stored():
+        act("cst", "cw0", b("cw", 0, 224), b("st", 0, 1344, 6))
+        act("cst", "cw1", b("cw", 224, 448), b("st", 0, 1344, 6), -1.0)
+
+    def lay_out():
+        act("cw0 cw1 cwk cwn lf", "ds1", b("ds1"), T.cw[:, 0:528].indirect(b("lf")))
+
+    begin(0, T.xin, "xa", "xb")
+    quant("yt", "ldz", b("ld", 128, 256), b("sld", 128, 256), b("yt"))
+    mask = topo.mask(core, prv)
+    rid, pid = topo.addr(prv)[:2]
+    order("g", ["ldz"], [], False)
+    g.remote_sem_update(T.sem["ready"], T.sem["loc"], pid, rid, mask)
+    nloc = [len(topo.engines(core, prv))]
+    iota("yd", b("yd"), [[0, 256], [1, 2]], 0, 0, True)
+    for s, c in ((0, 0), (3, 1), (4, -1), (5, 1)):
+        iota("+sgc", b("sg", s, 1344, 6), [[0, 224]], c, 0, True)
+    iota("st1", b("st", 1, 1344, 6), [[0, 224]], 0, 0, True)
+    iota("oe0", b("oe0"), [[16, 25]], 0, 0)
+    fill("ndw", b("ndw"), 0)
+    tt("t14f t14c", "t14g", b("t14a"), b("t14f"), b("t14c"), A.add)
+    tt("dum0 lane", "dum", b("dum"), b("dum0"), b("lane", 0, 2), A.add)
+    for h in range(2):
+        cp("r3", "+ndw", b("ndw", 16 * h, 16 * h + 14), b("r3", 224 * h + 15, 224 * h + 224, 16))
+    ts("t14g", "t14h", b("t14f"), b("t14a"), 391, A.min)
+    cp("dum", "+ndw", b("ndw", 14, 32, 16), b("dum"))
+    tt("fx fl", "+lfi", b("lfi", 0, 4), b("fx", 0, 4), b("fl", 0, 4), A.add)
+    cp("t14h", "lc", b("lc"), b("t14f"))
+    ts("ndw", "ndh", b("ndh"), b("ndw"), 4, A.arith_shift_right)
+    ts("ndw", "ndl", b("ndl"), b("ndw"), 15, A.bitwise_and)
+    tt("fx fl", "+lfi", b("lfi", 60, 64), b("fx", 4, 8), b("fl", 0, 4), A.add)
+    ts("arin lc", "cst", b("st", 0, 1344, 6), T.arin[:, 0:392].indirect(b("lc")), UNIT, A.mult)
+    stored()
+    fill("cwk", b("cw", 512, 528), 0.0)
+    ts("ndh", "+cwn", b("cw", 448, 480), b("ndh"), 64, A.mult)
+    ts("ndl", "+cwn", b("cw", 480, 512), b("ndl"), 4, A.mult)
+    fill("cwk", b("cw", 512, 513), MARK)
+    cp("lfi", "lf", b("lf"), b("lfi"))
+    fill("capf", b("capf", 0, 448, 224), -BIG)
+    lay_out()
+    decode(0)
+
+    def rows(k):
+        return b("rf", 512 * k + 46, 512 * k + 46 + 28 * 16 - 15, 16)
+
+    def column(k):
+        ts("rf%d" % k, "+av0", b("av", 64 + 32 * k, 92 + 32 * k), rows(k), RND16, A.add, RND16, A.subtract)
+
+    def turned(k, h):
+        o = 28 * k + 14 * h
+        ts("ie cnt%d" % k, "+eq", b("eq", o, o + 14), b("ie", 0, 14), b("cnt", o + 13, o + 14), A.is_equal)
+
+    def slot(t):
+        ts("ow", "+ox", b("ox", 4 * t, 4 * t + 4), b("ow"), t, A.add)
+
+    def choose(k, tok, pm, beside):
+        o = 28 * k
+        for h in range(2):
+            ts(tok, "+lt%d" % k, b("ltb", o + 14 * h, o + 14 * h + 14), pm(h)[0], pm(h)[1], A.is_lt)
+        beside[0]()
+        scan("rst14 lt%d" % k, "cnt%d" % k, b("cnt", o, o + 28), b("rst14"), b("ltb", o, o + 28), 0.0, A.mult, A.add)
+        beside[1]()
+        for h in range(2):
+            ts("ie cnt%d" % k, "+ge", b("ge", 256 * h, 256 * h + 256), b("ie", 256 * h, 256 * h + 256), b("cnt", o + 14 * h + 13, o + 14 * h + 14), A.is_gt)
+        beside[2]()
+        scan("ge ds2", "rf%d" % k, b("rf", 512 * k, 512 * k + 512), b("ge"), b("ds2", 1, 1024, 2), 0.0, A.mult, A.add)
+
+    def differences():
+        scan("ds0 ds1", "ds2", b("ds2"), b("ds0"), b("ds1"), 0.0, A.mult, A.add)
+
+    def scores():
+        scan("cap16 smk", "scn", b("scn"), b("cap16"), b("smk"), 0.0, A.min, A.max)
+
+    def nothing():
+        return None
+
+    def late_constants():
+        ts("r3", "nd4", b("nd4"), b("r3", 15, 448, 16), 4.0, A.mult)
+        tt("h14 lane", "t14b", b("t14b"), b("h14"), b("lane", 0, 14), A.add)
+        tt("t14c h14", "t14d", b("t14d"), b("t14c"), b("h14"), A.add)
+        fill("capb", b("capb"), BIG)
+        tt("nd4 kc", "kb", b("kb"), b("nd4"), b("kc"), A.add)
+        fill("s2z", b("s2"), LOW)
+        cp("t14b", "li", b("li"), b("t14b"))
+        cp("t14d", "lk", b("lk"), b("t14d"))
+        fill("capb", b("capb", 0, 30, 15), -BIG)
+        fill("key0", b("key", 0, 1), 0.0)
+        fill("capz", b("capz", 0, 112, 14), FLOOR)
+
+    rid, pid = topo.addr(nxt)[:2]
+    mask = topo.mask(core, nxt)
+    engines = len(topo.engines(core, nxt))
+
+    for r in range(ROUNDS):
+        ft, fz = "ft%d" % r, "ft%d fz%d" % (r, r)
+        if r:
+            begin(r, T["ft%d" % (r - 1)], "ft%d" % (r - 1), "ft%d" % (r - 1))
+            decode(r)
+            differences()
+        cp("pq0", "ps2", b("ps", 320, 448), bank(2, 128))
+        tt("ps0 ps1 ps2 nd16 mask", "smk", b("smk"), T.ps[:, 0:448].indirect(b("nd16")), b("mask"), A.min)
+        if r == 0:
+            late_constants()
+        scan("capf smk", "pmf", b("pmf"), b("capf"), b("smk"), 0.0, A.min, A.max)
+        choose(0, "pmf", lambda h: (b("pmf", 224 * h + 15, 224 * h + 224, 16), b("pmf", 224 * h + 223, 224 * h + 224)),
+               [scores, differences if r == 0 else nothing, nothing])
+        ts("rf0", "pen", b("pen"), rows(0), 0.0, A.not_equal, -BIG, A.mult)
+        turned(0, 0)
+        for h in range(2):
+            tt("scn pen s2z", "+s2", b("s2", 15 * h, 15 * h + 14), b("scn", 224 * h + 15, 224 * h + 224, 16), b("pen", 14 * h, 14 * h + 14), A.add)
+        turned(0, 1)
+        scan("capb s2 s2z", "pm1", b("pm1"), b("capb"), b("s2"), 0.0, A.min, A.max)
+        tt("rf0", "+ow", b("ow", 0, 2), b("rf", 14, 495, 480), b("rf", 30, 511, 480), A.add)
+        choose(1, "pm1", lambda h: (b("pm1", 15 * h, 15 * h + 14), b("pm1", 15 * h + 14, 15 * h + 15)),
+               [lambda: tt("kb rf0", "+key", b("key", 1, 29), b("kb"), rows(0), A.add),
+                lambda: tt("kb rf0", "+key", b("key", 57, 85), b("kb"), rows(0), A.subtract), nothing])
+        column(0)
+        tt("kb rf1", "+key", b("key", 29, 57), b("kb"), rows(1), A.add)
+        tt("kb rf1", "+key", b("key", 85, 113), b("kb"), rows(1), A.subtract)
+        tt("rf1", "+ow", b("ow", 2, 4), b("rf", 526, 1007, 480), b("rf", 542, 1023, 480), A.add)
+        scan("key key0 capz", "ep", b("ep"), b("key", 0, 112), b("capz"), BIG, A.max, A.min)
+        slot(0)
+        tt("ep key", "tmn", b("tmn"), b("ep"), b("key", 1, 113), A.min)
+        tt("ep key", "+oi", b("oi", 0, 8), b("ep", 13, 112, 14), b("key", 14, 113, 14), A.max)
+        scan("capz tmn", "p2", b("p2"), b("capz"), b("tmn"), FLOOR, A.min, A.max)
+        slot(1)
+        cp("p2", "+oi", b("oi", 8, 16), b("p2", 13, 112, 14))
+        slot(2)
+        ts("oi", "oim", b("oim"), b("oi"), 2047, A.bitwise_and)
+        slot(3)
+        for t in range(4):
+            ts("oim", "off%d" % t, b("off", 16 * t, 16 * t + 16), b("oim"), t, A.add)
+        column(1)
+        turned(1, 0)
+        ts("av0", "av1", b("av", 0, 64), b("av", 64, 128), -1.0 / UNIT, A.mult, 0.0, A.max)
+        for t in range(4):
+            act(fz + " off%d" % t, "ag%d" % t, b("ag", t, 512, 4), T[ft][:, 0:XW].indirect(b("off", 16 * t, 16 * t + 8)))
+        for t in range(4):
+            act(fz + " ox", "+own", b("ys", 2 * t + 1, 512, 8), T[ft][:, 0:XW].indirect(b("ox", 4 * t, 4 * t + 4)), -2.0)
+        for t in (2, 3, 0, 1):
+            act("av%d li" % (0 if t > 1 else 1), "xg%d" % t, b("xg", 224 * t, 224 * t + 224), T.av[:, 32 * t:32 * t + 32].indirect(b("li")))
+        for t in range(4):
+            tt(fz + " off%d ag%d" % (t, t), "+su", b("su2", t, 512, 4), T[ft][:, 0:XW].indirect(b("off", 16 * t + 8, 16 * t + 16)), b("ag", t, 512, 4), A.add)
+        turned(1, 1)
+        tt("su", "mm", b("ys", 0, 512, 2), b("su2", 0, 256), b("su2", 256, 512), A.max)
+        tt("eq", "ph0", b("ph0"), b("eq", 0, 28), b("eq", 28, 56), A.add)
+        scan("yd mm own", "y2", b("ag"), b("yd"), b("ys"), 0.0, A.mult, A.add)
+        ts("ph0", "av2", b("av", 128, 156), b("ph0"), -2.0, A.mult, 1.0, A.add)
+        act("av2 li", "+sgp", b("sg", 1, 1344, 6), T.av[:, 128:160].indirect(b("li")), -1.0)
+        act("av2 lk", "+sgp", b("sg", 2, 1344, 6), T.av[:, 128:160].indirect(b("lk")))
+        ts("y2", "yt ag0 ag1 ag2 ag3", b("yt", 0, 256), b("ag", 1, 512, 2), 0.5, A.mult)
+        quant("yt", "qy%d" % r, T["qy%d" % r][:, 0:128], T["sqy%d" % r][:, 0:128], b("yt"))
+        order("g", ["qy%d" % r], [], False)
+        if r == 0:
+            g.wait_ge(T.sem["ready"], len(topo.engines(nxt, core)))
+        arr, at = "arr%d" % r, 64 * (ROUNDS - 1 - r)
+        g.remote_dma(T.ld[:, at:at + 64].bitcast(dt.uint8), T["qy%d" % r][:, 0:64].bitcast(dt.uint8), T.sem[arr], T.sem["loc"], pid, rid, mask)
+        g.remote_dma(T.sld[:, at:at + 64], T["sqy%d" % r][:, 0:64], T.sem[arr], T.sem["loc"], pid, rid, mask)
+        nloc[0] += 2 * engines
+        for t in (2, 3, 0, 1):
+            w = (64 + 32 * t) % 128
+            tt("av0 av1 lk xg%d" % t, "+pr", b("st", 2 + t, 1344, 6), T.av[:, w:w + 32].indirect(b("lk")), b("xg", 224 * t, 224 * t + 224), A.mult)
+        act("yt", "y32", b("y32"), b("yt", 0, 256), 32.0)
+        scan("sgc sgp st1 cst pr", "so", b("so"), b("sg"), b("st"), 0.0, A.mult, A.add)
+        ts("so", "cst", b("st", 0, 1344, 6), b("so", 5, 1344, 6), 3 * UNIT, A.min, -3 * UNIT, A.max)
+        if r == 0:
+            quant("vt", "qv", b("qv"), b("sqv"), b("vt"))
+        if r == ROUNDS - 1:
+            fill("cwk", b("cw", 512, 513), 0.0)
+            tt("oe0 lane", "oe", b("oe"), b("oe0"), b("lane", 0, 25), A.add)
+            ts("oe", "o1", b("o1"), b("oe"), -6.5, A.add, 1.0 / 14.0, A.mult)
+            ts("o1", "o2", b("o2"), b("o1"), RND0, A.add, RND0, A.subtract)
+            ts("o2", "o3", b("o3"), b("o2"), 2.0, A.mult, 32.5, A.add)
+            tt("o3 oe", "o4", b("o4"), b("o3"), b("oe"), A.add)
+            ts("o4", "loa", b("loa"), b("o4"), 2.0, A.mult)
+        stored()
+        lay_out()
+        if r == ROUNDS - 1:
+            act("ds1 loa", "oa1", b("oa1"), T.ds1[:, 0:1024].indirect(b("loa")), 1.0 / UNIT)
+            dma("y", "oa1", "", T.oa[:, :], b("oa1", 0, 392))
+        order("t", [], ["land%d" % r], False)
+        entry("land%d" % r)[0].append((arr, 2 * len(topo.engines(prv, core)), "remote"))
+        toks = ("pq0", "pq1", "pp0", "pp1")
+
+        def place(k, cols):
+            return T.pq[:, 512 * k:512 * k + cols] if k < 2 else T.pp[:, 512 * (k - 2):512 * (k - 2) + cols]
+
+        def sum_(k):
+            tt(toks[k] + " y32", "+wb%d" % (k // 2), b("wb", 64 * k, 64 * k + 64), place(k, 64), b("y32", k, 256, 4), A.add)
+
+        def scaled(k):
+            ts("wb%d" % k, "vv%d" % k, b("vv", 128 * k, 128 * k + 128), b("wb", 128 * k, 128 * k + 128), 0.03125, A.mult)
+
+        def scatter(k):
+            cp("vv%d ox" % k, ft, T[ft][:, 0:XW].indirect(b("ox", 8 * k, 8 * k + 8)), b("vv", 128 * k, 128 * k + 128))
+
+        for k in range(4):
+            mm("qw sw ldz land%d" % r, toks[k], place(k, 128), T.qw[:, 128 * k:128 * k + 128], T.sqw[:, 128 * k:128 * k + 128],
+               b("ld", at, at + 128), b("sld", at, at + 128))
+        sum_(0)
+        sum_(1)
+        sum_(2)
+        scaled(0)
+        sum_(3)
+        scatter(0)
+        scaled(1)
+        scatter(1)
+    qx, sx = quantise_state(3, T[ft], ft, ft)
+    for k in range(3):
+        lo, hi = CUTS[k], CUTS[k + 1]
+        mm("qv q%d3" % k, ("pp0", "pp1", "pq0")[k], bank(k, hi - lo), b("qv"), b("sqv"), qx[:, lo:hi], sx[:, lo:hi])
+    act("pp0", "yo0", b("yo", 0, 160), bank(0, 160))
+    act("pp1", "yo1", b("yo", 160, 320), bank(1, 160))
+    cp("pq0", "yo2", b("yo", 320, 448), bank(2, 128))
+    dma("y", "q03 q13", "", T.oc[:, 0:1280], qx[:, 0:320].bitcast(dt.uint8))
+    dma("s", "yo0 yo1", "", T.y[:, 0:320], b("yo", 0, 320))
+    dma("y", "yo2", "", T.y[:, 320:448], b("yo", 320, 448))
+    dma("s", "q23", "", T.oc[:, 1280:1792], qx[:, 320:448].bitcast(dt.uint8))
+    for k in range(4):
+        dma("sy"[k % 2], "q03 q13 q23", "", T.osc[4 * k:4 * k + 4, 0:448], sx[32 * k:32 * k + 4, 0:448])
+    g.wait_ge(T.sem["loc"], nloc[0])
+    for k in range(ndma[0]):
+        need("y", "dma%d" % k, 16)
+    for s in ("cv", "cs", "ct", "cg"):
+        need("y", s, count[s])

@@ -4,483 +4,455 @@ ROUNDS, C = 3, 448
 CUTS = (0, 160, 320, 448)
 XW = 1936
 UNIT = 65536.0
-MARK = 16384.0
+MARK = 0.125
+LIFT = 192.0
 FLOOR = 65536.0 + 4 * 448
 BIG = 2.0 ** 99
-LOW = -(2.0 ** 98)
-RND16 = 1.5 * 2.0 ** 39
-RND0 = 1.5 * 2.0 ** 23
+OUT = -(2.0 ** 98)
+NONE = -(2.0 ** 97)
+RND64 = 1.5 * 2.0 ** 29
+OPT = {"acc": 1, "pcopy": "ssv", "scat": 2, "join": 0}
 
 F32, B16, I32, U16, QC, U8 = "float32", "bfloat16", "int32", "uint16", "float8_e4m3fn_x4", "uint8"
-SCRATCH = {"pp": ("psum", [128, 1024], F32), "pd": ("psum", [128, 2048], F32), "pq": ("psum", [128, 1024], F32)}
+SCRATCH = {"pa": ("psum", [128, 2048], F32), "pb": ("psum", [128, 2048], F32)}
 for _d, _list in [
-        (B16, "xin 1792 ft0 1936 ft1 1936 ft2 1936 ut 512 vt 512 eb 516 ones 516 ie 528 mask 448 cap16 448 capf 448 rst14 28 "
-              "sg 1344 cw 528 ds0 1024 ds1 1024 ds2 1024 av 160 eq 56 ph0 28 xg 896 st 1344 so 1344 ltb 56 cnt 56 ge 512 "
-              "rf 1024 ag 512 su2 512 ys 512 yd 512 yt 512 y32 256 vv 256"),
-        (F32, "iw 448 r1 448 r2 448 r3 448 ps 448 smk 448 scn 448 pmf 448 oa1 400 wb 256 yo 448 key 113 ep 112 tmn 112 p2 112 "
-              "capz 112"),
-        (I32, "ndin 28 arin 392")]:
+        (B16, "xin 1792 ft0 1936 ft1 1936 ft2 1936 ut 512 vt 512 eb 516 ones 516 ie 256 mask 224 cap 224 cw 512 tab 464 dif 512 "
+              "ge 512 rf 1056 jk 64 ag 256 ea 768 ec 768 eo 768 yt 512 y32 256 wb 256 vv 256 ia 672 ib 672 ja 672 jb 672 so 672 "
+              "tm 64 rl 64 gt 64 pv 64 gv 64 lt 64 rst 32 cnb 32"),
+        (F32, "iw 448 r1 448 r2 448 r3 448 ps 448 smk 448 scn 448 pmf 448 oa1 400 yo 448 key 144 top 256 capz 64 capb 32 sc 8 "
+              "cnt 4 pen 32 s2 32 pm1 32 nd4 40 dn 32 kc 32 kb 32 hrow 14 ka 8 kd 8 kk 8 fa 14 fb 14 fc 14 fd 14 fe 14 ff 14 "
+              "fg 14 fh 14 fi 14 oe 25 o2 25 o3 25"),
+        (I32, "ndin 28 arin 392 lane0 1 lane 1 oi 16 oim 16 o1 25"),
+        (U16, "lrep 14 lu 8 ndn 28 nd16 28 li 14 li16 14 lk 14 lk16 14 lc 14 lf 28 loa 26 off 64 ox 16")]:
     _w = _list.split()
     for _k in range(0, len(_w), 2):
         SCRATCH[_w[_k]] = ("sbuf", [128, int(_w[_k + 1])], _d)
 for _n, _c in [("qw", 512), ("qu", 128), ("qr", 128), ("qv", 128), ("qe", 512), ("qx0", 448), ("qx1", 448), ("qx2", 448),
-               ("qx3", 448), ("qy0", 128), ("qy1", 128), ("qy2", 128), ("ld", 256)]:
+               ("qx3", 448), ("qy", 768), ("ld", 320)]:
     SCRATCH[_n] = ("sbuf", [128, _c], QC)
     SCRATCH["s" + _n] = ("sbuf", [128, _c], U8)
-SMALL = {}
-for _buf, _d, _step, _list in [
-        ("smalli", I32, 8, "lane0 56 lane 56 t28a 28 t28b 28 t28c 28 t8 8 ndw 32 ndh 32 ndl 32 dum 2 dum0 2 kc 28 h14 14 d14 14 "
-                           "h196 14 t14a 14 t14b 14 t14c 14 t14d 14 t14e 14 t14f 14 fj 56 fh 56 fi0 56 fi 56 fl 56 "
-                           "fm 56 fn 56 fo 56 f1 56 f2 56 f3 56 f4 56 f5 56 f6 56 f7 56 f8 56 f9 56 fa 56 fx 8 lfi 64 oe0 25 oi 16 "
-                           "oim 16 ow 4"),
-        ("smallu", U16, 16, "lrep 28 lu 8 ndn 28 nd16 28 li 14 lk 14 lc 14 lf 64 loa 25 off 64 ox 16"),
-        ("smallf", F32, 8, "lanef 1 capb 30 nd4 28 kb 28 oe 25 o1 25 o2 25 o3 25 o4 25 pm1 30 pen 28 s2 30")]:
-    _w, _at = _list.split(), 0
-    for _k in range(0, len(_w), 2):
-        SMALL[_w[_k]] = (_buf, _at, int(_w[_k + 1]))
-        _at += (int(_w[_k + 1]) + _step - 1) // _step * _step
-    SCRATCH[_buf] = ("sbuf", [128, _at], _d)
 
-NDMA = 24
-SEMAPHORES = ["cv", "cs", "ct", "cg", "ready", "loc", "arr0", "arr1", "arr2"] + ["dma%d" % _k for _k in range(NDMA)]
+NDMA = 20
+SEMAPHORES = ["cv", "cs", "ct", "cg", "loc"] + ["arr%d" % _k for _k in range(2 * ROUNDS)] + ["dma%d" % _k for _k in range(NDMA)]
+
+ORDER = [int(_k) for _k in """
+10 8 0 1 4 2 3 7 9 6 5 15 11 73 58 71 66 16 54 17 23 75 72 55 20 37 26 64 25 62 22 38 18 56 60 63 27 24 19 39 87 28 40 53 89 41 12 14 42 32 43 13 88 44 94 111 109 78 45 95 110 80 59 69 79 21 90 70 76 114 112 115 67 113 98 97 29 46 91 96 77 116 117 105 106 93 92 81 118 107 65 61 47 100 99 128 108 101 134 82 129 119 74 135 131 57 103 127 137 102 126 123 104 132 138 83 122 133 120 139 130 68 143 140 136 84 141 158 144 121 159 142 145 160 146 149 124 161 147 150 162 148 125 151 152 163 153 198 199 164 156 166 168 192 200 167 193 154 165 201 172 85 169 170 202 174 173 203 171 155 157 175 196 207 176 206 214 194 195 204 177 35 178 197 212 222 205 208 215 210 213 209 181 211 34 30 216 179 180 217 48 36 218 219 224 189 33 220 86 183 49 31 227 223 50 226 51 228 221 187 182 185 52 190 238 236 242 240 237 239 184 241 246 225 243 247 186 248 244 250 188 249 251 245 254 252 191 253 255 230 256 257 229 258 259 261 260 262 231 263 264 265 270 232 266 234 269 277 233 283 267 235 278 268 284 280 279 286 275 281 276 287 273 274 282 288 289 285 336 292 302 290 308 293 307 291 294 309 295 301 333 298 272 310 296 299 311 297 271 300 312 341 332 347 348 314 306 313 349 319 315 316 331 317 371 350 342 320 323 351 321 318 305 352 324 304 303 353 322 344 357 354 356 372 325 359 355 363 358 330 361 326 360 327 346 364 343 328 362 345 329 373 334 365 339 366 335 370 367 338 368 369 337 340 386 388 390 375 385 387 392 389 391 393 374 379 376 378 394 396 395 377 397 398 399 400 401 402 403 405 404 406 407 408 410 409 411 380 413 412 414 417 381 415 383 419 426 382 432 416 384 427 418 433 429 428 435 423 424 430 425 436 421 431 437 438 434 441 439 457 456 451 442 422 420 481 440 458 480 443 459 444 450 447 531 460 445 453 485 455 448 452 446 454 449 461 490 497 464 496 465 462 470 498 483 466 491 463 499 472 471 500 468 520 467 492 501 487 469 473 503 495 502 474 508 493 505 504 521 475 506 509 494 476 510 522 507 512 477 482 478 525 511 513 488 514 484 515 486 523 524 516 517 526 518 489 479 528 535 537 538 527 542 536 541 539 540 519 529 543 530 546 544 545 532 548 533 547 549 550 552 534 551 553 555 554 556 557 559 560 562 561 563 565 571 568 564 569 573 558 566 567 572 574 570 575
+""".split()]
+
+
+def calls(core, T, topo):
+    A = AluOpType
+    COPY, SIGN = ActivationFunctionType.Copy, ActivationFunctionType.Sign
+    IDENT, RELU = ActivationFunctionType.Identity, ActivationFunctionType.Relu
+    rank, n = T.rank_of(core), len(T.cores)
+    nxt = T.cores[(rank + 1) % n]
+    rid, pid = topo.addr(nxt)[:2]
+    mask = topo.mask(core, nxt)
+    L = []
+
+    def b(name, lo=0, hi=None, step=1):
+        hi = SCRATCH[name][1][1] if hi is None else hi
+        ap = T[name][:, lo:hi:step] if step > 1 else T[name][:, lo:hi]
+        if SCRATCH[name][0] == "psum":
+            return ap, [(name, 1 << (lo // 512))]
+        bits = 0
+        for c in range(lo, hi, step):
+            bits |= 1 << c
+        return ap, [(name, bits)]
+
+    def by(win, off):
+        return win[0].indirect(off[0]), win[1], off[1]
+
+    def bank(k, cols):
+        return b("pa" if k < 4 else "pb", 512 * (k % 4), 512 * (k % 4) + cols)
+
+    def op(q, f, outs, ins, kind="c"):
+        R, W = [], []
+        for v in ins:
+            if isinstance(v, tuple):
+                R += v[1] + (v[2] if len(v) > 2 else [])
+        for v in outs:
+            W += v[1]
+            R += v[2] if len(v) > 2 else []
+        L.append((q, f, R, W, kind))
+
+    def x(v):
+        return v[0] if isinstance(v, tuple) else v
+
+    def ts(out, in0, s1, op0, s2=None, op1=None):
+        if op1 is None:
+            op("v", lambda e: e.tensor_scalar(out[0], in0[0], x(s1), None, op0), [out], [in0, s1])
+        else:
+            op("v", lambda e: e.tensor_scalar(out[0], in0[0], x(s1), x(s2), op0, op1), [out], [in0, s1, s2])
+
+    def tt(out, in0, in1, o):
+        op("v", lambda e: e.tensor_tensor(out[0], in0[0], in1[0], o), [out], [in0, in1])
+
+    def cp(out, in_):
+        op("v", lambda e: e.tensor_copy(out[0], in_[0]), [out], [in_])
+
+    def fill(out, c):
+        op("v", lambda e: e.memset(out[0], c), [out], [])
+
+    def scan(out, d0, d1, init, o0, o1):
+        op("v", lambda e: e.tensor_tensor_scan(out[0], d0[0], d1[0], init, o0, o1), [out], [d0, d1])
+
+    def act(out, in_, scale=1.0, func=COPY, bias=None, acc=None):
+        if acc is not None:
+            op("s", lambda e: e.activation(out[0], in_[0], func, bias=x(bias), scale=scale, accum_out=acc[0]), [out, acc], [in_, bias])
+        elif bias is not None:
+            op("s", lambda e: e.activation(out[0], in_[0], func, bias=bias, scale=scale), [out], [in_])
+        elif scale == 1.0:
+            op("s", lambda e: e.activation(out[0], in_[0], func), [out], [in_])
+        else:
+            op("s", lambda e: e.activation(out[0], in_[0], func, scale=scale), [out], [in_])
+
+    def const(name, lo, hi, step, c):
+        act(b(name, lo, hi, step), b("ones", 0, len(range(lo, hi, step))), float(c))
+
+    def quant(q, lo, hi, in_):
+        qo, so = b(q, lo, hi), b("s" + q, lo, hi)
+        op("v", lambda e: e.quantize_mx(qo[0], so[0], in_[0]), [qo, so], [in_])
+
+    def mm(out, a, alo, m, mlo, mhi):
+        v = [b(a, alo, alo + 128), b("s" + a, alo, alo + 128), b(m, mlo, mhi), b("s" + m, mlo, mhi)]
+        op("t", lambda e: e.matmul_mx(out[0], v[0][0], v[1][0], v[2][0], v[3][0], True, True), [out], v)
+
+    def iota(out, pattern, base, cm, small=True):
+        if small:
+            op("g", lambda e: e.iota(out[0], pattern, base, cm, allow_small_or_imprecise_dtypes=True), [out], [])
+        else:
+            op("g", lambda e: e.iota(out[0], pattern, base, cm), [out], [])
+
+    def load(q, out, src, codes=False):
+        ap = out[0].bitcast(dt.uint8) if codes else out[0]
+        op(q, lambda e: e.dma_start(ap, src), [out], [], "d")
+
+    def store(q, dst, in_, ap=None):
+        ap = in_[0] if ap is None else ap
+        op(q, lambda e: e.dma_start(dst, ap), [], [in_], "d")
+
+    def send(k):
+        lo, at, arr = 128 * k + 32 * (k % 2), 32 * (5 - k), T.sem["arr%d" % k]
+        qo, so, ql, sl = b("qy", lo, lo + 32), b("sqy", lo, lo + 32), b("ld", at, at + 32), b("sld", at, at + 32)
+        op("g", lambda e: e.remote_dma(ql[0].bitcast(dt.uint8), qo[0].bitcast(dt.uint8), arr, T.sem["loc"], pid, rid, mask), [ql], [qo], "r%d" % k)
+        op("g", lambda e: e.remote_dma(sl[0], so[0], arr, T.sem["loc"], pid, rid, mask), [sl], [so], "r%d" % k)
+        return at
+
+    load("y", b("ndin"), T.nd[:, :])
+    load("s", b("xin", 896, 1792), T.x[:, 896:1792])
+    load("y", b("xin", 0, 896), T.x[:, 0:896])
+    load("y", b("ut"), T.u[:, :])
+    load("y", b("arin"), T.ar[:, :])
+    load("y", b("sqw"), T.ws[:, :])
+    load("y", b("qw"), T.wc[:, :], True)
+    load("y", b("vt"), T.v[:, :])
+
+    iota(b("lane0"), [[0, 1]], 0, 1, False)
+    iota(b("ie"), [[0, 16], [1, 16]], 0, 0)
+    fill(b("ones"), 1.0)
+    scan(b("iw"), b("ones", 0, 448), b("ones", 0, 448), -1.0, A.mult, A.add)
+    e0, o0 = b("eb"), b("ones")
+    op("g", lambda e: e.affine_select(e0[0], o0[0], [[-1, 516]], A.is_equal, 0.0, 3, 4), [e0], [o0])
+    iota(b("hrow"), [[0, 7], [16, 2]], 0, 0)
+    iota(b("kc"), [[0, 2], [-2048, 16]], 14 * 2048, 0)
+    ts(b("lane"), b("lane0"), 15, A.bitwise_and)
+    lane, l14, l14c, dead, ncol, l4 = [b("sc", k, k + 1) for k in range(6)]
+    cp(lane, b("lane"))
+    ts(l14, b("lane"), 14.0, A.mult)
+    ts(l14c, b("lane"), 13.0, A.min, 14.0, A.mult)
+    ts(dead, b("lane"), 14.0, A.is_ge, 480.0, A.mult)
+    ts(ncol, b("lane"), 672.0, A.add)
+    ts(l4, b("lane"), 449.0, A.add, 4.0, A.mult)
+    ts(b("mask"), b("ie", 0, 224), lane, A.not_equal, OUT, A.mult)
+    ts(b("cap"), b("ie", 0, 224), 0.0, A.is_equal, -BIG, A.mult)
+    ts(b("lrep"), b("iw", 0, 14), l14, A.add)
+    cp(b("lu"), b("iw", 0, 128, 16))
+    ts(b("ka", 0, 7), b("iw", 1, 8), lane, A.add)
+    ts(b("kd", 0, 7), b("ka", 0, 7), 14.0, A.is_ge, -14.0, A.mult)
+    tt(b("kk", 0, 7), b("ka", 0, 7), b("kd", 0, 7), A.add)
+    for h in range(2):
+        ts(b("lc", h, 14, 2), b("kk", 0, 7), l14c, A.add, 196.0 * h, A.add)
+        ts(b("lk", h, 14, 2), b("kk", 0, 7), 16.0 * h, A.add)
+        ts(b("lk16", h, 14, 2), b("kk", 0, 7), 16.0 * h, A.add, 16.0, A.mult)
+    ts(b("li"), b("hrow"), lane, A.add)
+    ts(b("li16"), b("hrow"), lane, A.add, 16.0, A.mult)
+    ts(b("fa"), b("iw", 0, 14), -1.0, A.mult, lane, A.add)
+    ts(b("fb"), b("fa"), 0.0, A.is_lt, 14.0, A.mult)
+    tt(b("fc"), b("fa"), b("fb"), A.add)
+    ts(b("fd"), b("fc"), 7.0, A.is_gt, 1000.0, A.mult)
+    ts(b("fe"), b("fc"), 32.0, A.mult)
+    ts(b("ff"), b("fc"), -32.0, A.mult, ncol, A.add)
+    tt(b("fg"), b("fd"), b("iw", 0, 14), A.add)
+    tt(b("fh"), b("fg"), b("fe"), A.add)
+    tt(b("fi"), b("fh"), b("ff"), A.min)
+    ts(b("lf", 0, 14), b("fi"), dead, A.max, 495.0, A.min)
+    ts(b("lf", 14, 28), b("lf", 0, 14), 16.0, A.add)
+    ts(b("oe"), b("iw", 0, 400, 16), lane, A.add)
+    ts(b("o1"), b("oe"), -6.5, A.add, 1.0 / 14.0, A.mult)
+    ts(b("o2"), b("o1"), 2.0, A.mult)
+    tt(b("o3"), b("o2"), b("oe"), A.add)
+    cp(b("loa", 0, 25), b("o3"))
+    const("yt", 0, 512, 1, 0.0)
+    const("cw", 0, 32, 1, (16 + MARK) * UNIT)
+    const("cw", 480, 512, 1, 16 * UNIT)
+    const("tab", 448, 464, 1, 16 * UNIT)
+    const("rf", 0, 16, 1, 0.0)
+    const("rf", 514, 528, 1, 0.0)
+    const("rf", 1042, 1056, 1, 0.0)
+    const("s2", 0, 32, 1, NONE)
+    const("key", 0, 144, 1, 0.0)
+    const("capz", 0, 64, 1, BIG)
+    const("capz", 0, 64, 16, FLOOR)
+    const("capb", 0, 32, 1, BIG)
+    const("capb", 0, 32, 16, -BIG)
+    const("nd4", 0, 40, 1, 0.0)
+    for e in ("ea", "ec"):
+        const(e, 2, 384, 3, -BIG)
+        const(e, 385, 768, 3, -BIG)
+        const(e, 386, 768, 3, 0.0)
+    for e in ("ja", "jb"):
+        const(e, 0, 672, 3, 0.0)
+    for t in range(ROUNDS):
+        const("ft%d" % t, 1792, XW, 1, 0.0)
+    if not OPT["acc"]:
+        act(b("rst"), b("ie", 0, 32), 1.0, SIGN)
+        const("lt", 0, 64, 1, 0.0)
+
+    quant("qu", 0, 128, b("ut"))
+    qr, qu, lu, sr, su = b("qr"), b("qu"), b("lu"), b("sqr"), b("squ")
+    op("v", lambda e: e.tensor_copy(qr[0].bitcast(dt.uint32), qu[0].bitcast(dt.uint32).indirect(lu[0])), [qr], [qu, lu])
+    act(sr, by(su, lu))
+    for k in range(4):
+        quant("qe", 128 * k, 128 * k + 128, b("eb", 3 - k, 515 - k))
+    quant("ld", 192, 320, b("yt"))
+    quant("qv", 0, 128, b("vt"))
+
+    cp(b("ndn"), b("ndin"))
+    cp(b("r1", 0, 224), by(b("iw"), b("ndn", 0, 14)))
+    act(b("r1", 224, 448), by(b("iw"), b("ndn", 14, 28)))
+    for h in range(2):
+        lo, hi = 224 * h, 224 * h + 224
+        tt(b("r2", lo, hi), by(b("r1", lo, hi), b("lrep")), b("mask"), A.add)
+        scan(b("r3", lo, hi), b("cap"), b("r2", lo, hi), 0.0, A.add, A.max)
+        cp(b("nd16", 14 * h, 14 * h + 14), b("r3", lo + 15, hi, 16))
+        ts(b("nd4", 16 * h, 16 * h + 14), b("r3", lo + 15, hi, 16), 4.0, A.mult)
+    ts(b("nd4", 14, 32, 16), b("iw", 0, 65, 64), l4, A.add)
+    tt(b("kb"), b("nd4", 0, 32), b("kc"), A.add)
+    tt(b("dn"), b("nd4", 0, 32), b("nd4", 1, 33), A.subtract)
+    for h in range(2):
+        o = 256 * h + 224
+        ts(b("dif", o, o + 16), b("dn", 16 * h, 16 * h + 16), RND64, A.add, RND64, A.subtract)
+        tt(b("dif", o + 16, o + 32), b("dn", 16 * h, 16 * h + 16), b("dif", o, o + 16), A.subtract)
+    ts(b("ia", 2, 672, 3), by(b("arin"), b("lc")), LIFT, A.add)
+
+    def table():
+        act(b("cw", 32, 256), b("ia", 2, 672, 3), UNIT, IDENT, (16 - LIFT) * UNIT)
+        act(b("cw", 256, 480), b("ia", 2, 672, 3), -UNIT, IDENT, (16 + LIFT) * UNIT)
+        act(b("tab", 0, 448), by(b("cw"), b("lf")))
+
+    def differences():
+        for h in range(2):
+            scan(b("dif", 256 * h, 256 * h + 224), b("tab", 224 * h, 224 * h + 224), b("tab", 224 * h + 1, 224 * h + 225), 0.0, A.max, A.subtract)
+
+    def quantise_state(r, src):
+        for k in range(3):
+            quant("qx%d" % r, CUTS[k], CUTS[k + 1], b(src, 4 * CUTS[k], 4 * CUTS[k + 1]))
+
+    def evacuate(dst):
+        for k in range(3):
+            lo, hi = CUTS[k], CUTS[k + 1]
+            (act if OPT["pcopy"][k] == "s" else cp)(b(dst, lo, hi), bank(k, hi - lo))
+
+    def rows(k):
+        return b("rf", 528 * k + 16, 528 * k + 528, 16)
+
+    def column(k, h, pm, most):
+        if OPT["acc"]:
+            c = b("cnt", 2 * k + h, 2 * k + h + 1)
+            act(b("jk", 32 * k + 16 * h, 32 * k + 16 * h + 14 + k), pm, -1.0, SIGN, most, c)
+        else:
+            o = 32 * k + 16 * h
+            c = b("cnb", 16 * h + 14, 16 * h + 15)
+            ts(b("lt", o, o + 14 + k), pm, most, A.is_lt)
+            scan(b("cnb", 16 * h, 16 * h + 15), b("ones", 0, 15), b("lt", o, o + 15), 0.0, A.mult, A.add)
+        ts(b("ge", 256 * h, 256 * h + 256), b("ie"), c, A.is_gt)
+        o = 528 * k + 256 * h + 2
+        scan(b("rf", o, o + 256), b("ge", 256 * h, 256 * h + 256), b("dif", 256 * h, 256 * h + 256), 0.0, A.mult, A.add)
+
+    def half(r, k, ft):
+        e, o = ("ea", "ec")[k], 72 * k
+        for h in range(2):
+            p = 528 * k + 256 * h + 240
+            ts(b("ox", 8 * k + h, 8 * k + 8, 2), b("iw", 0, 4), b("rf", p, p + 1), A.add, b("rf", p + 16, p + 17), A.add)
+        for t in range(4):
+            act(b(e, 3 * t + 1, 384, 12), by(b(ft), b("ox", 8 * k + 2 * t, 8 * k + 2 * t + 2)), -2.0)
+        tt(b("key", o + 1, o + 33), b("kb"), rows(k), A.add)
+        tt(b("key", o + 33, o + 65), b("kb"), rows(k), A.subtract)
+        p = 128 * k
+        scan(b("top", p, p + 64), b("key", o, o + 64), b("capz"), BIG, A.max, A.min)
+        scan(b("top", p + 64, p + 128), b("key", o + 1, o + 65), b("top", p, p + 64), FLOOR, A.max, A.min)
+        cp(b("oi", 8 * k, 8 * k + 8), b("top", p + 15, p + 128, 16))
+        ts(b("oim", 8 * k, 8 * k + 8), b("oi", 8 * k, 8 * k + 8), 2047, A.bitwise_and)
+        for t in range(4):
+            w = 32 * k + 8 * t
+            ts(b("off", w, w + 8), b("oim", 8 * k, 8 * k + 8), float(t), A.add)
+        for t in range(4):
+            w = 32 * k + 8 * t
+            act(b("ag", 64 * t, 64 * t + 64), by(b(ft), b("off", w, w + 4)))
+            tt(b(e, 3 * t, 768, 12), by(b(ft), b("off", w + 4, w + 8)), b("ag", 64 * t, 64 * t + 64), A.add)
+        o = 384 * k
+        scan(b("eo", o, o + 384), b(e, 0, 384), b(e, 384, 768), 0.0, A.add, A.max)
+        ts(b("yt", p, p + 128), b("eo", o + 1, o + 384, 3), 0.5, A.mult)
+        quant("qy", 128 * (2 * r + k), 128 * (2 * r + k) + 128, b("yt"))
+        at = send(2 * r + k)
+        act(b("y32", p, p + 128), b("eo", o + 1, o + 384, 3), 16.0)
+        return at
+
+    def mutate(k):
+        i, j, out, o = ("ia", "ib")[k], ("ja", "jb")[k], ("ib", "so")[k], 32 * k
+        win = b("rf", 528 * k + 16, 528 * k + 528)
+        ts(b("tm", o, o + 32), rows(k), MARK * UNIT, A.is_equal, -2.0 - MARK, A.mult)
+        ts(b("rl", o, o + 32), rows(k), 0.0, A.max, 1.0 / UNIT, A.mult)
+        ts(b("gt", o, o + 32), rows(k), 0.0, A.is_gt, -MARK, A.mult)
+        tt(b("pv", o, o + 32), b("rl", o, o + 32), b("tm", o, o + 32), A.add)
+        tt(b("gv", o, o + 32), b("gt", o, o + 32), b("tm", o, o + 32), A.subtract)
+        act(b(j, 2, 672, 3), by(win, b("lk16")), -1.0 / UNIT)
+        act(b(j, 1, 672, 3), by(b("gv", o, o + 32), b("lk")))
+        act(b(i, 0, 672, 3), by(win, b("li16")), 1.0 / (MARK * UNIT))
+        act(b(i, 1, 672, 3), by(b("pv", o, o + 32), b("li")))
+        scan(b(out), b(j), b(i), 0.0, A.mult, A.add)
+
+    def renew(k, at, ft):
+        p = 128 * k
+        for t in range(4):
+            mm(bank(4 * k + t, 128), "qw", 128 * t, "ld", at, at + 128)
+        for t in range(4):
+            tt(b("wb", p + 32 * t, p + 32 * t + 32), bank(4 * k + t, 32), b("y32", p + t, p + 128, 4), A.add)
+        pieces = OPT["scat"] if k else 1
+        w = 128 // pieces
+        for s in range(pieces):
+            lo = p + w * s
+            ts(b("vv", lo, lo + w), b("wb", lo, lo + w), 0.03125, A.mult)
+            cp(by(b(ft), b("ox", lo // 16, (lo + w) // 16)), b("vv", lo, lo + w))
+
+    table()
+    for r in range(ROUNDS):
+        ft, qx = "ft%d" % r, "qx%d" % r
+        quantise_state(r, "ft%d" % (r - 1) if r else "xin")
+        for k in range(3):
+            mm(bank(k, CUTS[k + 1] - CUTS[k]), "qr", 0, qx, CUTS[k], CUTS[k + 1])
+        evacuate("ps")
+        for k in range(4):
+            mm(bank(4 + k, 448), "qe", 128 * k, qx, 0, 448)
+        for k in range(4):
+            act(b(ft, k, 1792, 4), bank(4 + k, 448))
+        differences()
+        for h in range(2):
+            lo, hi = 224 * h, 224 * h + 224
+            tt(b("smk", lo, hi), by(b("ps"), b("nd16", 14 * h, 14 * h + 14)), b("mask"), A.add)
+            scan(b("pmf", lo, hi), b("smk", lo, hi), b("smk", lo, hi), -BIG, A.max, A.max)
+            scan(b("scn", lo, hi), b("cap"), b("smk", lo, hi), 0.0, A.add, A.max)
+            column(0, h, b("pmf", lo + 15, hi, 16), b("pmf", hi - 1, hi))
+        if OPT["join"]:
+            ts(b("pen"), rows(0), 0.0, A.not_equal, OUT, A.mult)
+        for h in range(2):
+            o = 16 * h
+            if not OPT["join"]:
+                ts(b("pen", o, o + 14), b("rf", 16 + 256 * h, 240 + 256 * h, 16), 0.0, A.not_equal, OUT, A.mult)
+            tt(b("s2", o, o + 14), b("scn", 224 * h + 15, 224 * h + 224, 16), b("pen", o, o + 14), A.add)
+            if not OPT["join"]:
+                scan(b("pm1", o, o + 15), b("s2", o, o + 15), b("s2", o, o + 15), -BIG, A.max, A.max)
+        if OPT["join"]:
+            scan(b("pm1"), b("capb"), b("s2"), 0.0, A.min, A.max)
+        for h in range(2):
+            column(1, h, b("pm1", 16 * h, 16 * h + 15), b("pm1", 16 * h + 14, 16 * h + 15))
+        at0 = half(r, 0, ft)
+        mutate(0)
+        at1 = half(r, 1, ft)
+        mutate(1)
+        ts(b("ia", 2, 672, 3), b("so", 2, 672, 3), LIFT + 3, A.min, LIFT - 3, A.max)
+        if r == ROUNDS - 1:
+            const("cw", 0, 32, 1, 16 * UNIT)
+        table()
+        renew(0, at0, ft)
+        renew(1, at1, ft)
+    act(b("oa1"), by(b("tab"), b("loa", 0, 25)), 1.0 / UNIT, IDENT, -16.0)
+    store("y", T.oa[:, :], b("oa1", 0, 392))
+    quantise_state(3, ft)
+    for k in range(3):
+        mm(bank(k, CUTS[k + 1] - CUTS[k]), "qv", 0, "qx3", CUTS[k], CUTS[k + 1])
+    evacuate("yo")
+    store("y", T.oc[:, 0:1280], b("qx3", 0, 320), T.qx3[:, 0:320].bitcast(dt.uint8))
+    store("y", T.oc[:, 1280:1792], b("qx3", 320, 448), T.qx3[:, 320:448].bitcast(dt.uint8))
+    for k in range(4):
+        store("sy"[k % 2], T.osc[4 * k:4 * k + 4, 0:448], b("sqx3"), T.sqx3[32 * k:32 * k + 4, 0:448])
+    store("s", T.y[:, 0:320], b("yo", 0, 320))
+    store("y", T.y[:, 320:448], b("yo", 320, 448))
+    return L
+
+
+def needs(L):
+    seen, E = {}, []
+    for i, (q, f, R, W, kind) in enumerate(L):
+        d = {}
+        for name, bits, w in [(a, c, False) for a, c in R] + [(a, c, True) for a, c in W]:
+            psum = SCRATCH[name][0] == "psum"
+            for j, jbits, jw in seen.setdefault(name, []):
+                if j == i or not bits & jbits:
+                    continue
+                same = L[j][0] == q and L[j][4] == "c" and kind == "c"
+                if jw or (w and not same) or (psum and not same):
+                    d[j] = True
+                elif w:
+                    d.setdefault(j, False)
+            if w:
+                seen[name] = [s for s in seen[name] if s[1] & ~bits or s[0] == i]
+            seen[name].append((i, bits, w))
+        E.append(d)
+    return E
 
 
 def rank_program(g, core, T, topo):
     rank = T.rank_of(core)
     if rank is None:
         return
-    A = AluOpType
-    COPY, SIGN, IDENT = ActivationFunctionType.Copy, ActivationFunctionType.Sign, ActivationFunctionType.Identity
     n = len(T.cores)
     nxt, prv = T.cores[(rank + 1) % n], T.cores[(rank - 1) % n]
-
+    L = calls(core, T, topo)
+    E = needs(L)
+    order = ORDER if ORDER else list(range(len(L)))
     queue = {"v": g.vector, "s": g.scalar, "t": g.tensor, "g": g, "y": g.sync}
-    semof = {"v": "cv", "s": "cs", "t": "ct", "g": "cg"}
-    count = {"cv": 0, "cs": 0, "ct": 0, "cg": 0}
-    state, seen, ndma = {}, {}, [0]
-
-    def entry(t):
-        return state.setdefault(t, [[], [], [], True])
+    count, done, seen, ndma, sent = {"v": 0, "s": 0, "t": 0, "g": 0}, {}, {}, 0, 0
 
     def need(q, sem, val):
         if seen.get((q, sem), 0) < val:
             queue[q].wait_ge(T.sem[sem], val)
             seen[(q, sem)] = val
 
-    def order(q, R, W, dma):
-        want = []
-        for t in R:
-            want += entry(t)[0]
-        for t in W:
-            s = entry(t.lstrip("+"))
-            if t[0] != "+" or s[1] or s[3]:
-                s[2] = s[0] + [e for e in s[1] if dma or e[2] != q]
-                s[0], s[1], s[3] = [], [], t[0] != "+"
-            want += s[2]
+    for i in order:
+        q, f, R, W, kind = L[i]
         most = {}
-        for sem, val, w in want:
-            most[sem] = max(most.get(sem, 0), val)
+        for j in E[i]:
+            sem, val = done[j]
+            if E[i][j]:
+                most[sem] = max(most.get(sem, 0), val)
         for sem in most:
             need(q, sem, most[sem])
-
-    def note(R, W, e):
-        for t in R:
-            entry(t)[1].append(e)
-        for t in W:
-            entry(t.lstrip("+"))[0].append(e)
-
-    def op(q, R, W, f):
-        R, W = R.split(), W.split()
-        order(q, R, W, False)
-        s = semof[q]
-        count[s] += 1
-        f(queue[q]).then_inc(T.sem[s], 1)
-        note(R, W, (s, count[s], q))
-
-    def dma(q, R, W, out, in_):
-        R, W = R.split(), W.split()
-        order(q, R, W, True)
-        s = "dma%d" % ndma[0]
-        ndma[0] += 1
-        queue[q].dma_start(out, in_).then_inc(T.sem[s], 16)
-        note(R, W, (s, 16, "dma"))
-
-    def b(name, lo=0, hi=None, step=1):
-        buf, at, cols = SMALL[name] if name in SMALL else (name, 0, SCRATCH[name][1][1])
-        hi = cols if hi is None else hi
-        return T[buf][:, at + lo:at + hi:step] if step > 1 else T[buf][:, at + lo:at + hi]
-
-    def ts(R, W, out, in0, s1, op0, s2=None, op1=None):
-        if op1 is None:
-            op("v", R, W, lambda e: e.tensor_scalar(out, in0, s1, None, op0))
+        call = f(queue[q])
+        if kind == "c":
+            count[q] += 1
+            call.then_inc(T.sem["c" + q], 1)
+            done[i] = ("c" + q, count[q])
+        elif kind == "d":
+            call.then_inc(T.sem["dma%d" % ndma], 16)
+            done[i] = ("dma%d" % ndma, 16)
+            ndma += 1
         else:
-            op("v", R, W, lambda e: e.tensor_scalar(out, in0, s1, s2, op0, op1))
-
-    def tt(R, W, out, in0, in1, o):
-        op("v", R, W, lambda e: e.tensor_tensor(out, in0, in1, o))
-
-    def cp(R, W, out, in_):
-        op("v", R, W, lambda e: e.tensor_copy(out, in_))
-
-    def fill(W, out, c):
-        op("v", "", W, lambda e: e.memset(out, c))
-
-    def scan(R, W, out, d0, d1, init, o0, o1):
-        op("v", R, W, lambda e: e.tensor_tensor_scan(out, d0, d1, init, o0, o1))
-
-    def act(R, W, out, in_, scale=1.0, func=COPY):
-        if scale == 1.0:
-            op("s", R, W, lambda e: e.activation(out, in_, func))
-        else:
-            op("s", R, W, lambda e: e.activation(out, in_, func, scale=scale))
-
-    def const(W, out, c, cols):
-        op("s", "ie", W, lambda e: e.activation(out, b("ie", 0, cols), IDENT, bias=c, scale=0.0))
-
-    def quant(R, W, q, s, in_):
-        op("v", R, W, lambda e: e.quantize_mx(q, s, in_))
-
-    def mm(R, W, out, a, sa, m, sm):
-        op("t", R, W, lambda e: e.matmul_mx(out, a, sa, m, sm, True, True))
-
-    def iota(W, out, pattern, base, cm, small=False):
-        if small:
-            op("g", "", W, lambda e: e.iota(out, pattern, base, cm, allow_small_or_imprecise_dtypes=True))
-        else:
-            op("g", "", W, lambda e: e.iota(out, pattern, base, cm))
-
-    dma("y", "", "ndin", b("ndin"), T.nd[:, :])
-    dma("s", "", "xb", b("xin", 896, 1792), T.x[:, 896:1792])
-    dma("y", "", "ut", b("ut"), T.u[:, :])
-    dma("y", "", "xa", b("xin", 0, 896), T.x[:, 0:896])
-    dma("y", "", "arin", b("arin"), T.ar[:, :])
-    dma("y", "", "sw", b("sqw"), T.ws[:, :])
-    dma("y", "", "qw", T.qw[:, :].bitcast(dt.uint8), T.wc[:, :])
-    dma("y", "", "vt", b("vt"), T.v[:, :])
-
-    iota("lane0", b("lane0"), [[0, 56]], 0, 1)
-    iota("fi0", b("fi0"), [[0, 28], [8, 2]], 0, 0)
-    iota("fj", b("fj"), [[0, 2], [1, 14], [0, 2]], 0, 0)
-    iota("t28a", b("t28a"), [[224, 2], [1, 14]], 0, 0)
-    iota("d14", b("d14"), [[0, 2], [1, 7]], 1, 0)
-    iota("fh", b("fh"), [[112, 2], [0, 28]], 0, 0)
-    iota("t8", b("t8"), [[16, 8]], 0, 0)
-    iota("iw", b("iw"), [[1, 448]], 0, 0, True)
-    iota("ie", b("ie"), [[0, 33], [1, 16]], 0, 0, True)
-    iota("h14", b("h14"), [[14, 2], [0, 7]], 0, 0)
-    iota("h196", b("h196"), [[196, 2], [0, 7]], 0, 0)
-    iota("+fx", b("fx", 0, 4), [[32, 2], [8, 2]], 448, 0)
-    iota("+fx", b("fx", 4, 8), [[32, 2], [8, 2]], 464, 0)
-    iota("dum0", b("dum0"), [[16, 2]], 449, 0)
-
-    fill("cap16", b("cap16"), BIG)
-    ts("lane0", "lane", b("lane"), b("lane0"), 15, A.bitwise_and)
-    ts("lane", "fm", b("fm"), b("lane"), 1, A.arith_shift_right)
-    ts("lane", "fn", b("fn"), b("lane"), 1, A.bitwise_and)
-    ts("lane", "t28b", b("t28b"), b("lane", 0, 28), 14, A.mult)
-    tt("fm fn", "fo", b("fo"), b("fm"), b("fn"), A.subtract)
-    ts("lane", "t14e", b("t14e"), b("lane", 0, 14), 14, A.mult)
-    ts("fo", "fl", b("fl"), b("fo"), 1, A.add)
-    cp("lane", "lanef", b("lanef"), b("lane", 0, 1))
-    tt("fl fi0", "fi", b("fi"), b("fl"), b("fi0"), A.add)
-    fill("cap16", b("cap16", 0, 448, 16), -BIG)
-    tt("fi fj", "f1", b("f1"), b("fi"), b("fj"), A.subtract)
-    tt("t28b t28a", "t28c", b("t28c"), b("t28b"), b("t28a"), A.add)
-    ts("f1", "f2", b("f2"), b("f1"), 0, A.is_lt, 14, A.mult)
-    cp("t28c", "lrep", b("lrep"), b("t28c"))
-    tt("f1 f2", "f3", b("f3"), b("f1"), b("f2"), A.add)
-    tt("d14 lane", "t14a", b("t14a"), b("d14"), b("lane", 0, 14), A.add)
-    ts("f3", "f4", b("f4"), b("f3"), 16, A.mult, -16, A.add)
-    ts("f3", "f6", b("f6"), b("f3"), -16, A.mult, 432, A.add)
-    cp("ndin", "ndn", b("ndn"), b("ndin"))
-    act("iw ndn", "r1", b("r1"), T.iw[:, 0:448].indirect(b("ndn")))
-    const("ones", b("ones"), 1.0, 516)
-    op("g", "ones", "eb", lambda e: e.affine_select(b("eb"), b("ones"), [[-1, 516]], A.is_equal, 0.0, 3, 4))
-    iota("kc", b("kc"), [[0, 2], [-2048, 14]], 14 * 2048, 0)
-    iota("ds0", b("ds0"), [[0, 512], [-1, 2]], 0, 0, True)
-    ts("f3", "f8", b("f8"), b("f3"), 7, A.is_le)
-    tt("f4 fj", "f5", b("f5"), b("f4"), b("fj"), A.add)
-    tt("f6 fi", "f7", b("f7"), b("f6"), b("fi"), A.add)
-    ts("t14a", "t14b", b("t14b"), b("t14a"), 14, A.is_ge, -14, A.mult)
-    tt("f5 f7", "f9", b("f9"), b("f5"), b("f7"), A.subtract)
-    ts("f3", "f4", b("f4"), b("f3"), 0, A.is_equal, 512, A.mult)
-    tt("f8 f9", "fa", b("fa"), b("f8"), b("f9"), A.mult)
-    tt("t14a t14b", "t14c", b("t14c"), b("t14a"), b("t14b"), A.add)
-    tt("fa f7", "f1", b("f1"), b("fa"), b("f7"), A.add)
-    ts("fi", "f6", b("f6"), b("fi"), 14, A.is_ge, 513, A.mult)
-    tt("f1 fh", "f2", b("f2"), b("f1"), b("fh"), A.add)
-    cp("t8", "lu", b("lu"), b("t8"))
-    tt("f2 f4", "f5", b("f5"), b("f2"), b("f4"), A.max)
-    ts("ie lanef", "mask0", b("mask"), b("ie", 0, 448), b("lanef"), A.is_equal, BIG, A.mult)
-    tt("f5 f6", "+lfi", b("lfi", 4, 60), b("f5"), b("f6"), A.max)
-    quant("ut", "qu", b("qu"), b("squ"), b("ut"))
-    ts("mask0", "mask", b("mask"), b("mask"), LOW, A.add)
-    op("v", "qu lu", "qr", lambda e: e.tensor_copy(T.qr[:, 0:128].bitcast(dt.uint32), T.qu[:, 0:128].bitcast(dt.uint32).indirect(b("lu"))))
-    act("qu lu", "sr", b("sqr"), T.squ[:, 0:128].indirect(b("lu")))
-    tt("r1 lrep mask", "r2", b("r2"), T.r1[:, 0:448].indirect(b("lrep")), b("mask"), A.min)
-    tt("t14e h196", "t14f", b("t14f"), b("t14e"), b("h196"), A.add)
-    scan("cap16 r2", "r3", b("r3"), b("cap16"), b("r2"), 0.0, A.min, A.max)
-    const("yt", b("yt"), 0.0, 512)
-    const("capf", b("capf"), BIG, 448)
-    const("capz", b("capz"), BIG, 112)
-    const("av0 av1 av2", b("av"), 0.0, 160)
-    for h in range(2):
-        act("ie", "+rst14", b("rst14", 14 * h, 14 * h + 14), b("ie", 0, 14), 1.0, SIGN)
-    for t in range(ROUNDS):
-        const("fz%d" % t, b("ft%d" % t, 1792, XW), 0.0, XW - 1792)
-
-    def bank(k, cols):
-        return (T.pp[:, 0:cols], T.pp[:, 512:512 + cols], T.pq[:, 0:cols])[k]
-
-    def quantise_state(r, src, ta, tb):
-        qx, sx = T["qx%d" % r], T["sqx%d" % r]
-        for k in range(3):
-            lo, hi = CUTS[k], CUTS[k + 1]
-            quant((ta, ta + " " + tb, tb)[k], "q%d%d" % (k, r), qx[:, lo:hi], sx[:, lo:hi], src[:, 4 * lo:4 * hi])
-        return qx, sx
-
-    def begin(r, src, ta, tb):
-        qx, sx = quantise_state(r, src, ta, tb)
-        if r == 0:
-            cp("r3", "nd16", b("nd16"), b("r3", 15, 448, 16))
-            for k in range(4):
-                quant("eb", "+qe", T.qe[:, 128 * k:128 * k + 128], T.sqe[:, 128 * k:128 * k + 128], T.eb[:, 3 - k:515 - k])
-        for k in range(3):
-            lo, hi = CUTS[k], CUTS[k + 1]
-            mm("qr sr q%d%d" % (k, r), ("pp0", "pp1", "pq0")[k], bank(k, hi - lo), b("qr"), b("sqr"), qx[:, lo:hi], sx[:, lo:hi])
-        for k in range(4):
-            mm("qe q0%d q1%d q2%d" % (r, r, r), "pd%d" % k, T.pd[:, 512 * k:512 * k + 448], T.qe[:, 128 * k:128 * k + 128],
-               T.sqe[:, 128 * k:128 * k + 128], qx[:, 0:448], sx[:, 0:448])
-        act("pp0", "ps0", b("ps", 0, 160), bank(0, 160))
-        act("pp1", "ps1", b("ps", 160, 320), bank(1, 160))
-
-    def decode(r):
-        ft = "ft%d" % r
-        for k in range(4):
-            act("pd%d" % k, "+" + ft, b(ft, k, 1792, 4), T.pd[:, 512 * k:512 * k + 448])
-
-    def stored():
-        act("cst", "cw0", b("cw", 0, 224), b("st", 0, 1344, 6))
-        act("cst", "cw1", b("cw", 224, 448), b("st", 0, 1344, 6), -1.0)
-
-    def lay_out():
-        act("cw0 cw1 cwk cwn lf", "ds1", b("ds1"), T.cw[:, 0:528].indirect(b("lf")))
-
-    begin(0, T.xin, "xa", "xb")
-    quant("yt", "ldz", b("ld", 128, 256), b("sld", 128, 256), b("yt"))
-    mask = topo.mask(core, prv)
-    rid, pid = topo.addr(prv)[:2]
-    order("g", ["ldz"], [], False)
-    g.remote_sem_update(T.sem["ready"], T.sem["loc"], pid, rid, mask)
-    nloc = [len(topo.engines(core, prv))]
-    iota("yd", b("yd"), [[0, 256], [1, 2]], 0, 0, True)
-    for s, c in ((0, 0), (3, 1), (4, -1), (5, 1)):
-        iota("+sgc", b("sg", s, 1344, 6), [[0, 224]], c, 0, True)
-    iota("st1", b("st", 1, 1344, 6), [[0, 224]], 0, 0, True)
-    iota("oe0", b("oe0"), [[16, 25]], 0, 0)
-    fill("ndw", b("ndw"), 0)
-    tt("t14f t14c", "t14g", b("t14a"), b("t14f"), b("t14c"), A.add)
-    tt("dum0 lane", "dum", b("dum"), b("dum0"), b("lane", 0, 2), A.add)
-    for h in range(2):
-        cp("r3", "+ndw", b("ndw", 16 * h, 16 * h + 14), b("r3", 224 * h + 15, 224 * h + 224, 16))
-    ts("t14g", "t14h", b("t14f"), b("t14a"), 391, A.min)
-    cp("dum", "+ndw", b("ndw", 14, 32, 16), b("dum"))
-    tt("fx fl", "+lfi", b("lfi", 0, 4), b("fx", 0, 4), b("fl", 0, 4), A.add)
-    cp("t14h", "lc", b("lc"), b("t14f"))
-    ts("ndw", "ndh", b("ndh"), b("ndw"), 4, A.arith_shift_right)
-    ts("ndw", "ndl", b("ndl"), b("ndw"), 15, A.bitwise_and)
-    tt("fx fl", "+lfi", b("lfi", 60, 64), b("fx", 4, 8), b("fl", 0, 4), A.add)
-    ts("arin lc", "cst", b("st", 0, 1344, 6), T.arin[:, 0:392].indirect(b("lc")), UNIT, A.mult)
-    stored()
-    fill("cwk", b("cw", 512, 528), 0.0)
-    ts("ndh", "+cwn", b("cw", 448, 480), b("ndh"), 64, A.mult)
-    ts("ndl", "+cwn", b("cw", 480, 512), b("ndl"), 4, A.mult)
-    fill("cwk", b("cw", 512, 513), MARK)
-    cp("lfi", "lf", b("lf"), b("lfi"))
-    fill("capf", b("capf", 0, 448, 224), -BIG)
-    lay_out()
-    decode(0)
-
-    def rows(k):
-        return b("rf", 512 * k + 46, 512 * k + 46 + 28 * 16 - 15, 16)
-
-    def column(k):
-        ts("rf%d" % k, "+av0", b("av", 64 + 32 * k, 92 + 32 * k), rows(k), RND16, A.add, RND16, A.subtract)
-
-    def turned(k, h):
-        o = 28 * k + 14 * h
-        ts("ie cnt%d" % k, "+eq", b("eq", o, o + 14), b("ie", 0, 14), b("cnt", o + 13, o + 14), A.is_equal)
-
-    def slot(t):
-        ts("ow", "+ox", b("ox", 4 * t, 4 * t + 4), b("ow"), t, A.add)
-
-    def choose(k, tok, pm, beside):
-        o = 28 * k
-        for h in range(2):
-            ts(tok, "+lt%d" % k, b("ltb", o + 14 * h, o + 14 * h + 14), pm(h)[0], pm(h)[1], A.is_lt)
-        beside[0]()
-        scan("rst14 lt%d" % k, "cnt%d" % k, b("cnt", o, o + 28), b("rst14"), b("ltb", o, o + 28), 0.0, A.mult, A.add)
-        beside[1]()
-        for h in range(2):
-            ts("ie cnt%d" % k, "+ge", b("ge", 256 * h, 256 * h + 256), b("ie", 256 * h, 256 * h + 256), b("cnt", o + 14 * h + 13, o + 14 * h + 14), A.is_gt)
-        beside[2]()
-        scan("ge ds2", "rf%d" % k, b("rf", 512 * k, 512 * k + 512), b("ge"), b("ds2", 1, 1024, 2), 0.0, A.mult, A.add)
-
-    def differences():
-        scan("ds0 ds1", "ds2", b("ds2"), b("ds0"), b("ds1"), 0.0, A.mult, A.add)
-
-    def scores():
-        scan("cap16 smk", "scn", b("scn"), b("cap16"), b("smk"), 0.0, A.min, A.max)
-
-    def nothing():
-        return None
-
-    def late_constants():
-        ts("r3", "nd4", b("nd4"), b("r3", 15, 448, 16), 4.0, A.mult)
-        tt("h14 lane", "t14b", b("t14b"), b("h14"), b("lane", 0, 14), A.add)
-        tt("t14c h14", "t14d", b("t14d"), b("t14c"), b("h14"), A.add)
-        fill("capb", b("capb"), BIG)
-        tt("nd4 kc", "kb", b("kb"), b("nd4"), b("kc"), A.add)
-        fill("s2z", b("s2"), LOW)
-        cp("t14b", "li", b("li"), b("t14b"))
-        cp("t14d", "lk", b("lk"), b("t14d"))
-        fill("capb", b("capb", 0, 30, 15), -BIG)
-        fill("key0", b("key", 0, 1), 0.0)
-        fill("capz", b("capz", 0, 112, 14), FLOOR)
-
-    rid, pid = topo.addr(nxt)[:2]
-    mask = topo.mask(core, nxt)
-    engines = len(topo.engines(core, nxt))
-
-    for r in range(ROUNDS):
-        ft, fz = "ft%d" % r, "ft%d fz%d" % (r, r)
-        if r:
-            begin(r, T["ft%d" % (r - 1)], "ft%d" % (r - 1), "ft%d" % (r - 1))
-            decode(r)
-            differences()
-        cp("pq0", "ps2", b("ps", 320, 448), bank(2, 128))
-        tt("ps0 ps1 ps2 nd16 mask", "smk", b("smk"), T.ps[:, 0:448].indirect(b("nd16")), b("mask"), A.min)
-        if r == 0:
-            late_constants()
-        scan("capf smk", "pmf", b("pmf"), b("capf"), b("smk"), 0.0, A.min, A.max)
-        choose(0, "pmf", lambda h: (b("pmf", 224 * h + 15, 224 * h + 224, 16), b("pmf", 224 * h + 223, 224 * h + 224)),
-               [scores, differences if r == 0 else nothing, nothing])
-        ts("rf0", "pen", b("pen"), rows(0), 0.0, A.not_equal, -BIG, A.mult)
-        turned(0, 0)
-        for h in range(2):
-            tt("scn pen s2z", "+s2", b("s2", 15 * h, 15 * h + 14), b("scn", 224 * h + 15, 224 * h + 224, 16), b("pen", 14 * h, 14 * h + 14), A.add)
-        turned(0, 1)
-        scan("capb s2 s2z", "pm1", b("pm1"), b("capb"), b("s2"), 0.0, A.min, A.max)
-        tt("rf0", "+ow", b("ow", 0, 2), b("rf", 14, 495, 480), b("rf", 30, 511, 480), A.add)
-        choose(1, "pm1", lambda h: (b("pm1", 15 * h, 15 * h + 14), b("pm1", 15 * h + 14, 15 * h + 15)),
-               [lambda: tt("kb rf0", "+key", b("key", 1, 29), b("kb"), rows(0), A.add),
-                lambda: tt("kb rf0", "+key", b("key", 57, 85), b("kb"), rows(0), A.subtract), nothing])
-        column(0)
-        tt("kb rf1", "+key", b("key", 29, 57), b("kb"), rows(1), A.add)
-        tt("kb rf1", "+key", b("key", 85, 113), b("kb"), rows(1), A.subtract)
-        tt("rf1", "+ow", b("ow", 2, 4), b("rf", 526, 1007, 480), b("rf", 542, 1023, 480), A.add)
-        scan("key key0 capz", "ep", b("ep"), b("key", 0, 112), b("capz"), BIG, A.max, A.min)
-        slot(0)
-        tt("ep key", "tmn", b("tmn"), b("ep"), b("key", 1, 113), A.min)
-        tt("ep key", "+oi", b("oi", 0, 8), b("ep", 13, 112, 14), b("key", 14, 113, 14), A.max)
-        scan("capz tmn", "p2", b("p2"), b("capz"), b("tmn"), FLOOR, A.min, A.max)
-        slot(1)
-        cp("p2", "+oi", b("oi", 8, 16), b("p2", 13, 112, 14))
-        slot(2)
-        ts("oi", "oim", b("oim"), b("oi"), 2047, A.bitwise_and)
-        slot(3)
-        for t in range(4):
-            ts("oim", "off%d" % t, b("off", 16 * t, 16 * t + 16), b("oim"), t, A.add)
-        column(1)
-        turned(1, 0)
-        ts("av0", "av1", b("av", 0, 64), b("av", 64, 128), -1.0 / UNIT, A.mult, 0.0, A.max)
-        for t in range(4):
-            act(fz + " off%d" % t, "ag%d" % t, b("ag", t, 512, 4), T[ft][:, 0:XW].indirect(b("off", 16 * t, 16 * t + 8)))
-        for t in range(4):
-            act(fz + " ox", "+own", b("ys", 2 * t + 1, 512, 8), T[ft][:, 0:XW].indirect(b("ox", 4 * t, 4 * t + 4)), -2.0)
-        for t in (2, 3, 0, 1):
-            act("av%d li" % (0 if t > 1 else 1), "xg%d" % t, b("xg", 224 * t, 224 * t + 224), T.av[:, 32 * t:32 * t + 32].indirect(b("li")))
-        for t in range(4):
-            tt(fz + " off%d ag%d" % (t, t), "+su", b("su2", t, 512, 4), T[ft][:, 0:XW].indirect(b("off", 16 * t + 8, 16 * t + 16)), b("ag", t, 512, 4), A.add)
-        turned(1, 1)
-        tt("su", "mm", b("ys", 0, 512, 2), b("su2", 0, 256), b("su2", 256, 512), A.max)
-        tt("eq", "ph0", b("ph0"), b("eq", 0, 28), b("eq", 28, 56), A.add)
-        scan("yd mm own", "y2", b("ag"), b("yd"), b("ys"), 0.0, A.mult, A.add)
-        ts("ph0", "av2", b("av", 128, 156), b("ph0"), -2.0, A.mult, 1.0, A.add)
-        act("av2 li", "+sgp", b("sg", 1, 1344, 6), T.av[:, 128:160].indirect(b("li")), -1.0)
-        act("av2 lk", "+sgp", b("sg", 2, 1344, 6), T.av[:, 128:160].indirect(b("lk")))
-        ts("y2", "yt ag0 ag1 ag2 ag3", b("yt", 0, 256), b("ag", 1, 512, 2), 0.5, A.mult)
-        quant("yt", "qy%d" % r, T["qy%d" % r][:, 0:128], T["sqy%d" % r][:, 0:128], b("yt"))
-        order("g", ["qy%d" % r], [], False)
-        if r == 0:
-            g.wait_ge(T.sem["ready"], len(topo.engines(nxt, core)))
-        arr, at = "arr%d" % r, 64 * (ROUNDS - 1 - r)
-        g.remote_dma(T.ld[:, at:at + 64].bitcast(dt.uint8), T["qy%d" % r][:, 0:64].bitcast(dt.uint8), T.sem[arr], T.sem["loc"], pid, rid, mask)
-        g.remote_dma(T.sld[:, at:at + 64], T["sqy%d" % r][:, 0:64], T.sem[arr], T.sem["loc"], pid, rid, mask)
-        nloc[0] += 2 * engines
-        for t in (2, 3, 0, 1):
-            w = (64 + 32 * t) % 128
-            tt("av0 av1 lk xg%d" % t, "+pr", b("st", 2 + t, 1344, 6), T.av[:, w:w + 32].indirect(b("lk")), b("xg", 224 * t, 224 * t + 224), A.mult)
-        act("yt", "y32", b("y32"), b("yt", 0, 256), 32.0)
-        scan("sgc sgp st1 cst pr", "so", b("so"), b("sg"), b("st"), 0.0, A.mult, A.add)
-        ts("so", "cst", b("st", 0, 1344, 6), b("so", 5, 1344, 6), 3 * UNIT, A.min, -3 * UNIT, A.max)
-        if r == 0:
-            quant("vt", "qv", b("qv"), b("sqv"), b("vt"))
-        if r == ROUNDS - 1:
-            fill("cwk", b("cw", 512, 513), 0.0)
-            tt("oe0 lane", "oe", b("oe"), b("oe0"), b("lane", 0, 25), A.add)
-            ts("oe", "o1", b("o1"), b("oe"), -6.5, A.add, 1.0 / 14.0, A.mult)
-            ts("o1", "o2", b("o2"), b("o1"), RND0, A.add, RND0, A.subtract)
-            ts("o2", "o3", b("o3"), b("o2"), 2.0, A.mult, 32.5, A.add)
-            tt("o3 oe", "o4", b("o4"), b("o3"), b("oe"), A.add)
-            ts("o4", "loa", b("loa"), b("o4"), 2.0, A.mult)
-        stored()
-        lay_out()
-        if r == ROUNDS - 1:
-            act("ds1 loa", "oa1", b("oa1"), T.ds1[:, 0:1024].indirect(b("loa")), 1.0 / UNIT)
-            dma("y", "oa1", "", T.oa[:, :], b("oa1", 0, 392))
-        order("t", [], ["land%d" % r], False)
-        entry("land%d" % r)[0].append((arr, 2 * len(topo.engines(prv, core)), "remote"))
-        toks = ("pq0", "pq1", "pp0", "pp1")
-
-        def place(k, cols):
-            return T.pq[:, 512 * k:512 * k + cols] if k < 2 else T.pp[:, 512 * (k - 2):512 * (k - 2) + cols]
-
-        def sum_(k):
-            tt(toks[k] + " y32", "+wb%d" % (k // 2), b("wb", 64 * k, 64 * k + 64), place(k, 64), b("y32", k, 256, 4), A.add)
-
-        def scaled(k):
-            ts("wb%d" % k, "vv%d" % k, b("vv", 128 * k, 128 * k + 128), b("wb", 128 * k, 128 * k + 128), 0.03125, A.mult)
-
-        def scatter(k):
-            cp("vv%d ox" % k, ft, T[ft][:, 0:XW].indirect(b("ox", 8 * k, 8 * k + 8)), b("vv", 128 * k, 128 * k + 128))
-
-        for k in range(4):
-            mm("qw sw ldz land%d" % r, toks[k], place(k, 128), T.qw[:, 128 * k:128 * k + 128], T.sqw[:, 128 * k:128 * k + 128],
-               b("ld", at, at + 128), b("sld", at, at + 128))
-        sum_(0)
-        sum_(1)
-        sum_(2)
-        scaled(0)
-        sum_(3)
-        scatter(0)
-        scaled(1)
-        scatter(1)
-    qx, sx = quantise_state(3, T[ft], ft, ft)
-    for k in range(3):
-        lo, hi = CUTS[k], CUTS[k + 1]
-        mm("qv q%d3" % k, ("pp0", "pp1", "pq0")[k], bank(k, hi - lo), b("qv"), b("sqv"), qx[:, lo:hi], sx[:, lo:hi])
-    act("pp0", "yo0", b("yo", 0, 160), bank(0, 160))
-    act("pp1", "yo1", b("yo", 160, 320), bank(1, 160))
-    cp("pq0", "yo2", b("yo", 320, 448), bank(2, 128))
-    dma("y", "q03 q13", "", T.oc[:, 0:1280], qx[:, 0:320].bitcast(dt.uint8))
-    dma("s", "yo0 yo1", "", T.y[:, 0:320], b("yo", 0, 320))
-    dma("y", "yo2", "", T.y[:, 320:448], b("yo", 320, 448))
-    dma("s", "q23", "", T.oc[:, 1280:1792], qx[:, 320:448].bitcast(dt.uint8))
-    for k in range(4):
-        dma("sy"[k % 2], "q03 q13 q23", "", T.osc[4 * k:4 * k + 4, 0:448], sx[32 * k:32 * k + 4, 0:448])
-    g.wait_ge(T.sem["loc"], nloc[0])
-    for k in range(ndma[0]):
+            done[i] = ("arr" + kind[1:], 2 * len(topo.engines(prv, core)))
+            sent += len(topo.engines(core, nxt))
+    g.wait_ge(T.sem["loc"], sent)
+    for k in range(ndma):
         need("y", "dma%d" % k, 16)
-    for s in ("cv", "cs", "ct", "cg"):
-        need("y", s, count[s])
+    for q in count:
+        need("y", "c" + q, count[q])

@@ -1,34 +1,36 @@
 from concourse.mybir import dt, AluOpType, ActivationFunctionType
 
 ROUNDS, C = 3, 448
-CUTS = (0, 160, 320, 448)
+CUTS = (0, 128, 320, 448)
 XW = 1936
-UNIT = 65536.0
+UNIT = 2.0 ** 19
 MARK = 0.125
 LIFT = 192.0
-FLOOR = 65536.0 + 4 * 448
+FLOOR = UNIT + 4 * 448
 BIG = 2.0 ** 99
 OUT = -(2.0 ** 98)
 NONE = -(2.0 ** 97)
 RND64 = 1.5 * 2.0 ** 29
-OPT = {"acc": 1, "pcopy": "ssv", "scat": 2, "join": 0}
+LAND = 192
+OPT = {"acc": 1, "pcopy": "ssv", "scat": 1, "join": 0, "r1s": 1, "fast": "01", "scale": "vv", "colmask": 0,
+       "dsplit": 2, "yq": "sys", "waw": 0, "mode": "S", "yts": "sv", "fac": 2, "pmf": 1, "iwg": 0, "trans": 1, "agc": 2, "tab0": 1}
 
 F32, B16, I32, U16, QC, U8 = "float32", "bfloat16", "int32", "uint16", "float8_e4m3fn_x4", "uint8"
 SCRATCH = {"pa": ("psum", [128, 2048], F32), "pb": ("psum", [128, 2048], F32)}
 for _d, _list in [
-        (B16, "xin 1792 ft0 1936 ft1 1936 ft2 1936 ut 512 vt 512 eb 516 ones 516 ie 256 mask 224 cap 224 cw 512 tab 464 dif 512 "
-              "ge 512 rf 1056 jk 64 ag 256 ea 768 ec 768 eo 768 yt 512 y32 256 wb 256 vv 256 ia 672 ib 672 ja 672 jb 672 so 672 "
-              "tm 64 rl 64 gt 64 pv 64 gv 64 lt 64 rst 32 cnb 32"),
-        (F32, "iw 448 r1 448 r2 448 r3 448 ps 448 smk 448 scn 448 pmf 448 oa1 400 yo 448 key 144 top 256 capz 64 capb 32 sc 8 "
-              "cnt 4 pen 32 s2 32 pm1 32 nd4 40 dn 32 kc 32 kb 32 hrow 14 ka 8 kd 8 kk 8 fa 14 fb 14 fc 14 fd 14 fe 14 ff 14 "
-              "fg 14 fh 14 fi 14 oe 25 o2 25 o3 25"),
+        (B16, "xin 1792 ft0 1936 ft1 1936 ft2 1936 ut 512 vt 512 eb 516 ones 516 ie 256 mask 224 cap 224 cw 512 tab 480 arb 400 dif 512 "
+              "ge 512 rf 1056 jk 64 ag 512 tob 256 keb 144 mc 448 ea 1536 eo 768 yt 512 y32 256 wb 256 vv 256 ia 672 ib 672 ja 672 jb 672 so 672 "
+              "tm 64 rl 64 gt 64 pv 64 gv 64 jrow 28"),
+        (F32, "iw 448 r1 448 r2 448 r3 448 ps 448 smk 448 scn 448 pmf 448 oa1 400 yo 448 key 144 top 256 capz 128 capb 32 sc 8 "
+              "cnt 4 pen 32 s2 32 pm1 32 nd4 40 dn 32 kc 32 toc 256 capy 128 kb 32 low 16 hrow 14 ka 8 kd 8 kk 8 fa 14 fb 14 fc 14 fd 14 fe 14 ff 14 "
+              "fg 14 fh 14 fi 14 oe 25 o2 25 o3 25 za 28 zb 28 zc 28"),
         (I32, "ndin 28 arin 392 lane0 1 lane 1 oi 16 oim 16 o1 25"),
-        (U16, "lrep 14 lu 8 ndn 28 nd16 28 li 14 li16 14 lk 14 lk16 14 lc 14 lf 28 loa 26 off 64 ox 16")]:
+        (U16, "lrep 14 lu 8 ndn 28 nd16 28 li 14 li16 14 lk 14 lk16 14 lc 14 lf 28 l0 28 loa 26 off 64 ox 16")]:
     _w = _list.split()
     for _k in range(0, len(_w), 2):
         SCRATCH[_w[_k]] = ("sbuf", [128, int(_w[_k + 1])], _d)
-for _n, _c in [("qw", 512), ("qu", 128), ("qr", 128), ("qv", 128), ("qe", 512), ("qx0", 448), ("qx1", 448), ("qx2", 448),
-               ("qx3", 448), ("qy", 768), ("ld", 320)]:
+for _n, _c in [("qw", 512), ("qu", 128), ("qr", 128), ("qv", 128), ("qe", 512), ("qx0", LAND + 448), ("qx1", 448),
+               ("qx2", 448), ("qx3", 448), ("qy", 768)]:
     SCRATCH[_n] = ("sbuf", [128, _c], QC)
     SCRATCH["s" + _n] = ("sbuf", [128, _c], U8)
 
@@ -36,6 +38,18 @@ NDMA = 20
 SEMAPHORES = ["cv", "cs", "ct", "cg", "loc"] + ["arr%d" % _k for _k in range(2 * ROUNDS)] + ["dma%d" % _k for _k in range(NDMA)]
 
 ORDER = [int(_k) for _k in """
+8 0 1 10 2 3 19 4 9 15 11 25 66 26 69 63 65 62 64 16 67 17 12 20 28 70 29 34 75 21 32 68 45 71 22 33 72 35 100 73 18 23 80 31 36 30 24 89 13 37 38 14 87 90 84 86 85 91 81 92 74 83 112 5 6 77 7 82 61 110 111 115 96 113 114 93 116 119 118 79 97 117 94 107 76 78 120 99 98 95 133 108 122 139 134 126 102 124 132 121 140 136 125 105 103 131 137 142 123 104 101 106 143 128 138 135 129 144 127 145 141 130 148 219 160 159 146 149 165 147 150 158 166 151 157 40 154 39 167 152 162 161 155 163 168 153 164 156 109 172 169 187 189 179 190 170 171 173 188 195 175 197 180 192 196 177 198 191 194 174 193 176 199 178 200 203 224 181 204 202 201 56 46 182 205 223 206 210 184 42 208 207 211 209 218 57 183 233 228 212 44 47 213 41 230 214 220 185 50 215 186 49 222 216 48 43 225 217 58 229 221 88 51 231 226 27 52 227 53 59 234 232 236 235 243 245 247 249 244 242 248 254 246 252 258 255 256 253 250 259 257 251 260 60 54 261 55 262 263 265 264 237 266 268 267 269 272 238 239 240 273 270 291 274 285 278 241 292 286 271 293 294 288 284 279 295 283 289 281 296 290 280 282 300 276 287 297 382 301 312 311 298 275 302 309 317 299 306 370 310 318 303 277 307 319 304 380 320 308 305 315 313 321 322 314 324 325 342 341 327 323 340 339 331 347 329 349 326 350 348 346 344 345 332 343 351 371 328 316 355 376 353 330 362 352 354 358 372 333 356 363 360 359 334 357 335 361 385 336 337 374 364 381 373 338 365 377 383 375 367 379 378 368 369 386 384 388 387 394 366 395 398 397 399 396 401 400 407 389 404 406 411 402 405 408 390 410 409 391 392 403 412 393 413 414 415 543 417 416 436 418 435 420 419 421 423 422 437 424 427 443 428 425 438 429 444 440 426 439 446 430 441 447 432 442 448 431 445 434 452 449 464 463 433 453 534 450 469 454 462 523 451 470 461 458 524 522 455 471 465 459 532 456 472 460 466 457 468 476 474 467 473 494 483 493 475 491 479 492 499 481 501 484 495 500 477 502 482 497 498 503 480 528 537 505 504 478 506 510 507 526 508 485 514 511 512 509 486 515 496 513 533 488 525 516 487 489 529 535 527 490 517 531 518 519 538 536 520 530 521 539 540 549 547 550 553 548 551 541 558 554 552 557 542 560 562 555 559 561 545 564 544 563 556 546 565 566 567 570 569 571 573 578 568 580 579 572 582 583 581 574 576 575 577 585 584 586
+""".split()]
+_OLD4 = [int(_k) for _k in """
+0 1 10 8 2 3 19 4 15 9 25 11 26 64 66 62 65 29 12 20 63 16 69 17 18 72 33 28 34 67 21 100 22 73 45 35 32 70 31 68 36 23 75 13 30 74 14 89 37 76 38 24 85 90 86 87 84 91 81 5 6 92 7 71 112 79 82 83 111 78 110 115 77 96 114 80 113 93 117 122 118 116 97 61 94 121 107 130 99 95 119 98 133 108 139 120 129 102 134 140 136 124 105 103 131 142 132 127 137 104 126 106 101 123 143 138 125 135 128 144 145 141 219 148 160 159 146 149 165 147 150 158 166 151 157 154 39 40 167 164 152 163 155 161 162 168 153 109 156 172 169 187 190 179 189 224 170 171 173 188 195 175 197 177 180 198 192 196 191 174 194 193 176 199 178 200 203 181 204 201 202 218 182 56 41 205 206 208 184 42 210 207 209 228 211 223 220 183 46 212 233 44 57 213 230 222 185 47 186 215 226 214 49 216 48 229 58 217 221 27 43 50 51 225 231 59 52 88 53 227 232 234 236 245 242 235 249 244 246 243 248 254 247 255 258 252 259 253 250 256 257 251 260 54 261 55 262 264 263 265 267 237 268 266 60 272 238 269 270 239 274 291 240 285 278 273 241 292 286 271 293 294 288 284 282 295 280 283 289 279 296 290 281 300 287 276 297 371 311 275 312 301 298 382 317 302 299 372 318 306 310 303 309 277 370 319 307 380 304 320 308 316 305 313 314 323 321 315 324 341 329 342 331 339 322 340 325 347 327 349 374 346 350 344 348 343 332 381 351 328 326 376 355 353 330 362 354 352 358 333 356 363 360 359 334 357 345 361 335 336 385 364 337 373 338 375 365 383 377 378 367 379 366 368 384 369 386 388 387 394 395 398 396 399 397 400 401 404 389 405 407 408 402 406 409 411 390 410 403 392 391 412 413 393 414 543 415 417 416 435 418 436 420 419 421 423 422 437 424 428 443 427 425 438 430 444 440 426 439 446 429 441 447 432 442 448 431 445 433 452 449 464 523 434 463 453 450 532 469 454 451 522 470 458 462 455 461 534 525 471 459 456 467 468 472 460 465 466 457 476 475 474 528 473 493 483 494 479 492 491 481 524 499 477 501 484 496 497 502 498 500 535 482 503 478 505 507 480 510 504 506 514 526 485 508 512 511 515 486 509 495 513 487 488 533 516 489 527 490 529 537 517 531 519 518 536 538 520 521 530 539 540 548 550 552 549 547 554 559 541 558 560 553 551 557 542 563 562 555 564 561 556 565 566 570 545 544 546 567 569 571 573 572 580 578 582 568 579 581 576 575 584 574 577 583 585 586
+""".split()]
+_OLD3 = [int(_k) for _k in """
+10 4 8 1 3 5 14 2 0 6 7 15 73 11 55 63 13 9 68 61 62 56 59 16 18 21 65 54 17 20 12 37 26 25 48 35 38 27 23 22 39 28 49 24 58 19 42 40 41 30 66 83 94 67 57 74 70 60 71 72 43 69 53 33 31 80 32 84 64 81 75 105 29 77 85 107 106 44 76 78 101 103 117 45 86 109 79 124 90 110 108 115 112 102 111 125 46 87 120 91 113 114 116 88 89 92 93 47 128 104 96 134 129 121 118 97 135 95 99 127 131 98 126 137 100 122 123 132 138 130 119 133 139 136 213 140 34 152 153 142 222 141 214 158 212 143 160 147 159 161 216 150 144 151 50 162 148 145 157 166 165 156 154 155 149 146 171 163 164 182 173 184 183 181 167 172 191 189 174 218 169 168 192 190 170 186 219 223 193 36 188 185 187 175 197 195 217 176 200 51 196 194 220 178 204 221 179 52 198 201 205 202 199 224 203 215 177 206 225 180 207 208 209 227 82 226 210 211 228 237 229 230 239 238 231 236 246 241 247 243 232 240 249 242 250 248 251 244 233 234 253 254 252 245 235 256 255 257 279 260 259 263 258 262 280 266 261 265 270 264 281 269 278 287 277 267 276 282 288 268 284 283 290 285 272 291 271 286 275 292 289 273 293 306 366 305 274 303 294 295 377 311 365 313 296 312 314 367 297 368 300 304 375 315 298 301 318 299 308 302 324 316 334 309 317 337 320 336 369 335 310 319 342 307 344 321 326 343 341 345 325 322 346 327 340 371 372 348 338 350 339 323 353 349 347 370 357 328 351 354 355 358 329 352 378 356 331 376 359 332 374 373 333 360 381 362 379 380 363 364 382 383 392 389 330 361 391 384 390 396 393 400 395 394 385 399 397 402 404 386 401 403 398 387 388 406 405 407 409 408 539 410 432 413 412 411 416 433 415 419 414 423 418 417 440 420 431 434 430 421 441 425 435 422 443 442 437 444 424 438 427 445 426 439 429 436 519 446 530 458 459 518 448 447 464 456 428 449 466 465 467 457 453 520 450 521 468 461 454 462 451 463 472 455 460 452 479 471 470 531 488 489 490 480 469 477 495 497 525 524 487 475 496 498 473 478 493 499 476 502 494 492 503 474 501 508 500 522 510 481 506 509 504 511 482 507 491 505 484 512 528 529 523 485 486 513 533 526 527 515 534 532 516 517 535 536 544 483 514 537 546 545 543 548 550 549 554 547 553 538 551 556 558 540 555 557 552 541 542 559 560 561 563 562 564 565 568 567 569 571 576 566 570 572 578 580 574 573 575 579 581 577 582 584 583
+""".split()]
+_OLD2 = [int(_k) for _k in """
+1 8 10 2 0 3 5 9 7 4 6 15 11 57 54 61 56 63 67 55 12 16 17 58 74 18 25 37 59 26 24 72 22 38 27 66 65 20 23 64 62 70 39 28 19 21 53 41 40 29 14 13 42 83 32 79 43 85 84 75 44 94 90 77 73 45 107 60 71 86 76 46 106 110 105 109 87 91 108 101 115 112 69 111 113 47 88 103 78 93 102 89 92 128 114 104 80 134 116 129 120 96 95 135 131 121 97 99 137 119 127 132 98 126 100 138 136 133 139 130 216 140 81 122 152 142 141 118 117 153 150 151 123 143 158 33 160 217 147 144 159 161 215 124 148 162 145 125 149 165 163 146 171 182 166 164 167 184 183 181 173 172 169 191 189 168 154 156 174 157 170 155 190 185 192 194 186 175 187 196 193 195 198 199 219 221 176 203 200 197 178 205 30 207 204 206 201 208 188 68 202 226 48 209 179 31 220 180 210 211 36 49 212 227 50 222 34 213 51 214 35 225 52 223 82 218 224 228 177 241 231 229 239 240 243 242 232 244 249 245 246 250 247 251 230 253 254 252 255 257 233 256 248 259 258 260 262 261 263 265 234 264 268 266 273 267 235 269 237 284 236 270 290 238 272 285 291 271 287 286 293 283 281 288 275 282 294 280 289 295 279 292 276 296 309 308 277 306 298 297 372 314 278 316 371 299 317 315 307 303 373 300 374 274 318 304 301 322 310 320 305 311 302 329 321 338 313 319 339 325 340 330 323 337 345 377 347 312 326 327 348 352 344 349 350 343 351 346 342 324 361 328 359 355 353 354 357 356 331 363 362 341 360 332 358 384 364 334 381 365 335 375 336 366 333 378 376 367 368 382 380 369 370 383 386 385 397 388 398 395 401 396 402 405 399 400 406 379 403 407 409 389 410 408 404 387 412 411 413 415 414 416 418 417 419 421 390 420 424 422 429 423 391 425 446 393 392 428 440 394 427 447 441 426 436 442 449 439 548 443 438 435 450 444 437 451 433 445 448 431 452 465 434 464 463 453 454 432 462 470 430 455 472 471 473 459 527 456 529 528 474 468 460 467 457 469 475 476 466 461 479 458 477 481 494 478 496 533 495 483 493 480 485 501 503 497 498 484 537 504 502 507 505 508 506 500 512 486 482 517 510 515 511 509 531 513 487 519 518 499 516 488 514 539 520 490 530 538 521 491 492 532 534 522 540 535 536 524 542 525 526 541 543 545 554 544 553 552 523 555 489 546 563 562 557 564 558 556 559 547 565 567 566 560 550 568 570 569 549 561 551 572 571 573 574 577 576 578 580 585 579 586 589 587 590 588 583 581 575 582 584 592 591 593
+""".split()]
+_OLD1 = [int(_k) for _k in """
 10 8 0 1 4 2 3 7 9 6 5 15 11 73 58 71 66 16 54 17 23 75 72 55 20 37 26 64 25 62 22 38 18 56 60 63 27 24 19 39 87 28 40 53 89 41 12 14 42 32 43 13 88 44 94 111 109 78 45 95 110 80 59 69 79 21 90 70 76 114 112 115 67 113 98 97 29 46 91 96 77 116 117 105 106 93 92 81 118 107 65 61 47 100 99 128 108 101 134 82 129 119 74 135 131 57 103 127 137 102 126 123 104 132 138 83 122 133 120 139 130 68 143 140 136 84 141 158 144 121 159 142 145 160 146 149 124 161 147 150 162 148 125 151 152 163 153 198 199 164 156 166 168 192 200 167 193 154 165 201 172 85 169 170 202 174 173 203 171 155 157 175 196 207 176 206 214 194 195 204 177 35 178 197 212 222 205 208 215 210 213 209 181 211 34 30 216 179 180 217 48 36 218 219 224 189 33 220 86 183 49 31 227 223 50 226 51 228 221 187 182 185 52 190 238 236 242 240 237 239 184 241 246 225 243 247 186 248 244 250 188 249 251 245 254 252 191 253 255 230 256 257 229 258 259 261 260 262 231 263 264 265 270 232 266 234 269 277 233 283 267 235 278 268 284 280 279 286 275 281 276 287 273 274 282 288 289 285 336 292 302 290 308 293 307 291 294 309 295 301 333 298 272 310 296 299 311 297 271 300 312 341 332 347 348 314 306 313 349 319 315 316 331 317 371 350 342 320 323 351 321 318 305 352 324 304 303 353 322 344 357 354 356 372 325 359 355 363 358 330 361 326 360 327 346 364 343 328 362 345 329 373 334 365 339 366 335 370 367 338 368 369 337 340 386 388 390 375 385 387 392 389 391 393 374 379 376 378 394 396 395 377 397 398 399 400 401 402 403 405 404 406 407 408 410 409 411 380 413 412 414 417 381 415 383 419 426 382 432 416 384 427 418 433 429 428 435 423 424 430 425 436 421 431 437 438 434 441 439 457 456 451 442 422 420 481 440 458 480 443 459 444 450 447 531 460 445 453 485 455 448 452 446 454 449 461 490 497 464 496 465 462 470 498 483 466 491 463 499 472 471 500 468 520 467 492 501 487 469 473 503 495 502 474 508 493 505 504 521 475 506 509 494 476 510 522 507 512 477 482 478 525 511 513 488 514 484 515 486 523 524 516 517 526 518 489 479 528 535 537 538 527 542 536 541 539 540 519 529 543 530 546 544 545 532 548 533 547 549 550 552 534 551 553 555 554 556 557 559 560 562 561 563 565 571 568 564 569 573 558 566 567 572 574 570 575
 """.split()]
 
@@ -49,6 +63,8 @@ def calls(core, T, topo):
     rid, pid = topo.addr(nxt)[:2]
     mask = topo.mask(core, nxt)
     L = []
+    MADE = ((0, 1),) if OPT["mode"] == "J" else ((0,), (1,))
+    SENT = ((0,), (1,)) if OPT["mode"] == "S" else ((0, 1),)
 
     def b(name, lo=0, hi=None, step=1):
         hi = SCRATCH[name][1][1] if hi is None else hi
@@ -124,43 +140,59 @@ def calls(core, T, topo):
         else:
             op("g", lambda e: e.iota(out[0], pattern, base, cm), [out], [])
 
-    def load(q, out, src, codes=False):
+    def load(q, out, src, codes=False, after=None):
         ap = out[0].bitcast(dt.uint8) if codes else out[0]
-        op(q, lambda e: e.dma_start(ap, src), [out], [], "d")
+        op(q, lambda e: e.dma_start(ap, src), [out], [after], "l")
 
     def store(q, dst, in_, ap=None):
         ap = in_[0] if ap is None else ap
         op(q, lambda e: e.dma_start(dst, ap), [], [in_], "d")
 
-    def send(k):
-        lo, at, arr = 128 * k + 32 * (k % 2), 32 * (5 - k), T.sem["arr%d" % k]
-        qo, so, ql, sl = b("qy", lo, lo + 32), b("sqy", lo, lo + 32), b("ld", at, at + 32), b("sld", at, at + 32)
+    def send(r, ks):
+        k, w = 2 * r + ks[0], 32 * len(ks)
+        lo, at, arr = 128 * k + 32 * ks[0], 192 - 32 * k - w, T.sem["arr%d" % k]
+        quant("qy", 128 * k, 128 * k + 128, b("yt"))
+        qo, so, ql, sl = b("qy", lo, lo + w), b("sqy", lo, lo + w), b("qx0", at, at + w), b("sqx0", at, at + w)
         op("g", lambda e: e.remote_dma(ql[0].bitcast(dt.uint8), qo[0].bitcast(dt.uint8), arr, T.sem["loc"], pid, rid, mask), [ql], [qo], "r%d" % k)
         op("g", lambda e: e.remote_dma(sl[0], so[0], arr, T.sem["loc"], pid, rid, mask), [sl], [so], "r%d" % k)
         return at
 
     load("y", b("ndin"), T.nd[:, :])
     load("s", b("xin", 896, 1792), T.x[:, 896:1792])
-    load("y", b("xin", 0, 896), T.x[:, 0:896])
     load("y", b("ut"), T.u[:, :])
+    load("y", b("xin", 0, 896), T.x[:, 0:896])
     load("y", b("arin"), T.ar[:, :])
-    load("y", b("sqw"), T.ws[:, :])
+    load("y", b("sqw"), T.ws[:, :], False, b("xin"))
     load("y", b("qw"), T.wc[:, :], True)
     load("y", b("vt"), T.v[:, :])
 
     iota(b("lane0"), [[0, 1]], 0, 1, False)
     iota(b("ie"), [[0, 16], [1, 16]], 0, 0)
     fill(b("ones"), 1.0)
-    scan(b("iw"), b("ones", 0, 448), b("ones", 0, 448), -1.0, A.mult, A.add)
+    if OPT["iwg"]:
+        iota(b("iw"), [[1, 448]], 0, 0)
+    else:
+        scan(b("iw"), b("ones", 0, 448), b("ones", 0, 448), -1.0, A.mult, A.add)
     e0, o0 = b("eb"), b("ones")
     op("g", lambda e: e.affine_select(e0[0], o0[0], [[-1, 516]], A.is_equal, 0.0, 3, 4), [e0], [o0])
     iota(b("hrow"), [[0, 7], [16, 2]], 0, 0)
-    iota(b("kc"), [[0, 2], [-2048, 16]], 14 * 2048, 0)
+    iota(b("kc"), [[0, 2], [-16384, 16]], 14 * 16384, 0)
     ts(b("lane"), b("lane0"), 15, A.bitwise_and)
-    lane, l14, l14c, dead, ncol, l4 = [b("sc", k, k + 1) for k in range(6)]
+    lane, l14, l14c, dead, ncol, l4, alive = [b("sc", k, k + 1) for k in range(7)]
     cp(lane, b("lane"))
     ts(l14, b("lane"), 14.0, A.mult)
-    ts(l14c, b("lane"), 13.0, A.min, 14.0, A.mult)
+    if OPT["tab0"]:
+        ts(l14c, b("lane"), 16.0, A.mult)
+        iota(b("jrow"), [[0, 2], [1, 14]], 0, 0)
+        ts(alive, b("lane"), 14.0, A.is_ge, 392.0, A.mult)
+        ts(b("za"), b("jrow"), lane, A.is_equal, 1000.0, A.mult)
+        ts(b("zb"), b("iw", 0, 392, 14), lane, A.add, alive, A.max)
+        tt(b("zc"), b("za"), b("zb"), A.add)
+        ts(b("l0"), b("zc"), 394.0, A.min)
+        const("arb", 392, 394, 1, 16 * UNIT)
+        const("arb", 394, 400, 1, (16 + MARK) * UNIT)
+    else:
+        ts(l14c, b("lane"), 13.0, A.min, 14.0, A.mult)
     ts(dead, b("lane"), 14.0, A.is_ge, 480.0, A.mult)
     ts(ncol, b("lane"), 672.0, A.add)
     ts(l4, b("lane"), 449.0, A.add, 4.0, A.mult)
@@ -172,7 +204,7 @@ def calls(core, T, topo):
     ts(b("kd", 0, 7), b("ka", 0, 7), 14.0, A.is_ge, -14.0, A.mult)
     tt(b("kk", 0, 7), b("ka", 0, 7), b("kd", 0, 7), A.add)
     for h in range(2):
-        ts(b("lc", h, 14, 2), b("kk", 0, 7), l14c, A.add, 196.0 * h, A.add)
+        ts(b("lc", h, 14, 2), b("kk", 0, 7), l14c, A.add, (224.0 if OPT["tab0"] else 196.0) * h, A.add)
         ts(b("lk", h, 14, 2), b("kk", 0, 7), 16.0 * h, A.add)
         ts(b("lk16", h, 14, 2), b("kk", 0, 7), 16.0 * h, A.add, 16.0, A.mult)
     ts(b("li"), b("hrow"), lane, A.add)
@@ -196,21 +228,24 @@ def calls(core, T, topo):
     const("yt", 0, 512, 1, 0.0)
     const("cw", 0, 32, 1, (16 + MARK) * UNIT)
     const("cw", 480, 512, 1, 16 * UNIT)
-    const("tab", 448, 464, 1, 16 * UNIT)
-    const("rf", 0, 16, 1, 0.0)
-    const("rf", 514, 528, 1, 0.0)
-    const("rf", 1042, 1056, 1, 0.0)
+    const("tab", 448, 480, 1, 16 * UNIT)
     const("s2", 0, 32, 1, NONE)
-    const("key", 0, 144, 1, 0.0)
-    const("capz", 0, 64, 1, BIG)
-    const("capz", 0, 64, 16, FLOOR)
-    const("capb", 0, 32, 1, BIG)
-    const("capb", 0, 32, 16, -BIG)
+    const("key", 0, 144, 72, 0.0)
+    const("capz", 0, 128, 1, BIG)
+    const("capz", 0, 128, 16, FLOOR)
+    if "2" in OPT["fast"]:
+        const("keb", 0, 144, 72, 0.0)
+        const("capy", 0, 128, 1, BIG)
+        const("capy", 0, 128, 16, UNIT)
+    if OPT["join"]:
+        const("capb", 0, 32, 1, BIG)
+        const("capb", 0, 32, 16, -BIG)
     const("nd4", 0, 40, 1, 0.0)
-    for e in ("ea", "ec"):
-        const(e, 2, 384, 3, -BIG)
-        const(e, 385, 768, 3, -BIG)
-        const(e, 386, 768, 3, 0.0)
+    for ks in MADE:
+        e, span = 768 * ks[0], 384 * len(ks)
+        const("ea", e + 2, e + span, 3, -BIG)
+        const("ea", e + span + 1, e + 2 * span, 3, -BIG)
+        const("ea", e + span + 2, e + 2 * span, 3, 0.0)
     for e in ("ja", "jb"):
         const(e, 0, 672, 3, 0.0)
     for t in range(ROUNDS):
@@ -225,11 +260,10 @@ def calls(core, T, topo):
     act(sr, by(su, lu))
     for k in range(4):
         quant("qe", 128 * k, 128 * k + 128, b("eb", 3 - k, 515 - k))
-    quant("ld", 192, 320, b("yt"))
     quant("qv", 0, 128, b("vt"))
 
     cp(b("ndn"), b("ndin"))
-    cp(b("r1", 0, 224), by(b("iw"), b("ndn", 0, 14)))
+    (act if OPT["r1s"] else cp)(b("r1", 0, 224), by(b("iw"), b("ndn", 0, 14)))
     act(b("r1", 224, 448), by(b("iw"), b("ndn", 14, 28)))
     for h in range(2):
         lo, hi = 224 * h, 224 * h + 224
@@ -244,7 +278,12 @@ def calls(core, T, topo):
         o = 256 * h + 224
         ts(b("dif", o, o + 16), b("dn", 16 * h, 16 * h + 16), RND64, A.add, RND64, A.subtract)
         tt(b("dif", o + 16, o + 32), b("dn", 16 * h, 16 * h + 16), b("dif", o, o + 16), A.subtract)
-    ts(b("ia", 2, 672, 3), by(b("arin"), b("lc")), LIFT, A.add)
+    if OPT["tab0"]:
+        ts(b("arb", 0, 392), b("arin"), 16.0, A.add, UNIT, A.mult)
+        act(b("tab", 0, 448), by(b("arb"), b("l0")))
+        act(b("ia", 2, 672, 3), by(b("tab"), b("lc")), 1.0 / UNIT, IDENT, LIFT - 16)
+    else:
+        ts(b("ia", 2, 672, 3), by(b("arin"), b("lc")), LIFT, A.add)
 
     def table():
         act(b("cw", 32, 256), b("ia", 2, 672, 3), UNIT, IDENT, (16 - LIFT) * UNIT)
@@ -257,7 +296,8 @@ def calls(core, T, topo):
 
     def quantise_state(r, src):
         for k in range(3):
-            quant("qx%d" % r, CUTS[k], CUTS[k + 1], b(src, 4 * CUTS[k], 4 * CUTS[k + 1]))
+            o = 0 if r else LAND
+            quant("qx%d" % r, o + CUTS[k], o + CUTS[k + 1], b(src, 4 * CUTS[k], 4 * CUTS[k + 1]))
 
     def evacuate(dst):
         for k in range(3):
@@ -265,7 +305,7 @@ def calls(core, T, topo):
             (act if OPT["pcopy"][k] == "s" else cp)(b(dst, lo, hi), bank(k, hi - lo))
 
     def rows(k):
-        return b("rf", 528 * k + 16, 528 * k + 528, 16)
+        return b("rf", 512 * k + 16, 512 * k + 528, 16)
 
     def column(k, h, pm, most):
         if OPT["acc"]:
@@ -277,83 +317,143 @@ def calls(core, T, topo):
             ts(b("lt", o, o + 14 + k), pm, most, A.is_lt)
             scan(b("cnb", 16 * h, 16 * h + 15), b("ones", 0, 15), b("lt", o, o + 15), 0.0, A.mult, A.add)
         ts(b("ge", 256 * h, 256 * h + 256), b("ie"), c, A.is_gt)
-        o = 528 * k + 256 * h + 2
+        o = 512 * k + 256 * h + 2
         scan(b("rf", o, o + 256), b("ge", 256 * h, 256 * h + 256), b("dif", 256 * h, 256 * h + 256), 0.0, A.mult, A.add)
 
-    def half(r, k, ft):
-        e, o = ("ea", "ec")[k], 72 * k
-        for h in range(2):
-            p = 528 * k + 256 * h + 240
-            ts(b("ox", 8 * k + h, 8 * k + 8, 2), b("iw", 0, 4), b("rf", p, p + 1), A.add, b("rf", p + 16, p + 17), A.add)
+    def place(k, t):
+        return 8 * k + 2 * t if len(SENT) > 1 else 4 * t + 2 * k
+
+    def make(ks, ft):
+        k0, m = ks[0], len(ks)
+        o, p, w, e, span, fast = 72 * k0, 128 * k0, 64 * m, 768 * k0, 384 * m, OPT["fast"][k0]
+        for k in ks:
+            for h in range(2):
+                c = 512 * k + 256 * h + 240
+                ts(b("ox", place(k, 0) + h, place(k, 3) + 2, place(k, 1) - place(k, 0)), b("iw", 0, 4), b("rf", c, c + 1), A.add, b("rf", c + 16, c + 17), A.add)
+            c = o + 1 + 32 * (k - k0)
+            tt(b("key", c, c + 32), b("kb"), rows(k), A.add)
+            tt(b("key", c + 32 * m, c + 32 * m + 32), b("kb"), rows(k), A.subtract)
         for t in range(4):
-            act(b(e, 3 * t + 1, 384, 12), by(b(ft), b("ox", 8 * k + 2 * t, 8 * k + 2 * t + 2)), -2.0)
-        tt(b("key", o + 1, o + 33), b("kb"), rows(k), A.add)
-        tt(b("key", o + 33, o + 65), b("kb"), rows(k), A.subtract)
-        p = 128 * k
-        scan(b("top", p, p + 64), b("key", o, o + 64), b("capz"), BIG, A.max, A.min)
-        scan(b("top", p + 64, p + 128), b("key", o + 1, o + 65), b("top", p, p + 64), FLOOR, A.max, A.min)
-        cp(b("oi", 8 * k, 8 * k + 8), b("top", p + 15, p + 128, 16))
-        ts(b("oim", 8 * k, 8 * k + 8), b("oi", 8 * k, 8 * k + 8), 2047, A.bitwise_and)
+            act(b("ea", e + 3 * t + 1, e + span, 12), by(b(ft), b("ox", place(k0, t), place(k0, t) + 2 * m)), -2.0)
+        scan(b("top", p, p + w), b("key", o, o + w), b("capz", 0, w), BIG, A.max, A.min)
+        scan(b("top", p + w, p + 2 * w), b("key", o + 1, o + w + 1), b("top", p, p + w), FLOOR, A.max, A.min)
+        n8, c8 = 8 * m, 8 * k0
+        if fast == "0":
+            cp(b("oi", c8, c8 + n8), b("top", p + 15, p + 2 * w, 16))
+            ts(b("oim", c8, c8 + n8), b("oi", c8, c8 + n8), 2047, A.bitwise_and)
+            for t in range(4):
+                c = 32 * k0 + n8 * t
+                ts(b("off", c, c + n8), b("oim", c8, c8 + n8), float(t), A.add)
+        else:
+            if fast == "1":
+                scan(b("tob", p, p + w), b("key", o, o + w), b("capz", 0, w), BIG, A.max, A.min)
+                scan(b("tob", p + w, p + 2 * w), b("key", o + 1, o + w + 1), b("top", p, p + w), FLOOR, A.max, A.min)
+                tt(b("low", c8, c8 + n8), b("top", p + 15, p + 2 * w, 16), b("tob", p + 15, p + 2 * w, 16), A.subtract)
+                for t in range(4):
+                    c = 32 * k0 + n8 * t
+                    ts(b("off", c, c + n8), b("low", c8, c8 + n8), float(t), A.add)
+            else:
+                for k in ks:
+                    c = o + 1 + 32 * (k - k0)
+                    tt(b("keb", c, c + 32), b("kb"), rows(k), A.add)
+                    tt(b("keb", c + 32 * m, c + 32 * m + 32), b("kb"), rows(k), A.subtract)
+                scan(b("toc", p, p + w), b("keb", o, o + w), b("capy", 0, w), BIG, A.max, A.min)
+                scan(b("toc", p + w, p + 2 * w), b("keb", o + 1, o + w + 1), b("toc", p, p + w), UNIT, A.max, A.min)
+                for c in range(n8):
+                    z, n4 = p + 15 + 16 * c, 4 * m
+                    lo = 32 * k0 + 4 * n4 * (c // n4)
+                    ts(b("off", lo + c % n4, lo + 4 * n4, n4), b("iw", 0, 4), b("top", z, z + 1), A.add, b("toc", z, z + 1), A.subtract)
         for t in range(4):
-            w = 32 * k + 8 * t
-            ts(b("off", w, w + 8), b("oim", 8 * k, 8 * k + 8), float(t), A.add)
-        for t in range(4):
-            w = 32 * k + 8 * t
-            act(b("ag", 64 * t, 64 * t + 64), by(b(ft), b("off", w, w + 4)))
-            tt(b(e, 3 * t, 768, 12), by(b(ft), b("off", w + 4, w + 8)), b("ag", 64 * t, 64 * t + 64), A.add)
-        o = 384 * k
-        scan(b("eo", o, o + 384), b(e, 0, 384), b(e, 384, 768), 0.0, A.add, A.max)
-        ts(b("yt", p, p + 128), b("eo", o + 1, o + 384, 3), 0.5, A.mult)
-        quant("qy", 128 * (2 * r + k), 128 * (2 * r + k) + 128, b("yt"))
-        at = send(2 * r + k)
-        act(b("y32", p, p + 128), b("eo", o + 1, o + 384, 3), 16.0)
-        return at
+            c, a = 32 * k0 + n8 * t, 256 * k0 + w * t
+            if fast == "2":
+                c, step = 32 * k0 + 4 * m * t, 4 // OPT["agc"]
+                if t % step == 0:
+                    act(b("ag", a, a + w * step), by(b(ft), b("off", c, c + 4 * m * step)))
+                c += 12 * m
+            else:
+                act(b("ag", a, a + w), by(b(ft), b("off", c, c + 4 * m)))
+            tt(b("ea", e + 3 * t, e + 2 * span, 12), by(b(ft), b("off", c + 4 * m, c + n8)), b("ag", a, a + w), A.add)
+        o = 384 * k0
+        scan(b("eo", o, o + span), b("ea", e, e + span), b("ea", e + span, e + 2 * span), 0.0, A.add, A.max)
+        if OPT["yts"][k0] == "s":
+            act(b("yt", p, p + 128 * m), b("eo", o + 1, o + span, 3), 0.5)
+        else:
+            ts(b("yt", p, p + 128 * m), b("eo", o + 1, o + span, 3), 0.5, A.mult)
+        act(b("y32", p, p + 128 * m), b("eo", o + 1, o + span, 3), 16.0)
+
+    def factors(ks):
+        o, hi = 32 * ks[0], 32 * ks[-1] + 32
+        rw = b("rf", 512 * ks[0] + 16, 512 * ks[-1] + 528, 16)
+        ts(b("tm", o, hi), rw, MARK * UNIT, A.is_equal, -2.0 - MARK, A.mult)
+        act(b("rl", o, hi), rw, 1.0 / UNIT, RELU, 0.0)
+        ts(b("gt", o, hi), rw, 0.0, A.is_gt, -MARK, A.mult)
+        tt(b("pv", o, hi), b("rl", o, hi), b("tm", o, hi), A.add)
+        tt(b("gv", o, hi), b("gt", o, hi), b("tm", o, hi), A.subtract)
 
     def mutate(k):
         i, j, out, o = ("ia", "ib")[k], ("ja", "jb")[k], ("ib", "so")[k], 32 * k
-        win = b("rf", 528 * k + 16, 528 * k + 528)
-        ts(b("tm", o, o + 32), rows(k), MARK * UNIT, A.is_equal, -2.0 - MARK, A.mult)
-        ts(b("rl", o, o + 32), rows(k), 0.0, A.max, 1.0 / UNIT, A.mult)
-        ts(b("gt", o, o + 32), rows(k), 0.0, A.is_gt, -MARK, A.mult)
-        tt(b("pv", o, o + 32), b("rl", o, o + 32), b("tm", o, o + 32), A.add)
-        tt(b("gv", o, o + 32), b("gt", o, o + 32), b("tm", o, o + 32), A.subtract)
+        win = b("rf", 512 * k + 16, 512 * k + 514)
         act(b(j, 2, 672, 3), by(win, b("lk16")), -1.0 / UNIT)
         act(b(j, 1, 672, 3), by(b("gv", o, o + 32), b("lk")))
         act(b(i, 0, 672, 3), by(win, b("li16")), 1.0 / (MARK * UNIT))
         act(b(i, 1, 672, 3), by(b("pv", o, o + 32), b("li")))
         scan(b(out), b(j), b(i), 0.0, A.mult, A.add)
 
-    def renew(k, at, ft):
-        p = 128 * k
+    def renew(ks, at, ft):
+        k, m = ks[-1], 32 * len(ks)
+        p = 128 * ks[0]
         for t in range(4):
-            mm(bank(4 * k + t, 128), "qw", 128 * t, "ld", at, at + 128)
+            mm(bank(4 * k + t, 128), "qw", 128 * t, "qx0", at, at + 128)
         for t in range(4):
-            tt(b("wb", p + 32 * t, p + 32 * t + 32), bank(4 * k + t, 32), b("y32", p + t, p + 128, 4), A.add)
+            tt(b("wb", p + m * t, p + m * t + m), bank(4 * k + t, m), b("y32", p + t, p + 4 * m, 4), A.add)
         pieces = OPT["scat"] if k else 1
-        w = 128 // pieces
+        w = 4 * m // pieces
         for s in range(pieces):
             lo = p + w * s
-            ts(b("vv", lo, lo + w), b("wb", lo, lo + w), 0.03125, A.mult)
+            if OPT["scale"][k] == "s":
+                act(b("vv", lo, lo + w), b("wb", lo, lo + w), 0.03125)
+            else:
+                ts(b("vv", lo, lo + w), b("wb", lo, lo + w), 0.03125, A.mult)
             cp(by(b(ft), b("ox", lo // 16, (lo + w) // 16)), b("vv", lo, lo + w))
 
-    table()
+    if not OPT["tab0"]:
+        table()
     for r in range(ROUNDS):
         ft, qx = "ft%d" % r, "qx%d" % r
+        early, q0 = OPT["colmask"] and r > 0, 0 if r else LAND
         quantise_state(r, "ft%d" % (r - 1) if r else "xin")
         for k in range(3):
-            mm(bank(k, CUTS[k + 1] - CUTS[k]), "qr", 0, qx, CUTS[k], CUTS[k + 1])
-        evacuate("ps")
+            mm(bank(k, CUTS[k + 1] - CUTS[k]), "qr", 0, qx, q0 + CUTS[k], q0 + CUTS[k + 1])
+        if early:
+            for k in range(3):
+                tt(b("ps", CUTS[k], CUTS[k + 1]), bank(k, CUTS[k + 1] - CUTS[k]), b("mc", CUTS[k], CUTS[k + 1]), A.add)
+        else:
+            evacuate("ps")
         for k in range(4):
-            mm(bank(4 + k, 448), "qe", 128 * k, qx, 0, 448)
+            mm(bank(4 + k, 448), "qe", 128 * k, qx, q0, q0 + 448)
+        w = 448 // OPT["dsplit"]
         for k in range(4):
-            act(b(ft, k, 1792, 4), bank(4 + k, 448))
+            for s in range(OPT["dsplit"]):
+                act(b(ft, k + 4 * w * s, 4 * w * (s + 1), 4), b("pb", 512 * k + w * s, 512 * k + w * (s + 1)))
         differences()
+        if OPT["colmask"] and r == 0:
+            for h in range(2):
+                cp(by(b("mc"), b("nd16", 14 * h, 14 * h + 14)), b("mask"))
         for h in range(2):
             lo, hi = 224 * h, 224 * h + 224
-            tt(b("smk", lo, hi), by(b("ps"), b("nd16", 14 * h, 14 * h + 14)), b("mask"), A.add)
-            scan(b("pmf", lo, hi), b("smk", lo, hi), b("smk", lo, hi), -BIG, A.max, A.max)
+            if early:
+                (cp, act)[h](b("smk", lo, hi), by(b("ps"), b("nd16", 14 * h, 14 * h + 14)))
+            else:
+                tt(b("smk", lo, hi), by(b("ps"), b("nd16", 14 * h, 14 * h + 14)), b("mask"), A.add)
+            if OPT["pmf"]:
+                scan(b("pmf", lo, hi), b("smk", lo, hi), b("smk", lo, hi), -BIG, A.max, A.max)
             scan(b("scn", lo, hi), b("cap"), b("smk", lo, hi), 0.0, A.add, A.max)
-            column(0, h, b("pmf", lo + 15, hi, 16), b("pmf", hi - 1, hi))
+            if OPT["pmf"]:
+                column(0, h, b("pmf", lo + 15, hi, 16), b("pmf", hi - 1, hi))
+            else:
+                sc = b("scn", lo + 15, hi, 16)
+                scan(b("pmf", 16 * h, 16 * h + 14), sc, sc, -BIG, A.max, A.max)
+                column(0, h, b("pmf", 16 * h, 16 * h + 14), b("pmf", 16 * h + 13, 16 * h + 14))
         if OPT["join"]:
             ts(b("pen"), rows(0), 0.0, A.not_equal, OUT, A.mult)
         for h in range(2):
@@ -367,16 +467,22 @@ def calls(core, T, topo):
             scan(b("pm1"), b("capb"), b("s2"), 0.0, A.min, A.max)
         for h in range(2):
             column(1, h, b("pm1", 16 * h, 16 * h + 15), b("pm1", 16 * h + 14, 16 * h + 15))
-        at0 = half(r, 0, ft)
+        at = {}
+        for ks in MADE:
+            make(ks, ft)
+            for sent in SENT:
+                if sent[-1] == ks[-1]:
+                    at[sent] = send(r, sent)
+        for ks in ((0,), (1,)) if OPT["fac"] == 2 else ((0, 1),):
+            factors(ks)
         mutate(0)
-        at1 = half(r, 1, ft)
         mutate(1)
         ts(b("ia", 2, 672, 3), b("so", 2, 672, 3), LIFT + 3, A.min, LIFT - 3, A.max)
         if r == ROUNDS - 1:
             const("cw", 0, 32, 1, 16 * UNIT)
         table()
-        renew(0, at0, ft)
-        renew(1, at1, ft)
+        for ks in SENT:
+            renew(ks, at[ks], ft)
     act(b("oa1"), by(b("tab"), b("loa", 0, 25)), 1.0 / UNIT, IDENT, -16.0)
     store("y", T.oa[:, :], b("oa1", 0, 392))
     quantise_state(3, ft)
@@ -387,8 +493,8 @@ def calls(core, T, topo):
     store("y", T.oc[:, 1280:1792], b("qx3", 320, 448), T.qx3[:, 320:448].bitcast(dt.uint8))
     for k in range(4):
         store("sy"[k % 2], T.osc[4 * k:4 * k + 4, 0:448], b("sqx3"), T.sqx3[32 * k:32 * k + 4, 0:448])
-    store("s", T.y[:, 0:320], b("yo", 0, 320))
-    store("y", T.y[:, 320:448], b("yo", 320, 448))
+    for k in range(3):
+        store(OPT["yq"][k], T.y[:, CUTS[k]:CUTS[k + 1]], b("yo", CUTS[k], CUTS[k + 1]))
     return L
 
 
@@ -396,16 +502,18 @@ def needs(L):
     seen, E = {}, []
     for i, (q, f, R, W, kind) in enumerate(L):
         d = {}
+        if kind == "l":
+            for j in range(i):
+                if L[j][0] == q:
+                    d[j] = False
         for name, bits, w in [(a, c, False) for a, c in R] + [(a, c, True) for a, c in W]:
             psum = SCRATCH[name][0] == "psum"
             for j, jbits, jw in seen.setdefault(name, []):
                 if j == i or not bits & jbits:
                     continue
                 same = L[j][0] == q and L[j][4] == "c" and kind == "c"
-                if jw or (w and not same) or (psum and not same):
+                if jw or w or (psum and not same):
                     d[j] = True
-                elif w:
-                    d.setdefault(j, False)
             if w:
                 seen[name] = [s for s in seen[name] if s[1] & ~bits or s[0] == i]
             seen[name].append((i, bits, w))
@@ -425,26 +533,30 @@ def rank_program(g, core, T, topo):
     queue = {"v": g.vector, "s": g.scalar, "t": g.tensor, "g": g, "y": g.sync}
     count, done, seen, ndma, sent = {"v": 0, "s": 0, "t": 0, "g": 0}, {}, {}, 0, 0
 
-    def need(q, sem, val):
-        if seen.get((q, sem), 0) < val:
-            queue[q].wait_ge(T.sem[sem], val)
-            seen[(q, sem)] = val
+    known = {}
 
+    def need(q, sem, val):
+        if seen[q].get(sem, 0) < val:
+            queue[q].wait_ge(T.sem[sem], val)
+            seen[q][sem] = val
+
+    for q in queue:
+        seen[q] = {}
     for i in order:
         q, f, R, W, kind = L[i]
-        most = {}
-        for j in E[i]:
-            sem, val = done[j]
-            if E[i][j]:
-                most[sem] = max(most.get(sem, 0), val)
-        for sem in most:
-            need(q, sem, most[sem])
+        want = sorted([j for j in E[i] if E[i][j]], key=lambda j: -known[j][0])
+        for j in want:
+            need(q, done[j][0], done[j][1])
+            if OPT["trans"] and L[j][4][0] != "r":
+                for sem, val in known[j][1].items():
+                    seen[q][sem] = max(seen[q].get(sem, 0), val)
+        known[i] = (len(known), dict(seen[q]))
         call = f(queue[q])
         if kind == "c":
             count[q] += 1
             call.then_inc(T.sem["c" + q], 1)
             done[i] = ("c" + q, count[q])
-        elif kind == "d":
+        elif kind in "dl":
             call.then_inc(T.sem["dma%d" % ndma], 16)
             done[i] = ("dma%d" % ndma, 16)
             ndma += 1
@@ -452,7 +564,8 @@ def rank_program(g, core, T, topo):
             done[i] = ("arr" + kind[1:], 2 * len(topo.engines(prv, core)))
             sent += len(topo.engines(core, nxt))
     g.wait_ge(T.sem["loc"], sent)
-    for k in range(ndma):
-        need("y", "dma%d" % k, 16)
+    seen["y"] = {}
     for q in count:
         need("y", "c" + q, count[q])
+    for k in range(ndma):
+        need("y", "dma%d" % k, 16)

from concourse.mybir import dt, AluOpType, ActivationFunctionType

ROUNDS, C = 3, 448
CUTS = (0, 128, 320, 448)
XW = 1936
UNIT = 2.0 ** 19
MARK = 0.125
LIFT = 192.0
FLOOR = UNIT + 4 * 448
BIG = 2.0 ** 99
OUT = -(2.0 ** 98)
NONE = -(2.0 ** 97)
RND64 = 1.5 * 2.0 ** 29
LAND = 192
OPT = {"acc": 1, "pcopy": "ssv", "scat": 1, "join": 0, "r1s": 1, "fast": "01", "scale": "vv", "colmask": 0,
       "dsplit": 2, "yq": "sys", "waw": 0, "mode": "S", "yts": "sv", "fac": 2, "pmf": 1, "iwg": 0, "trans": 1, "agc": 2, "tab0": 1}

F32, B16, I32, U16, QC, U8 = "float32", "bfloat16", "int32", "uint16", "float8_e4m3fn_x4", "uint8"
SCRATCH = {"pa": ("psum", [128, 2048], F32), "pb": ("psum", [128, 2048], F32)}
for _d, _list in [
        (B16, "xin 1792 ft0 1936 ft1 1936 ft2 1936 ut 512 vt 512 eb 516 ones 516 ie 256 mask 224 cap 224 cw 512 tab 480 arb 400 dif 512 "
              "ge 512 rf 1056 jk 64 ag 512 tob 256 keb 144 mc 448 ea 1536 eo 768 yt 512 y32 256 wb 256 vv 256 ia 672 ib 672 ja 672 jb 672 so 672 "
              "tm 64 rl 64 gt 64 pv 64 gv 64 jrow 28"),
        (F32, "iw 448 r1 448 r2 448 r3 448 ps 448 smk 448 scn 448 pmf 448 oa1 400 yo 448 key 144 top 256 capz 128 capb 32 sc 8 "
              "cnt 4 pen 32 s2 32 pm1 32 nd4 40 dn 32 kc 32 toc 256 capy 128 kb 32 low 16 hrow 14 ka 8 kd 8 kk 8 fa 14 fb 14 fc 14 fd 14 fe 14 ff 14 "
              "fg 14 fh 14 fi 14 oe 25 o2 25 o3 25 za 28 zb 28 zc 28"),
        (I32, "ndin 28 arin 392 lane0 1 lane 1 oi 16 oim 16 o1 25"),
        (U16, "lrep 14 lu 8 ndn 28 nd16 28 li 14 li16 14 lk 14 lk16 14 lc 14 lf 28 l0 28 loa 26 off 64 ox 16")]:
    _w = _list.split()
    for _k in range(0, len(_w), 2):
        SCRATCH[_w[_k]] = ("sbuf", [128, int(_w[_k + 1])], _d)
for _n, _c in [("qw", 512), ("qu", 128), ("qr", 128), ("qv", 128), ("qe", 512), ("qx0", LAND + 448), ("qx1", 448),
               ("qx2", 448), ("qx3", 448), ("qy", 768)]:
    SCRATCH[_n] = ("sbuf", [128, _c], QC)
    SCRATCH["s" + _n] = ("sbuf", [128, _c], U8)

NDMA = 20
SEMAPHORES = ["cv", "cs", "ct", "cg", "loc"] + ["arr%d" % _k for _k in range(2 * ROUNDS)] + ["dma%d" % _k for _k in range(NDMA)]

ORDER = [int(_k) for _k in """
8 0 1 10 2 3 19 4 9 15 11 25 66 26 69 63 65 62 64 16 67 17 12 20 28 70 29 34 75 21 32 68 45 71 22 33 72 35 100 73 18 23 80 31 36 30 24 89 13 37 38 14 87 90 84 86 85 91 81 92 74 83 112 5 6 77 7 82 61 110 111 115 96 113 114 93 116 119 118 79 97 117 94 107 76 78 120 99 98 95 133 108 122 139 134 126 102 124 132 121 140 136 125 105 103 131 137 142 123 104 101 106 143 128 138 135 129 144 127 145 141 130 148 219 160 159 146 149 165 147 150 158 166 151 157 40 154 39 167 152 162 161 155 163 168 153 164 156 109 172 169 187 189 179 190 170 171 173 188 195 175 197 180 192 196 177 198 191 194 174 193 176 199 178 200 203 224 181 204 202 201 56 46 182 205 223 206 210 184 42 208 207 211 209 218 57 183 233 228 212 44 47 213 41 230 214 220 185 50 215 186 49 222 216 48 43 225 217 58 229 221 88 51 231 226 27 52 227 53 59 234 232 236 235 243 245 247 249 244 242 248 254 246 252 258 255 256 253 250 259 257 251 260 60 54 261 55 262 263 265 264 237 266 268 267 269 272 238 239 240 273 270 291 274 285 278 241 292 286 271 293 294 288 284 279 295 283 289 281 296 290 280 282 300 276 287 297 382 301 312 311 298 275 302 309 317 299 306 370 310 318 303 277 307 319 304 380 320 308 305 315 313 321 322 314 324 325 342 341 327 323 340 339 331 347 329 349 326 350 348 346 344 345 332 343 351 371 328 316 355 376 353 330 362 352 354 358 372 333 356 363 360 359 334 357 335 361 385 336 337 374 364 381 373 338 365 377 383 375 367 379 378 368 369 386 384 388 387 394 366 395 398 397 399 396 401 400 407 389 404 406 411 402 405 408 390 410 409 391 392 403 412 393 413 414 415 543 417 416 436 418 435 420 419 421 423 422 437 424 427 443 428 425 438 429 444 440 426 439 446 430 441 447 432 442 448 431 445 434 452 449 464 463 433 453 534 450 469 454 462 523 451 470 461 458 524 522 455 471 465 459 532 456 472 460 466 457 468 476 474 467 473 494 483 493 475 491 479 492 499 481 501 484 495 500 477 502 482 497 498 503 480 528 537 505 504 478 506 510 507 526 508 485 514 511 512 509 486 515 496 513 533 488 525 516 487 489 529 535 527 490 517 531 518 519 538 536 520 530 521 539 540 549 547 550 553 548 551 541 558 554 552 557 542 560 562 555 559 561 545 564 544 563 556 546 565 566 567 570 569 571 573 578 568 580 579 572 582 583 581 574 576 575 577 585 584 586
""".split()]
_OLD4 = [int(_k) for _k in """
0 1 10 8 2 3 19 4 15 9 25 11 26 64 66 62 65 29 12 20 63 16 69 17 18 72 33 28 34 67 21 100 22 73 45 35 32 70 31 68 36 23 75 13 30 74 14 89 37 76 38 24 85 90 86 87 84 91 81 5 6 92 7 71 112 79 82 83 111 78 110 115 77 96 114 80 113 93 117 122 118 116 97 61 94 121 107 130 99 95 119 98 133 108 139 120 129 102 134 140 136 124 105 103 131 142 132 127 137 104 126 106 101 123 143 138 125 135 128 144 145 141 219 148 160 159 146 149 165 147 150 158 166 151 157 154 39 40 167 164 152 163 155 161 162 168 153 109 156 172 169 187 190 179 189 224 170 171 173 188 195 175 197 177 180 198 192 196 191 174 194 193 176 199 178 200 203 181 204 201 202 218 182 56 41 205 206 208 184 42 210 207 209 228 211 223 220 183 46 212 233 44 57 213 230 222 185 47 186 215 226 214 49 216 48 229 58 217 221 27 43 50 51 225 231 59 52 88 53 227 232 234 236 245 242 235 249 244 246 243 248 254 247 255 258 252 259 253 250 256 257 251 260 54 261 55 262 264 263 265 267 237 268 266 60 272 238 269 270 239 274 291 240 285 278 273 241 292 286 271 293 294 288 284 282 295 280 283 289 279 296 290 281 300 287 276 297 371 311 275 312 301 298 382 317 302 299 372 318 306 310 303 309 277 370 319 307 380 304 320 308 316 305 313 314 323 321 315 324 341 329 342 331 339 322 340 325 347 327 349 374 346 350 344 348 343 332 381 351 328 326 376 355 353 330 362 354 352 358 333 356 363 360 359 334 357 345 361 335 336 385 364 337 373 338 375 365 383 377 378 367 379 366 368 384 369 386 388 387 394 395 398 396 399 397 400 401 404 389 405 407 408 402 406 409 411 390 410 403 392 391 412 413 393 414 543 415 417 416 435 418 436 420 419 421 423 422 437 424 428 443 427 425 438 430 444 440 426 439 446 429 441 447 432 442 448 431 445 433 452 449 464 523 434 463 453 450 532 469 454 451 522 470 458 462 455 461 534 525 471 459 456 467 468 472 460 465 466 457 476 475 474 528 473 493 483 494 479 492 491 481 524 499 477 501 484 496 497 502 498 500 535 482 503 478 505 507 480 510 504 506 514 526 485 508 512 511 515 486 509 495 513 487 488 533 516 489 527 490 529 537 517 531 519 518 536 538 520 521 530 539 540 548 550 552 549 547 554 559 541 558 560 553 551 557 542 563 562 555 564 561 556 565 566 570 545 544 546 567 569 571 573 572 580 578 582 568 579 581 576 575 584 574 577 583 585 586
""".split()]
_OLD3 = [int(_k) for _k in """
10 4 8 1 3 5 14 2 0 6 7 15 73 11 55 63 13 9 68 61 62 56 59 16 18 21 65 54 17 20 12 37 26 25 48 35 38 27 23 22 39 28 49 24 58 19 42 40 41 30 66 83 94 67 57 74 70 60 71 72 43 69 53 33 31 80 32 84 64 81 75 105 29 77 85 107 106 44 76 78 101 103 117 45 86 109 79 124 90 110 108 115 112 102 111 125 46 87 120 91 113 114 116 88 89 92 93 47 128 104 96 134 129 121 118 97 135 95 99 127 131 98 126 137 100 122 123 132 138 130 119 133 139 136 213 140 34 152 153 142 222 141 214 158 212 143 160 147 159 161 216 150 144 151 50 162 148 145 157 166 165 156 154 155 149 146 171 163 164 182 173 184 183 181 167 172 191 189 174 218 169 168 192 190 170 186 219 223 193 36 188 185 187 175 197 195 217 176 200 51 196 194 220 178 204 221 179 52 198 201 205 202 199 224 203 215 177 206 225 180 207 208 209 227 82 226 210 211 228 237 229 230 239 238 231 236 246 241 247 243 232 240 249 242 250 248 251 244 233 234 253 254 252 245 235 256 255 257 279 260 259 263 258 262 280 266 261 265 270 264 281 269 278 287 277 267 276 282 288 268 284 283 290 285 272 291 271 286 275 292 289 273 293 306 366 305 274 303 294 295 377 311 365 313 296 312 314 367 297 368 300 304 375 315 298 301 318 299 308 302 324 316 334 309 317 337 320 336 369 335 310 319 342 307 344 321 326 343 341 345 325 322 346 327 340 371 372 348 338 350 339 323 353 349 347 370 357 328 351 354 355 358 329 352 378 356 331 376 359 332 374 373 333 360 381 362 379 380 363 364 382 383 392 389 330 361 391 384 390 396 393 400 395 394 385 399 397 402 404 386 401 403 398 387 388 406 405 407 409 408 539 410 432 413 412 411 416 433 415 419 414 423 418 417 440 420 431 434 430 421 441 425 435 422 443 442 437 444 424 438 427 445 426 439 429 436 519 446 530 458 459 518 448 447 464 456 428 449 466 465 467 457 453 520 450 521 468 461 454 462 451 463 472 455 460 452 479 471 470 531 488 489 490 480 469 477 495 497 525 524 487 475 496 498 473 478 493 499 476 502 494 492 503 474 501 508 500 522 510 481 506 509 504 511 482 507 491 505 484 512 528 529 523 485 486 513 533 526 527 515 534 532 516 517 535 536 544 483 514 537 546 545 543 548 550 549 554 547 553 538 551 556 558 540 555 557 552 541 542 559 560 561 563 562 564 565 568 567 569 571 576 566 570 572 578 580 574 573 575 579 581 577 582 584 583
""".split()]
_OLD2 = [int(_k) for _k in """
1 8 10 2 0 3 5 9 7 4 6 15 11 57 54 61 56 63 67 55 12 16 17 58 74 18 25 37 59 26 24 72 22 38 27 66 65 20 23 64 62 70 39 28 19 21 53 41 40 29 14 13 42 83 32 79 43 85 84 75 44 94 90 77 73 45 107 60 71 86 76 46 106 110 105 109 87 91 108 101 115 112 69 111 113 47 88 103 78 93 102 89 92 128 114 104 80 134 116 129 120 96 95 135 131 121 97 99 137 119 127 132 98 126 100 138 136 133 139 130 216 140 81 122 152 142 141 118 117 153 150 151 123 143 158 33 160 217 147 144 159 161 215 124 148 162 145 125 149 165 163 146 171 182 166 164 167 184 183 181 173 172 169 191 189 168 154 156 174 157 170 155 190 185 192 194 186 175 187 196 193 195 198 199 219 221 176 203 200 197 178 205 30 207 204 206 201 208 188 68 202 226 48 209 179 31 220 180 210 211 36 49 212 227 50 222 34 213 51 214 35 225 52 223 82 218 224 228 177 241 231 229 239 240 243 242 232 244 249 245 246 250 247 251 230 253 254 252 255 257 233 256 248 259 258 260 262 261 263 265 234 264 268 266 273 267 235 269 237 284 236 270 290 238 272 285 291 271 287 286 293 283 281 288 275 282 294 280 289 295 279 292 276 296 309 308 277 306 298 297 372 314 278 316 371 299 317 315 307 303 373 300 374 274 318 304 301 322 310 320 305 311 302 329 321 338 313 319 339 325 340 330 323 337 345 377 347 312 326 327 348 352 344 349 350 343 351 346 342 324 361 328 359 355 353 354 357 356 331 363 362 341 360 332 358 384 364 334 381 365 335 375 336 366 333 378 376 367 368 382 380 369 370 383 386 385 397 388 398 395 401 396 402 405 399 400 406 379 403 407 409 389 410 408 404 387 412 411 413 415 414 416 418 417 419 421 390 420 424 422 429 423 391 425 446 393 392 428 440 394 427 447 441 426 436 442 449 439 548 443 438 435 450 444 437 451 433 445 448 431 452 465 434 464 463 453 454 432 462 470 430 455 472 471 473 459 527 456 529 528 474 468 460 467 457 469 475 476 466 461 479 458 477 481 494 478 496 533 495 483 493 480 485 501 503 497 498 484 537 504 502 507 505 508 506 500 512 486 482 517 510 515 511 509 531 513 487 519 518 499 516 488 514 539 520 490 530 538 521 491 492 532 534 522 540 535 536 524 542 525 526 541 543 545 554 544 553 552 523 555 489 546 563 562 557 564 558 556 559 547 565 567 566 560 550 568 570 569 549 561 551 572 571 573 574 577 576 578 580 585 579 586 589 587 590 588 583 581 575 582 584 592 591 593
""".split()]
_OLD1 = [int(_k) for _k in """
10 8 0 1 4 2 3 7 9 6 5 15 11 73 58 71 66 16 54 17 23 75 72 55 20 37 26 64 25 62 22 38 18 56 60 63 27 24 19 39 87 28 40 53 89 41 12 14 42 32 43 13 88 44 94 111 109 78 45 95 110 80 59 69 79 21 90 70 76 114 112 115 67 113 98 97 29 46 91 96 77 116 117 105 106 93 92 81 118 107 65 61 47 100 99 128 108 101 134 82 129 119 74 135 131 57 103 127 137 102 126 123 104 132 138 83 122 133 120 139 130 68 143 140 136 84 141 158 144 121 159 142 145 160 146 149 124 161 147 150 162 148 125 151 152 163 153 198 199 164 156 166 168 192 200 167 193 154 165 201 172 85 169 170 202 174 173 203 171 155 157 175 196 207 176 206 214 194 195 204 177 35 178 197 212 222 205 208 215 210 213 209 181 211 34 30 216 179 180 217 48 36 218 219 224 189 33 220 86 183 49 31 227 223 50 226 51 228 221 187 182 185 52 190 238 236 242 240 237 239 184 241 246 225 243 247 186 248 244 250 188 249 251 245 254 252 191 253 255 230 256 257 229 258 259 261 260 262 231 263 264 265 270 232 266 234 269 277 233 283 267 235 278 268 284 280 279 286 275 281 276 287 273 274 282 288 289 285 336 292 302 290 308 293 307 291 294 309 295 301 333 298 272 310 296 299 311 297 271 300 312 341 332 347 348 314 306 313 349 319 315 316 331 317 371 350 342 320 323 351 321 318 305 352 324 304 303 353 322 344 357 354 356 372 325 359 355 363 358 330 361 326 360 327 346 364 343 328 362 345 329 373 334 365 339 366 335 370 367 338 368 369 337 340 386 388 390 375 385 387 392 389 391 393 374 379 376 378 394 396 395 377 397 398 399 400 401 402 403 405 404 406 407 408 410 409 411 380 413 412 414 417 381 415 383 419 426 382 432 416 384 427 418 433 429 428 435 423 424 430 425 436 421 431 437 438 434 441 439 457 456 451 442 422 420 481 440 458 480 443 459 444 450 447 531 460 445 453 485 455 448 452 446 454 449 461 490 497 464 496 465 462 470 498 483 466 491 463 499 472 471 500 468 520 467 492 501 487 469 473 503 495 502 474 508 493 505 504 521 475 506 509 494 476 510 522 507 512 477 482 478 525 511 513 488 514 484 515 486 523 524 516 517 526 518 489 479 528 535 537 538 527 542 536 541 539 540 519 529 543 530 546 544 545 532 548 533 547 549 550 552 534 551 553 555 554 556 557 559 560 562 561 563 565 571 568 564 569 573 558 566 567 572 574 570 575
""".split()]


def calls(core, T, topo):
    A = AluOpType
    COPY, SIGN = ActivationFunctionType.Copy, ActivationFunctionType.Sign
    IDENT, RELU = ActivationFunctionType.Identity, ActivationFunctionType.Relu
    rank, n = T.rank_of(core), len(T.cores)
    nxt = T.cores[(rank + 1) % n]
    rid, pid = topo.addr(nxt)[:2]
    mask = topo.mask(core, nxt)
    L = []
    MADE = ((0, 1),) if OPT["mode"] == "J" else ((0,), (1,))
    SENT = ((0,), (1,)) if OPT["mode"] == "S" else ((0, 1),)

    def b(name, lo=0, hi=None, step=1):
        hi = SCRATCH[name][1][1] if hi is None else hi
        ap = T[name][:, lo:hi:step] if step > 1 else T[name][:, lo:hi]
        if SCRATCH[name][0] == "psum":
            return ap, [(name, 1 << (lo // 512))]
        bits = 0
        for c in range(lo, hi, step):
            bits |= 1 << c
        return ap, [(name, bits)]

    def by(win, off):
        return win[0].indirect(off[0]), win[1], off[1]

    def bank(k, cols):
        return b("pa" if k < 4 else "pb", 512 * (k % 4), 512 * (k % 4) + cols)

    def op(q, f, outs, ins, kind="c"):
        R, W = [], []
        for v in ins:
            if isinstance(v, tuple):
                R += v[1] + (v[2] if len(v) > 2 else [])
        for v in outs:
            W += v[1]
            R += v[2] if len(v) > 2 else []
        L.append((q, f, R, W, kind))

    def x(v):
        return v[0] if isinstance(v, tuple) else v

    def ts(out, in0, s1, op0, s2=None, op1=None):
        if op1 is None:
            op("v", lambda e: e.tensor_scalar(out[0], in0[0], x(s1), None, op0), [out], [in0, s1])
        else:
            op("v", lambda e: e.tensor_scalar(out[0], in0[0], x(s1), x(s2), op0, op1), [out], [in0, s1, s2])

    def tt(out, in0, in1, o):
        op("v", lambda e: e.tensor_tensor(out[0], in0[0], in1[0], o), [out], [in0, in1])

    def cp(out, in_):
        op("v", lambda e: e.tensor_copy(out[0], in_[0]), [out], [in_])

    def fill(out, c):
        op("v", lambda e: e.memset(out[0], c), [out], [])

    def scan(out, d0, d1, init, o0, o1):
        op("v", lambda e: e.tensor_tensor_scan(out[0], d0[0], d1[0], init, o0, o1), [out], [d0, d1])

    def act(out, in_, scale=1.0, func=COPY, bias=None, acc=None):
        if acc is not None:
            op("s", lambda e: e.activation(out[0], in_[0], func, bias=x(bias), scale=scale, accum_out=acc[0]), [out, acc], [in_, bias])
        elif bias is not None:
            op("s", lambda e: e.activation(out[0], in_[0], func, bias=bias, scale=scale), [out], [in_])
        elif scale == 1.0:
            op("s", lambda e: e.activation(out[0], in_[0], func), [out], [in_])
        else:
            op("s", lambda e: e.activation(out[0], in_[0], func, scale=scale), [out], [in_])

    def const(name, lo, hi, step, c):
        act(b(name, lo, hi, step), b("ones", 0, len(range(lo, hi, step))), float(c))

    def quant(q, lo, hi, in_):
        qo, so = b(q, lo, hi), b("s" + q, lo, hi)
        op("v", lambda e: e.quantize_mx(qo[0], so[0], in_[0]), [qo, so], [in_])

    def mm(out, a, alo, m, mlo, mhi):
        v = [b(a, alo, alo + 128), b("s" + a, alo, alo + 128), b(m, mlo, mhi), b("s" + m, mlo, mhi)]
        op("t", lambda e: e.matmul_mx(out[0], v[0][0], v[1][0], v[2][0], v[3][0], True, True), [out], v)

    def iota(out, pattern, base, cm, small=True):
        if small:
            op("g", lambda e: e.iota(out[0], pattern, base, cm, allow_small_or_imprecise_dtypes=True), [out], [])
        else:
            op("g", lambda e: e.iota(out[0], pattern, base, cm), [out], [])

    def load(q, out, src, codes=False, after=None):
        ap = out[0].bitcast(dt.uint8) if codes else out[0]
        op(q, lambda e: e.dma_start(ap, src), [out], [after], "l")

    def store(q, dst, in_, ap=None):
        ap = in_[0] if ap is None else ap
        op(q, lambda e: e.dma_start(dst, ap), [], [in_], "d")

    def send(r, ks):
        k, w = 2 * r + ks[0], 32 * len(ks)
        lo, at, arr = 128 * k + 32 * ks[0], 192 - 32 * k - w, T.sem["arr%d" % k]
        quant("qy", 128 * k, 128 * k + 128, b("yt"))
        qo, so, ql, sl = b("qy", lo, lo + w), b("sqy", lo, lo + w), b("qx0", at, at + w), b("sqx0", at, at + w)
        op("g", lambda e: e.remote_dma(ql[0].bitcast(dt.uint8), qo[0].bitcast(dt.uint8), arr, T.sem["loc"], pid, rid, mask), [ql], [qo], "r%d" % k)
        op("g", lambda e: e.remote_dma(sl[0], so[0], arr, T.sem["loc"], pid, rid, mask), [sl], [so], "r%d" % k)
        return at

    load("y", b("ndin"), T.nd[:, :])
    load("s", b("xin", 896, 1792), T.x[:, 896:1792])
    load("y", b("ut"), T.u[:, :])
    load("y", b("xin", 0, 896), T.x[:, 0:896])
    load("y", b("arin"), T.ar[:, :])
    load("y", b("sqw"), T.ws[:, :], False, b("xin"))
    load("y", b("qw"), T.wc[:, :], True)
    load("y", b("vt"), T.v[:, :])

    iota(b("lane0"), [[0, 1]], 0, 1, False)
    iota(b("ie"), [[0, 16], [1, 16]], 0, 0)
    fill(b("ones"), 1.0)
    if OPT["iwg"]:
        iota(b("iw"), [[1, 448]], 0, 0)
    else:
        scan(b("iw"), b("ones", 0, 448), b("ones", 0, 448), -1.0, A.mult, A.add)
    e0, o0 = b("eb"), b("ones")
    op("g", lambda e: e.affine_select(e0[0], o0[0], [[-1, 516]], A.is_equal, 0.0, 3, 4), [e0], [o0])
    iota(b("hrow"), [[0, 7], [16, 2]], 0, 0)
    iota(b("kc"), [[0, 2], [-16384, 16]], 14 * 16384, 0)
    ts(b("lane"), b("lane0"), 15, A.bitwise_and)
    lane, l14, l14c, dead, ncol, l4, alive = [b("sc", k, k + 1) for k in range(7)]
    cp(lane, b("lane"))
    ts(l14, b("lane"), 14.0, A.mult)
    if OPT["tab0"]:
        ts(l14c, b("lane"), 16.0, A.mult)
        iota(b("jrow"), [[0, 2], [1, 14]], 0, 0)
        ts(alive, b("lane"), 14.0, A.is_ge, 392.0, A.mult)
        ts(b("za"), b("jrow"), lane, A.is_equal, 1000.0, A.mult)
        ts(b("zb"), b("iw", 0, 392, 14), lane, A.add, alive, A.max)
        tt(b("zc"), b("za"), b("zb"), A.add)
        ts(b("l0"), b("zc"), 394.0, A.min)
        const("arb", 392, 394, 1, 16 * UNIT)
        const("arb", 394, 400, 1, (16 + MARK) * UNIT)
    else:
        ts(l14c, b("lane"), 13.0, A.min, 14.0, A.mult)
    ts(dead, b("lane"), 14.0, A.is_ge, 480.0, A.mult)
    ts(ncol, b("lane"), 672.0, A.add)
    ts(l4, b("lane"), 449.0, A.add, 4.0, A.mult)
    ts(b("mask"), b("ie", 0, 224), lane, A.not_equal, OUT, A.mult)
    ts(b("cap"), b("ie", 0, 224), 0.0, A.is_equal, -BIG, A.mult)
    ts(b("lrep"), b("iw", 0, 14), l14, A.add)
    cp(b("lu"), b("iw", 0, 128, 16))
    ts(b("ka", 0, 7), b("iw", 1, 8), lane, A.add)
    ts(b("kd", 0, 7), b("ka", 0, 7), 14.0, A.is_ge, -14.0, A.mult)
    tt(b("kk", 0, 7), b("ka", 0, 7), b("kd", 0, 7), A.add)
    for h in range(2):
        ts(b("lc", h, 14, 2), b("kk", 0, 7), l14c, A.add, (224.0 if OPT["tab0"] else 196.0) * h, A.add)
        ts(b("lk", h, 14, 2), b("kk", 0, 7), 16.0 * h, A.add)
        ts(b("lk16", h, 14, 2), b("kk", 0, 7), 16.0 * h, A.add, 16.0, A.mult)
    ts(b("li"), b("hrow"), lane, A.add)
    ts(b("li16"), b("hrow"), lane, A.add, 16.0, A.mult)
    ts(b("fa"), b("iw", 0, 14), -1.0, A.mult, lane, A.add)
    ts(b("fb"), b("fa"), 0.0, A.is_lt, 14.0, A.mult)
    tt(b("fc"), b("fa"), b("fb"), A.add)
    ts(b("fd"), b("fc"), 7.0, A.is_gt, 1000.0, A.mult)
    ts(b("fe"), b("fc"), 32.0, A.mult)
    ts(b("ff"), b("fc"), -32.0, A.mult, ncol, A.add)
    tt(b("fg"), b("fd"), b("iw", 0, 14), A.add)
    tt(b("fh"), b("fg"), b("fe"), A.add)
    tt(b("fi"), b("fh"), b("ff"), A.min)
    ts(b("lf", 0, 14), b("fi"), dead, A.max, 495.0, A.min)
    ts(b("lf", 14, 28), b("lf", 0, 14), 16.0, A.add)
    ts(b("oe"), b("iw", 0, 400, 16), lane, A.add)
    ts(b("o1"), b("oe"), -6.5, A.add, 1.0 / 14.0, A.mult)
    ts(b("o2"), b("o1"), 2.0, A.mult)
    tt(b("o3"), b("o2"), b("oe"), A.add)
    cp(b("loa", 0, 25), b("o3"))
    const("yt", 0, 512, 1, 0.0)
    const("cw", 0, 32, 1, (16 + MARK) * UNIT)
    const("cw", 480, 512, 1, 16 * UNIT)
    const("tab", 448, 480, 1, 16 * UNIT)
    const("s2", 0, 32, 1, NONE)
    const("key", 0, 144, 72, 0.0)
    const("capz", 0, 128, 1, BIG)
    const("capz", 0, 128, 16, FLOOR)
    if "2" in OPT["fast"]:
        const("keb", 0, 144, 72, 0.0)
        const("capy", 0, 128, 1, BIG)
        const("capy", 0, 128, 16, UNIT)
    if OPT["join"]:
        const("capb", 0, 32, 1, BIG)
        const("capb", 0, 32, 16, -BIG)
    const("nd4", 0, 40, 1, 0.0)
    for ks in MADE:
        e, span = 768 * ks[0], 384 * len(ks)
        const("ea", e + 2, e + span, 3, -BIG)
        const("ea", e + span + 1, e + 2 * span, 3, -BIG)
        const("ea", e + span + 2, e + 2 * span, 3, 0.0)
    for e in ("ja", "jb"):
        const(e, 0, 672, 3, 0.0)
    for t in range(ROUNDS):
        const("ft%d" % t, 1792, XW, 1, 0.0)
    if not OPT["acc"]:
        act(b("rst"), b("ie", 0, 32), 1.0, SIGN)
        const("lt", 0, 64, 1, 0.0)

    quant("qu", 0, 128, b("ut"))
    qr, qu, lu, sr, su = b("qr"), b("qu"), b("lu"), b("sqr"), b("squ")
    op("v", lambda e: e.tensor_copy(qr[0].bitcast(dt.uint32), qu[0].bitcast(dt.uint32).indirect(lu[0])), [qr], [qu, lu])
    act(sr, by(su, lu))
    for k in range(4):
        quant("qe", 128 * k, 128 * k + 128, b("eb", 3 - k, 515 - k))
    quant("qv", 0, 128, b("vt"))

    cp(b("ndn"), b("ndin"))
    (act if OPT["r1s"] else cp)(b("r1", 0, 224), by(b("iw"), b("ndn", 0, 14)))
    act(b("r1", 224, 448), by(b("iw"), b("ndn", 14, 28)))
    for h in range(2):
        lo, hi = 224 * h, 224 * h + 224
        tt(b("r2", lo, hi), by(b("r1", lo, hi), b("lrep")), b("mask"), A.add)
        scan(b("r3", lo, hi), b("cap"), b("r2", lo, hi), 0.0, A.add, A.max)
        cp(b("nd16", 14 * h, 14 * h + 14), b("r3", lo + 15, hi, 16))
        ts(b("nd4", 16 * h, 16 * h + 14), b("r3", lo + 15, hi, 16), 4.0, A.mult)
    ts(b("nd4", 14, 32, 16), b("iw", 0, 65, 64), l4, A.add)
    tt(b("kb"), b("nd4", 0, 32), b("kc"), A.add)
    tt(b("dn"), b("nd4", 0, 32), b("nd4", 1, 33), A.subtract)
    for h in range(2):
        o = 256 * h + 224
        ts(b("dif", o, o + 16), b("dn", 16 * h, 16 * h + 16), RND64, A.add, RND64, A.subtract)
        tt(b("dif", o + 16, o + 32), b("dn", 16 * h, 16 * h + 16), b("dif", o, o + 16), A.subtract)
    if OPT["tab0"]:
        ts(b("arb", 0, 392), b("arin"), 16.0, A.add, UNIT, A.mult)
        act(b("tab", 0, 448), by(b("arb"), b("l0")))
        act(b("ia", 2, 672, 3), by(b("tab"), b("lc")), 1.0 / UNIT, IDENT, LIFT - 16)
    else:
        ts(b("ia", 2, 672, 3), by(b("arin"), b("lc")), LIFT, A.add)

    def table():
        act(b("cw", 32, 256), b("ia", 2, 672, 3), UNIT, IDENT, (16 - LIFT) * UNIT)
        act(b("cw", 256, 480), b("ia", 2, 672, 3), -UNIT, IDENT, (16 + LIFT) * UNIT)
        act(b("tab", 0, 448), by(b("cw"), b("lf")))

    def differences():
        for h in range(2):
            scan(b("dif", 256 * h, 256 * h + 224), b("tab", 224 * h, 224 * h + 224), b("tab", 224 * h + 1, 224 * h + 225), 0.0, A.max, A.subtract)

    def quantise_state(r, src):
        for k in range(3):
            o = 0 if r else LAND
            quant("qx%d" % r, o + CUTS[k], o + CUTS[k + 1], b(src, 4 * CUTS[k], 4 * CUTS[k + 1]))

    def evacuate(dst):
        for k in range(3):
            lo, hi = CUTS[k], CUTS[k + 1]
            (act if OPT["pcopy"][k] == "s" else cp)(b(dst, lo, hi), bank(k, hi - lo))

    def rows(k):
        return b("rf", 512 * k + 16, 512 * k + 528, 16)

    def column(k, h, pm, most):
        if OPT["acc"]:
            c = b("cnt", 2 * k + h, 2 * k + h + 1)
            act(b("jk", 32 * k + 16 * h, 32 * k + 16 * h + 14 + k), pm, -1.0, SIGN, most, c)
        else:
            o = 32 * k + 16 * h
            c = b("cnb", 16 * h + 14, 16 * h + 15)
            ts(b("lt", o, o + 14 + k), pm, most, A.is_lt)
            scan(b("cnb", 16 * h, 16 * h + 15), b("ones", 0, 15), b("lt", o, o + 15), 0.0, A.mult, A.add)
        ts(b("ge", 256 * h, 256 * h + 256), b("ie"), c, A.is_gt)
        o = 512 * k + 256 * h + 2
        scan(b("rf", o, o + 256), b("ge", 256 * h, 256 * h + 256), b("dif", 256 * h, 256 * h + 256), 0.0, A.mult, A.add)

    def place(k, t):
        return 8 * k + 2 * t if len(SENT) > 1 else 4 * t + 2 * k

    def make(ks, ft):
        k0, m = ks[0], len(ks)
        o, p, w, e, span, fast = 72 * k0, 128 * k0, 64 * m, 768 * k0, 384 * m, OPT["fast"][k0]
        for k in ks:
            for h in range(2):
                c = 512 * k + 256 * h + 240
                ts(b("ox", place(k, 0) + h, place(k, 3) + 2, place(k, 1) - place(k, 0)), b("iw", 0, 4), b("rf", c, c + 1), A.add, b("rf", c + 16, c + 17), A.add)
            c = o + 1 + 32 * (k - k0)
            tt(b("key", c, c + 32), b("kb"), rows(k), A.add)
            tt(b("key", c + 32 * m, c + 32 * m + 32), b("kb"), rows(k), A.subtract)
        for t in range(4):
            act(b("ea", e + 3 * t + 1, e + span, 12), by(b(ft), b("ox", place(k0, t), place(k0, t) + 2 * m)), -2.0)
        scan(b("top", p, p + w), b("key", o, o + w), b("capz", 0, w), BIG, A.max, A.min)
        scan(b("top", p + w, p + 2 * w), b("key", o + 1, o + w + 1), b("top", p, p + w), FLOOR, A.max, A.min)
        n8, c8 = 8 * m, 8 * k0
        if fast == "0":
            cp(b("oi", c8, c8 + n8), b("top", p + 15, p + 2 * w, 16))
            ts(b("oim", c8, c8 + n8), b("oi", c8, c8 + n8), 2047, A.bitwise_and)
            for t in range(4):
                c = 32 * k0 + n8 * t
                ts(b("off", c, c + n8), b("oim", c8, c8 + n8), float(t), A.add)
        else:
            if fast == "1":
                scan(b("tob", p, p + w), b("key", o, o + w), b("capz", 0, w), BIG, A.max, A.min)
                scan(b("tob", p + w, p + 2 * w), b("key", o + 1, o + w + 1), b("top", p, p + w), FLOOR, A.max, A.min)
                tt(b("low", c8, c8 + n8), b("top", p + 15, p + 2 * w, 16), b("tob", p + 15, p + 2 * w, 16), A.subtract)
                for t in range(4):
                    c = 32 * k0 + n8 * t
                    ts(b("off", c, c + n8), b("low", c8, c8 + n8), float(t), A.add)
            else:
                for k in ks:
                    c = o + 1 + 32 * (k - k0)
                    tt(b("keb", c, c + 32), b("kb"), rows(k), A.add)
                    tt(b("keb", c + 32 * m, c + 32 * m + 32), b("kb"), rows(k), A.subtract)
                scan(b("toc", p, p + w), b("keb", o, o + w), b("capy", 0, w), BIG, A.max, A.min)
                scan(b("toc", p + w, p + 2 * w), b("keb", o + 1, o + w + 1), b("toc", p, p + w), UNIT, A.max, A.min)
                for c in range(n8):
                    z, n4 = p + 15 + 16 * c, 4 * m
                    lo = 32 * k0 + 4 * n4 * (c // n4)
                    ts(b("off", lo + c % n4, lo + 4 * n4, n4), b("iw", 0, 4), b("top", z, z + 1), A.add, b("toc", z, z + 1), A.subtract)
        for t in range(4):
            c, a = 32 * k0 + n8 * t, 256 * k0 + w * t
            if fast == "2":
                c, step = 32 * k0 + 4 * m * t, 4 // OPT["agc"]
                if t % step == 0:
                    act(b("ag", a, a + w * step), by(b(ft), b("off", c, c + 4 * m * step)))
                c += 12 * m
            else:
                act(b("ag", a, a + w), by(b(ft), b("off", c, c + 4 * m)))
            tt(b("ea", e + 3 * t, e + 2 * span, 12), by(b(ft), b("off", c + 4 * m, c + n8)), b("ag", a, a + w), A.add)
        o = 384 * k0
        scan(b("eo", o, o + span), b("ea", e, e + span), b("ea", e + span, e + 2 * span), 0.0, A.add, A.max)
        if OPT["yts"][k0] == "s":
            act(b("yt", p, p + 128 * m), b("eo", o + 1, o + span, 3), 0.5)
        else:
            ts(b("yt", p, p + 128 * m), b("eo", o + 1, o + span, 3), 0.5, A.mult)
        act(b("y32", p, p + 128 * m), b("eo", o + 1, o + span, 3), 16.0)

    def factors(ks):
        o, hi = 32 * ks[0], 32 * ks[-1] + 32
        rw = b("rf", 512 * ks[0] + 16, 512 * ks[-1] + 528, 16)
        ts(b("tm", o, hi), rw, MARK * UNIT, A.is_equal, -2.0 - MARK, A.mult)
        act(b("rl", o, hi), rw, 1.0 / UNIT, RELU, 0.0)
        ts(b("gt", o, hi), rw, 0.0, A.is_gt, -MARK, A.mult)
        tt(b("pv", o, hi), b("rl", o, hi), b("tm", o, hi), A.add)
        tt(b("gv", o, hi), b("gt", o, hi), b("tm", o, hi), A.subtract)

    def mutate(k):
        i, j, out, o = ("ia", "ib")[k], ("ja", "jb")[k], ("ib", "so")[k], 32 * k
        win = b("rf", 512 * k + 16, 512 * k + 514)
        act(b(j, 2, 672, 3), by(win, b("lk16")), -1.0 / UNIT)
        act(b(j, 1, 672, 3), by(b("gv", o, o + 32), b("lk")))
        act(b(i, 0, 672, 3), by(win, b("li16")), 1.0 / (MARK * UNIT))
        act(b(i, 1, 672, 3), by(b("pv", o, o + 32), b("li")))
        scan(b(out), b(j), b(i), 0.0, A.mult, A.add)

    def renew(ks, at, ft):
        k, m = ks[-1], 32 * len(ks)
        p = 128 * ks[0]
        for t in range(4):
            mm(bank(4 * k + t, 128), "qw", 128 * t, "qx0", at, at + 128)
        for t in range(4):
            tt(b("wb", p + m * t, p + m * t + m), bank(4 * k + t, m), b("y32", p + t, p + 4 * m, 4), A.add)
        pieces = OPT["scat"] if k else 1
        w = 4 * m // pieces
        for s in range(pieces):
            lo = p + w * s
            if OPT["scale"][k] == "s":
                act(b("vv", lo, lo + w), b("wb", lo, lo + w), 0.03125)
            else:
                ts(b("vv", lo, lo + w), b("wb", lo, lo + w), 0.03125, A.mult)
            cp(by(b(ft), b("ox", lo // 16, (lo + w) // 16)), b("vv", lo, lo + w))

    if not OPT["tab0"]:
        table()
    for r in range(ROUNDS):
        ft, qx = "ft%d" % r, "qx%d" % r
        early, q0 = OPT["colmask"] and r > 0, 0 if r else LAND
        quantise_state(r, "ft%d" % (r - 1) if r else "xin")
        for k in range(3):
            mm(bank(k, CUTS[k + 1] - CUTS[k]), "qr", 0, qx, q0 + CUTS[k], q0 + CUTS[k + 1])
        if early:
            for k in range(3):
                tt(b("ps", CUTS[k], CUTS[k + 1]), bank(k, CUTS[k + 1] - CUTS[k]), b("mc", CUTS[k], CUTS[k + 1]), A.add)
        else:
            evacuate("ps")
        for k in range(4):
            mm(bank(4 + k, 448), "qe", 128 * k, qx, q0, q0 + 448)
        w = 448 // OPT["dsplit"]
        for k in range(4):
            for s in range(OPT["dsplit"]):
                act(b(ft, k + 4 * w * s, 4 * w * (s + 1), 4), b("pb", 512 * k + w * s, 512 * k + w * (s + 1)))
        differences()
        if OPT["colmask"] and r == 0:
            for h in range(2):
                cp(by(b("mc"), b("nd16", 14 * h, 14 * h + 14)), b("mask"))
        for h in range(2):
            lo, hi = 224 * h, 224 * h + 224
            if early:
                (cp, act)[h](b("smk", lo, hi), by(b("ps"), b("nd16", 14 * h, 14 * h + 14)))
            else:
                tt(b("smk", lo, hi), by(b("ps"), b("nd16", 14 * h, 14 * h + 14)), b("mask"), A.add)
            if OPT["pmf"]:
                scan(b("pmf", lo, hi), b("smk", lo, hi), b("smk", lo, hi), -BIG, A.max, A.max)
            scan(b("scn", lo, hi), b("cap"), b("smk", lo, hi), 0.0, A.add, A.max)
            if OPT["pmf"]:
                column(0, h, b("pmf", lo + 15, hi, 16), b("pmf", hi - 1, hi))
            else:
                sc = b("scn", lo + 15, hi, 16)
                scan(b("pmf", 16 * h, 16 * h + 14), sc, sc, -BIG, A.max, A.max)
                column(0, h, b("pmf", 16 * h, 16 * h + 14), b("pmf", 16 * h + 13, 16 * h + 14))
        if OPT["join"]:
            ts(b("pen"), rows(0), 0.0, A.not_equal, OUT, A.mult)
        for h in range(2):
            o = 16 * h
            if not OPT["join"]:
                ts(b("pen", o, o + 14), b("rf", 16 + 256 * h, 240 + 256 * h, 16), 0.0, A.not_equal, OUT, A.mult)
            tt(b("s2", o, o + 14), b("scn", 224 * h + 15, 224 * h + 224, 16), b("pen", o, o + 14), A.add)
            if not OPT["join"]:
                scan(b("pm1", o, o + 15), b("s2", o, o + 15), b("s2", o, o + 15), -BIG, A.max, A.max)
        if OPT["join"]:
            scan(b("pm1"), b("capb"), b("s2"), 0.0, A.min, A.max)
        for h in range(2):
            column(1, h, b("pm1", 16 * h, 16 * h + 15), b("pm1", 16 * h + 14, 16 * h + 15))
        at = {}
        for ks in MADE:
            make(ks, ft)
            for sent in SENT:
                if sent[-1] == ks[-1]:
                    at[sent] = send(r, sent)
        for ks in ((0,), (1,)) if OPT["fac"] == 2 else ((0, 1),):
            factors(ks)
        mutate(0)
        mutate(1)
        ts(b("ia", 2, 672, 3), b("so", 2, 672, 3), LIFT + 3, A.min, LIFT - 3, A.max)
        if r == ROUNDS - 1:
            const("cw", 0, 32, 1, 16 * UNIT)
        table()
        for ks in SENT:
            renew(ks, at[ks], ft)
    act(b("oa1"), by(b("tab"), b("loa", 0, 25)), 1.0 / UNIT, IDENT, -16.0)
    store("y", T.oa[:, :], b("oa1", 0, 392))
    quantise_state(3, ft)
    for k in range(3):
        mm(bank(k, CUTS[k + 1] - CUTS[k]), "qv", 0, "qx3", CUTS[k], CUTS[k + 1])
    evacuate("yo")
    store("y", T.oc[:, 0:1280], b("qx3", 0, 320), T.qx3[:, 0:320].bitcast(dt.uint8))
    store("y", T.oc[:, 1280:1792], b("qx3", 320, 448), T.qx3[:, 320:448].bitcast(dt.uint8))
    for k in range(4):
        store("sy"[k % 2], T.osc[4 * k:4 * k + 4, 0:448], b("sqx3"), T.sqx3[32 * k:32 * k + 4, 0:448])
    for k in range(3):
        store(OPT["yq"][k], T.y[:, CUTS[k]:CUTS[k + 1]], b("yo", CUTS[k], CUTS[k + 1]))
    return L


def needs(L):
    seen, E = {}, []
    for i, (q, f, R, W, kind) in enumerate(L):
        d = {}
        if kind == "l":
            for j in range(i):
                if L[j][0] == q:
                    d[j] = False
        for name, bits, w in [(a, c, False) for a, c in R] + [(a, c, True) for a, c in W]:
            psum = SCRATCH[name][0] == "psum"
            for j, jbits, jw in seen.setdefault(name, []):
                if j == i or not bits & jbits:
                    continue
                same = L[j][0] == q and L[j][4] == "c" and kind == "c"
                if jw or w or (psum and not same):
                    d[j] = True
            if w:
                seen[name] = [s for s in seen[name] if s[1] & ~bits or s[0] == i]
            seen[name].append((i, bits, w))
        E.append(d)
    return E


def rank_program(g, core, T, topo):
    rank = T.rank_of(core)
    if rank is None:
        return
    n = len(T.cores)
    nxt, prv = T.cores[(rank + 1) % n], T.cores[(rank - 1) % n]
    L = calls(core, T, topo)
    E = needs(L)
    order = ORDER if ORDER else list(range(len(L)))
    queue = {"v": g.vector, "s": g.scalar, "t": g.tensor, "g": g, "y": g.sync}
    count, done, seen, ndma, sent = {"v": 0, "s": 0, "t": 0, "g": 0}, {}, {}, 0, 0

    known = {}

    def need(q, sem, val):
        if seen[q].get(sem, 0) < val:
            queue[q].wait_ge(T.sem[sem], val)
            seen[q][sem] = val

    for q in queue:
        seen[q] = {}
    for i in order:
        q, f, R, W, kind = L[i]
        want = sorted([j for j in E[i] if E[i][j]], key=lambda j: -known[j][0])
        for j in want:
            need(q, done[j][0], done[j][1])
            if OPT["trans"] and L[j][4][0] != "r":
                for sem, val in known[j][1].items():
                    seen[q][sem] = max(seen[q].get(sem, 0), val)
        known[i] = (len(known), dict(seen[q]))
        call = f(queue[q])
        if kind == "c":
            count[q] += 1
            call.then_inc(T.sem["c" + q], 1)
            done[i] = ("c" + q, count[q])
        elif kind in "dl":
            call.then_inc(T.sem["dma%d" % ndma], 16)
            done[i] = ("dma%d" % ndma, 16)
            ndma += 1
        else:
            done[i] = ("arr" + kind[1:], 2 * len(topo.engines(prv, core)))
            sent += len(topo.engines(core, nxt))
    g.wait_ge(T.sem["loc"], sent)
    seen["y"] = {}
    for q in count:
        need("y", "c" + q, count[q])
    for k in range(ndma):
        need("y", "dma%d" % k, 16)
